import numpy as np, ml_dtypes
CORES = [35,38,43,46]
N = 4
BF = ml_dtypes.bfloat16
def gentries(a):
    return np.ascontiguousarray(a.reshape(8, 16, -1).transpose(0, 2, 1)).reshape(8, -1)
def gtable(e):
    e = np.asarray(e); return np.ascontiguousarray(e.reshape(8, -1, 16).transpose(0, 2, 1)).reshape(128, -1).astype(np.int32)
W, L, C, VIS, SLOT, Q = 4096, 4096, 256, 3, 128, 9
GM = 255 * L
def cuts(rng, tot, k):
    return np.diff(np.concatenate([[0], np.sort(rng.integers(0, tot + 1, k - 1)), [tot]]))
def some(rng, tot, k):
    n = np.zeros(C, np.int64); n[rng.permutation(C)[:k]] = cuts(rng, tot, k)
    return n
def pack(x, o, n, gt):
    return {"aud": np.ascontiguousarray(x.reshape(N, 128, W)).astype(np.float32).astype(BF), "spots": np.stack([gtable(a) for a in o]),
            "lens": np.ascontiguousarray(n).astype(np.int32), "gua": np.ascontiguousarray(gt.reshape(N, 128, C)).astype(np.int32)}
def contrast(rng, sizes):
    st = rng.choice(np.array(sizes), (N, 8, 1, 1)); tot = rng.integers(13 * L // 16, 15 * L // 16, (N, 8))
    for g in range(8):
        q = int(rng.integers(0, N)); st[q, g] = sizes[-1]; st[(q + 1) % N, g] = sizes[0]; tot[(q + 1) % N, g] = L
    return st, tot
def parts(rng):
    st, tot = contrast(rng, [0.45, 0.6, 0.8, 1.0])
    x = (255 * st * (0.25 + 0.75 * rng.random((N, 8, 1, W))) * (0.5 + 0.5 * rng.random((N, 8, 16, W)))).astype(np.int64)
    o = rng.integers(0, W, (N, 8, L))
    n = np.stack([np.stack([cuts(rng, int(tot[r, g]), C) for g in range(8)]) for r in range(N)])
    gt = 84 * (n[:, :, None] - 2 + 5 * rng.random((N, 8, 1, C))) * (0.85 + 0.3 * rng.random((N, 8, 16, C)))
    return x, o, n, np.minimum(np.maximum(gt, 0).astype(np.int64), GM)
def exact(rng, xg, o, n, R, S, low=False):
    tot = int(np.add.reduce(n)); end = np.add.accumulate(n); beg = end - n; own = np.repeat(np.arange(C), n)
    cs = np.concatenate([np.zeros((16, 1), np.int64), np.add.accumulate(xg[:, o[:tot]], axis=1)], axis=1)
    who = rng.permutation(C)
    if low: who = who[np.argsort(n[who], kind="stable")]
    short = np.zeros(C, bool); short[who[:S]] = True
    pool = np.nonzero(~short[own])[0]; cut = np.bincount(own[rng.permutation(pool)[:R]], minlength=C)
    coin = rng.random(C) < 0.5; pr = np.argsort(rng.random((16, C)), axis=0); lift = rng.choice(np.array([1, 40, GM]), C)
    hold = cs[:, end - cut] - cs[:, beg]; full = cs[:, end] - cs[:, beg]
    v = hold + lift * (coin & (pr < Q - 1)); u = np.where(pr < Q, full + 1, np.where(coin, 0, full + 1))
    return np.minimum(np.where(short, u, v), GM)
def hunger(rng, x, o, n, gt, g):
    for r in range(N):
        pr = np.argsort(rng.random((16, C)), axis=0); u = rng.integers(1, 512, (1, C)); k = rng.integers(Q, 17, C)
        o[r, g] = rng.integers(0, W, L); n[r, g] = 0
        if r % 2 == 0:
            c = int(rng.integers(0, C)); n[r, g, c] = L; k[c] = 0
        if r % 4 == 3: k[rng.permutation(C)[int(rng.integers(1, 4)):]] = Q - 1
        gt[r, g] = u * (pr < k)
def filled(rng, x, o, n, gt, g):
    xv = x[:, g]
    for r in range(N):
        bl = r + N * rng.permutation(W // N); pr = np.argsort(rng.random((16, C)), axis=0)
        o[r, g] = bl[rng.integers(0, W // N, L)]; n[r, g] = 0; gt[r, g] = 0
        if r % 4 == 0:
            top = rng.integers(200, 256, (16, W // N))
            for p in range(N): xv[p][:, bl] = top if p == r else top >> 2
            who = np.sort(rng.permutation(C)[:7]); n[r, g, who[1:]] = L // 8 + rng.integers(0, 16, 6)
            n[r, g, who[0]] = L - int(np.add.reduce(n[r, g]))
            end = np.add.accumulate(n[r, g])
            cs = np.concatenate([np.zeros((16, 1), np.int64), np.add.accumulate(xv[r][:, o[r, g]], axis=1)], axis=1)
            full = cs[:, end] - cs[:, end - n[r, g]]
            for j in range(6):
                c = int(who[j + 1])
                gt[r, g][:, c] = np.where(pr[:, c] < Q, full[:, c] + 1, 0) if j % 2 == 0 else np.where(pr[:, c] < Q - 1, GM, full[:, c])
        if r % 4 == 1:
            xv[:, :, bl] = 255; n[r, g, 0] = L
            gt[r, g] = (pr < Q) * rng.integers(0, 300, (1, C)); gt[r, g][:, 0] = GM
        if r % 4 == 2:
            xv[:, :, bl] = 0; xv[(r + VIS - 1) % N][:, bl] = 255
            c = int(rng.integers(0, C)); n[r, g, c] = L // 2; gt[r, g][:, c] = 255
        if r % 4 == 3:
            n[r, g] = cuts(rng, L, C); gt[r, g] = GM
def few(rng, x, o, n, gt, g):
    xv = x[:, g]; sh = int(rng.integers(0, 4))
    for r in range(N):
        v = (r + sh) % 4; u = r + N * rng.permutation(W // N)[:3]; low = rng.integers(1, 64, (16, 3)); pr = np.argsort(rng.random(16))
        xv[:, :, u] = low; goal = np.add.reduce(low[:, :v], axis=1); a, b = rng.permutation(C)[:2]
        if v: xv[(r + 1) % N][:, u[0]] = goal
        n[r, g] = 0; n[r, g, a] = v; o[r, g, :v] = u[:v]
        gt[r, g] = 0; gt[r, g][:, a] = goal; gt[r, g][:, b] = pr < Q
def setup_inputs(rng):
    return pack(*parts(rng))
def setup_inputs_spread(rng):
    st, tot = contrast(rng, [0.25, 0.5, 1.0])
    x = np.minimum((st * np.exp2(8 * rng.random((N, 8, 1, W))) * (0.25 + 0.75 * rng.random((N, 8, 16, W)))).astype(np.int64), 255)
    o = rng.integers(0, W, (N, 8, L)); n = np.zeros((N, 8, C), np.int64)
    for r in range(N):
        for g in range(8):
            k = int(tot[r, g]); c = np.sort((k * rng.random(C - 1) ** 3).astype(np.int64))
            n[r, g] = np.diff(np.concatenate([[0], c, [k]]))
    m = n[:, :, None]; e = rng.random((N, 8, 1, C))
    gt = np.where(m > 0, 17 * m * np.exp2(-3 + 3.7 * e), np.exp2(8 * e) - 1) * (0.7 + 0.6 * rng.random((N, 8, 16, C)))
    gt = np.where(rng.random((N, 8, 1, C)) < 0.0625, np.exp2(20 * rng.random((N, 8, 16, C))), gt)
    return pack(x, o, n, np.minimum(gt.astype(np.int64), GM))
def setup_inputs_ends(rng):
    x = 255 * ((rng.random((N, 8, 1, W)) < 0.6) ^ (rng.random((N, 8, 16, W)) < 0.05)).astype(np.int64)
    o = np.zeros((N, 8, L), np.int64); n = np.zeros((N, 8, C), np.int64); gt = np.zeros((N, 8, 16, C), np.int64)
    for r in range(N):
        vs = rng.permutation(5)
        for g in range(8):
            one = int(rng.integers(0, 2)); lone = (r + g) % 2 == 0
            x[r, g, :, 0] = 255 if lone else 255 * one; x[r, g, :, W - 1] = 255 if lone else 255 * (1 - one)
            pr = np.argsort(rng.random((16, C)), axis=0); live = rng.random(C) < 0.3; live[C - C // 16:] = False
            k = rng.integers(0, Q, C); k[C - C // 16:] = rng.integers(Q, 17, C // 16)
            ends = rng.choice(np.array([0, W - 1]), L)
            if lone: o[r, g] = ends
            else:
                o[r, g] = np.where(rng.random(L) < 0.8, ends, rng.integers(0, W, L)); s = np.argsort(rng.random(C) - 0.5 * live)[:3 * C // 10]
                n[r, g, s] = cuts(rng, 7 * L // 8, len(s))
            j = rng.integers(1, 4, C) if lone else 1 + (rng.random(C) * (n[r, g] + 1)).astype(np.int64)
            gt[r, g] = np.where(live, 255 * j, GM * (pr < k))
            if lone:
                c = int(rng.choice(np.array([0, C // 2 + 1, C - 1]))); v = int(vs[g // 2])
                if r == N - 1 and g == 7: c = C - 1; v = 0
                if r == 0 and g == 0: v = 1
                n[r, g, c] = L; h = pr[:, c]
                gt[r, g, :, c] = (GM * (h >= 0), (GM - 255) * (h >= 0), GM * (h < Q - 1), GM * (h < Q), 255 * (h >= 0))[v]
    return pack(x, o, n, np.minimum(gt, GM))
def setup_inputs_corners(rng):
    assert SLOT + 4 <= C
    x, o, n, gt = parts(rng)
    cases = [(SLOT, SLOT, L), (SLOT + 1, SLOT + 1, L - SLOT), (SLOT - 1, SLOT, L - SLOT), (1, 1, L), (0, C, L), (-1, 0, 0), (SLOT, 1, L), (3 * SLOT, SLOT + 1, L - SLOT + 1)]
    for r in range(0, N, 2):
        sh = int(rng.integers(0, 8)); q = r + 1
        for g in range(8):
            d, e, tot = cases[(g + sh) % 8]; s = int(rng.integers(0, C // 8))
            if d < 0: n[r, g] = some(rng, L, C - C // 8); gt[r, g] = exact(rng, x[r, g], o[r, g], n[r, g], L, C // 8, True)
            else: n[r, g] = cuts(rng, 15 * L // 16, C); gt[r, g] = exact(rng, x[r, g], o[r, g], n[r, g], s + d, s)
            k = 0 if e == 0 or e == C else int(rng.integers(0, 4))
            n[q, g] = cuts(rng, tot, C); gt[q, g] = exact(rng, x[q, g], o[q, g], n[q, g], k, e + k)
    return pack(x, o, n, gt)
def setup_inputs_crowd(rng):
    x, o, n, gt = parts(rng)
    for r in range(N):
        w = W - N + r
        for g in range(8):
            role = (g - r) % 8; o[r, g] = w
            if role in (1, 3): o[r, g, int(rng.integers(0, L))] = int(rng.integers(4, W - N))
            if role in (6, 7): o[r, g] = rng.choice(np.array([0, 1, 2, 3, w]), L)
            if role in (4, 5):
                n[r, g] = 0; c = int(rng.integers(0, C)); n[r, g, c] = L
                x[r, g, :, w] = 0; x[(r + 1) % N, g, :, w] = 255
                gt[r, g] = 255 * rng.integers(0, 2, (1, C)); gt[r, g, :, c] = 255 + (role == 5)
                continue
            n[r, g] = cuts(rng, L, C) if role < 2 else some(rng, L, C - C // 4) if role < 4 else cuts(rng, 7 * L // 8, C)
            R, S = ((0, C), (0, C - 1), (L, C // 4), (L - 1, C // 4), (0, 0), (0, 0), (C // 4, C // 4), (C // 8 + SLOT, C // 8))[role]
            gt[r, g] = exact(rng, x[r, g], o[r, g], n[r, g], R, S, role in (2, 3))
    two = rng.permutation(8)[:2]
    hunger(rng, x, o, n, gt, int(two[0])); filled(rng, x, o, n, gt, int(two[1]))
    return pack(x, o, n, gt)
def setup_inputs_calm(rng):
    x = np.repeat(rng.integers(100, 256, (1, 8, 16, W)), N, axis=0); base = x[0].copy()
    o = rng.integers(0, W, (N, 8, L)); n = np.zeros((N, 8, C), np.int64); gt = np.zeros((N, 8, 16, C), np.int64)
    for r in range(N):
        for g in range(8):
            bl = r + N * rng.permutation(W // N); R = rng.integers(0, 4, N); S = rng.integers(0, 4, N); R[1] = g % 4; S[1] = (g // 4 + r) % 4
            tau = np.concatenate([np.repeat(np.arange(N), R), np.repeat(np.arange(N), S)]); m = len(tau); h = int(np.add.reduce(R)); rel = np.arange(m) < h
            sc = rng.permutation(C)[:m]; a = bl[:m]; b = bl[m:m + h]; rest = bl[m + h:]
            pr = np.argsort(rng.random((16, m)), axis=0); xv = x[:, g]; xv[:, :, b] = 1
            for p in range(N):
                late = (p - r) % N >= tau
                xv[p][:, a] = base[g][:, a] - (pr < Q - (late == rel))
            tot = 3 * L // 4; nb = cuts(rng, tot, C); nm = rest[rng.integers(0, len(rest), tot)]; end = np.add.accumulate(nb); beg = end - nb
            cs = np.concatenate([np.zeros((16, 1), np.int64), np.add.accumulate(base[g][:, nm], axis=1)], axis=1); full = cs[:, end] - cs[:, beg]
            gt[r, g] = full + ((rng.random(C) < 0.5) & (np.argsort(rng.random((16, C)), axis=0) < Q - 1)); gt[r, g][:, sc] = full[:, sc] + base[g][:, a]
            names = np.concatenate([nm, a, b]); camp = np.concatenate([np.repeat(np.arange(C), nb), sc, sc[:h]])
            o[r, g, :len(names)] = names[np.argsort(camp, kind="stable")]; n[r, g] = np.bincount(camp, minlength=C)
    few(rng, x, o, n, gt, int(rng.integers(0, 8)))
    return pack(x, o, n, gt)
def check_inputs(d):
    bad = []
    for k, lo, hi in (("aud", 0, 255), ("spots", 0, W - 1), ("lens", 0, L), ("gua", 0, GM)):
        a = np.asarray(d[k]).astype(np.float64)
        if not np.all((a >= lo) & (a <= hi)): bad.append("range of " + k)
    a = np.asarray(d["aud"]).astype(np.float64)
    if np.any(a != np.floor(a)): bad.append("whole numbers in aud")
    if np.max(np.add.reduce(np.asarray(d["lens"]).astype(np.int64), axis=2)) > L: bad.append("sum of lens in a group")
    return bad
def reference(aud, spots, lens, gua):
    x = aud.astype(np.float32).astype(np.int64).reshape(N, 8, 16, W); gt = gua.astype(np.int64).reshape(N, 8, 16, C)
    nm = np.stack([gentries(a) for a in spots]).astype(np.int64); ln = lens.astype(np.int64)
    for t in range(VIS):
        kept, sent = {}, {}
        for r in range(N):
            p = (r + t) % N
            for g in range(8):
                k = ln[r, g]; tot = int(np.add.reduce(k)); o = nm[r, g, :tot]; own = np.repeat(np.arange(C), k)
                end = np.add.accumulate(k); beg = end - k
                cs = np.concatenate([np.zeros((16, 1), np.int64), np.add.accumulate(x[p, g][:, o], axis=1)], axis=1)
                before = cs[:, :tot] - cs[:, beg[own]]; full = cs[:, end] - cs[:, beg]
                need = np.add.reduce((before < gt[r, g][:, own]).astype(np.int64), axis=0) >= Q
                short = np.nonzero(np.add.reduce((full < gt[r, g]).astype(np.int64), axis=0) >= Q)[0]
                rel = o[~need]; a = min(len(rel), len(short))
                more = np.full(C, -1, np.int64); more[short[:a]] = rel[:a]
                kept[r, g] = (o[need], own[need], more, short[a:]); sent[r, g] = rel[a:a + SLOT]
        new, nl = np.full((N, 8, L), -1, np.int64), np.zeros((N, 8, C), np.int64)
        for r in range(N):
            for g in range(8):
                o, own, more, rest = kept[r, g]; come = sent[(r - 1) % N, g]; a = min(len(come), len(rest))
                more[rest[:a]] = come[:a]; c = np.nonzero(more >= 0)[0]
                camp = np.concatenate([own, c]); w = np.argsort(camp, kind="stable")[:L]
                new[r, g, :len(w)] = np.concatenate([o, more[c]])[w]; nl[r, g] = np.bincount(camp[w], minlength=C)
        nm, ln = new, nl
    return {"yo": np.stack([gtable(a) for a in nm]).astype(np.float32), "yn": ln.astype(np.float32)}

@@ -1,0 +1,706 @@
+from concourse.bass import DstId, RemoteDMATransfer
+from concourse.mybir import AluOpType as ALU, ActivationFunctionType as AF
+
+N = 4
+F32, BF, I32, U16 = "float32", "bfloat16", "int32", "uint16"
+G2, E2, G1, E1, NB, NONE, G0, NMW = 0, 400, 912, 1312, 1568, 5664, 5680, 6080
+GB = [G0, G1, G2]
+RW, BW, IW, UW, WW = 10752, 4096, 640, 1024, 5120
+SCRATCH = {
+    "au0": ("sbuf", [128, 4112], BF), "au1": ("sbuf", [128, 4112], BF), "au2": ("sbuf", [128, 4112], BF),
+    "xa": ("sbuf", [128, 4352], F32), "xb": ("sbuf", [128, 4352], F32),
+    "da": ("sbuf", [128, 4352], F32), "db": ("sbuf", [128, 4352], F32),
+    "fl": ("sbuf", [128, 4352], BF), "sg": ("sbuf", [128, 4096], BF),
+    "nm": ("sbuf", [128, NMW], F32), "zw": ("sbuf", [128, 4608], F32),
+    "rf": ("sbuf", [128, RW], F32), "rb": ("sbuf", [128, BW], BF), "ri": ("sbuf", [128, IW], I32),
+    "wu": ("sbuf", [128, UW], U16), "wf": ("sbuf", [128, WW], F32),
+    "spi": ("sbuf", [128, 256], I32), "gui": ("sbuf", [128, 256], I32), "lni": ("sbuf", [128, 256], I32),
+    "st3": ("sbuf", [128, 8, 2, 16], F32), "cs": ("sbuf", [128, 12], F32), "cn": ("sbuf", [128, 12], F32),
+    "lin": ("dram", [8, 4128], F32),
+}
+for _k in range(8):
+    SCRATCH["p%d" % _k] = ("psum", [128, 32, 16] if _k == 2 else [128, 512], F32)
+SEMAPHORES = (["cV", "cS", "cP", "cG"] + ["d%d" % k for k in range(16)] + ["lo%d" % k for k in range(12)]
+              + ["a1h0", "a1h1", "a2h0", "a2h1"] + ["rc%d" % t for t in range(3)] + ["rn%d" % t for t in range(3)])
+
+CY = 0.00104
+HOP = 0.10
+BIG = float(1 << 23)
+VG = [3, 3, 0]
+
+
+def ap(name, lo, hi, step=1, parts=None):
+    return ("ap", name, lo, hi, step, parts)
+
+
+def sub(a, lo, hi, step=1, parts=None):
+    return ("ap", a[1], a[2] + lo, a[2] + hi, step, parts)
+
+
+def ind(w, o):
+    return ("ind", w, o)
+
+
+def raw(name, lo, hi, fn, n):
+    return ("raw", name, lo, hi, fn, n)
+
+
+def count(a):
+    if a[0] == "ind":
+        return 16 * count(a[2])
+    if a[0] == "raw":
+        return a[5]
+    return (a[3] - a[2] + a[4] - 1) // a[4]
+
+
+def regions(a):
+    if not isinstance(a, tuple):
+        return []
+    if a[0] == "ind":
+        return regions(a[1]) + regions(a[2])
+    return [(a[1], a[2], a[3], a[4] if a[0] == "ap" else 1)]
+
+
+def wide(a):
+    return SCRATCH[a[1][1] if a[0] == "ind" else a[1]][2] in (F32, I32)
+
+
+def in_psum(a):
+    return a[0] != "ind" and SCRATCH[a[1]][0] == "psum"
+
+
+def build(rank, core, T, topo):
+    ops = []
+    free = {"rf": 0, "rb": 0, "ri": 0, "wu": 0, "wf": 0}
+
+    def R(a):
+        if not isinstance(a, tuple):
+            return a
+        if a[0] == "ind":
+            return R(a[1]).indirect(R(a[2]))
+        if a[0] == "raw":
+            return a[4](T[a[1]])
+        p = a[5]
+        rows = slice(None) if p is None else slice(p[0], p[1], p[2] if len(p) > 2 else None)
+        return T[a[1]][rows, slice(a[2], a[3], a[4] if a[4] != 1 else None)]
+
+    def new(buf, n):
+        lo = free[buf]
+        free[buf] = lo + (n + 15) // 16 * 16
+        assert free[buf] <= SCRATCH[buf][1][1], buf
+        return ap(buf, lo, lo + n)
+
+    def add(eng, emit, outs, ins, cost, lat=None, sem=None, cnt=0, after=()):
+        rd, wr = [], []
+        for a in ins:
+            rd += regions(a)
+        for a in outs:
+            if isinstance(a, tuple) and a[0] == "ind":
+                wr += regions(a[1])
+                rd += regions(a[2])
+            else:
+                wr += regions(a)
+        ops.append({"eng": eng, "emit": emit, "rd": rd, "wr": wr, "cost": cost, "lat": cost if lat is None else lat,
+                    "sem": sem, "cnt": cnt, "after": list(after)})
+        return len(ops) - 1
+
+    def vcost(out, ins, two=False):
+        n = max(count(out), count(ins[0]))
+        if out[0] == "ind":
+            c = 3.8 * n
+        elif ins[0][0] == "ind":
+            c = 1.56 * n
+        elif two:
+            c = n * (1 if any(in_psum(a) for a in ins) else 2)
+        else:
+            c = n * (1 if any(wide(a) for a in [out] + ins) else 0.5)
+        return max(c, 64) * CY + 0.03
+
+    def room(out, a):
+        return new(out, count(a)) if isinstance(out, str) else out
+
+    def cp(out, a):
+        out = room(out, a)
+        add("V", lambda g: g.vector.tensor_copy(R(out), R(a)), [out], [a], vcost(out, [a]))
+        return out
+
+    def tt(out, a, b, op):
+        out = room(out, a)
+        add("V", lambda g: g.vector.tensor_tensor(R(out), R(a), R(b), op), [out], [a, b], vcost(out, [a, b], True))
+        return out
+
+    def ts(out, a, s1, op0, s2=None, op1=None):
+        out = room(out, a)
+        if op1 is None:
+            add("V", lambda g: g.vector.tensor_scalar(R(out), R(a), R(s1), None, op0), [out], [a, s1], vcost(out, [a]))
+        else:
+            add("V", lambda g: g.vector.tensor_scalar(R(out), R(a), R(s1), R(s2), op0, op1), [out], [a, s1, s2], vcost(out, [a]))
+        return out
+
+    def scan(out, a, b, init, op0, op1):
+        out = room(out, a)
+        add("V", lambda g: g.vector.tensor_tensor_scan(R(out), R(a), R(b), R(init), op0, op1), [out], [a, b, init], vcost(out, [a, b]))
+        return out
+
+    def ms(out, v):
+        add("V", lambda g: g.vector.memset(R(out), v), [out], [], vcost(out, [out]))
+        return out
+
+    def act(out, a, func, bias=0.0, scale=1.0):
+        out = room(out, a)
+        c = max(count(a) * (1.56 if a[0] == "ind" else 1), 64) * CY + 0.05
+        add("S", lambda g: g.scalar.activation(R(out), R(a), func, bias=R(bias), scale=R(scale)), [out], [a, bias, scale], c)
+        return out
+
+    def lin_(out, a, scale, bias):
+        return act(out, a, AF.Identity, bias, scale)
+
+    def mm(out, terms):
+        for k, (l, r) in enumerate(terms):
+            c = max(64, count(r)) * (4 if wide(r) else 1) * CY * 0.8
+            add("P", lambda g, l=l, r=r, k=k: g.tensor.matmul(R(out), R(l), R(r), k == 0, k == len(terms) - 1), [out], [l, r], c, c + 0.06)
+        return out
+
+    def iota(out, pat, base, cm):
+        if SCRATCH[out[1]][2] == I32:
+            add("G", lambda g: g.iota(R(out), pat, base, cm), [out], [], 0.13 + 2 * count(out) * CY)
+        else:
+            add("G", lambda g: g.iota(R(out), pat, base, cm, allow_small_or_imprecise_dtypes=True), [out], [], 0.13 + 2 * count(out) * CY)
+        return out
+
+    nd = [0]
+
+    def dma(pairs, outs, ins, lat, eng="Y"):
+        s = "d%d" % nd[0]
+        nd[0] += 1
+
+        def emit(g):
+            q = g.sync if eng == "Y" else g.scalar
+            for o, i in pairs:
+                q.dma_start(o(), i()).then_inc(T.sem[s], 16)
+        return add(eng, emit, outs, ins, 0.08 * len(pairs), lat, s, 16 * len(pairs))
+
+    nl = [0]
+
+    def send(items, lat):
+        s = "lo%d" % nl[0]
+        nl[0] += 1
+
+        def emit(g):
+            if len(items) == 1:
+                src, dst, c, es, rs = items[0]
+                rid, pid, _se = topo.addr(c)
+                g.remote_dma(R(dst), R(src), T.sem[rs], T.sem[s], pid, rid, sum(1 << e for e in es))
+            else:
+                tr = []
+                for src, dst, c, es, rs in items:
+                    rid, pid, _se = topo.addr(c)
+                    tr.append(RemoteDMATransfer(dst_ids=[DstId(rid=rid, pnc=pid)], dma_engine_mask=sum(1 << e for e in es),
+                                                remote_sem=T.sem[rs], src=R(src), dst=R(dst)))
+                g.remote_dma_fused(tr, local_sem=T.sem[s])
+        return add("G", emit, [], [it[0] for it in items], 0.6, lat, s, sum(len(it[3]) for it in items))
+
+    def recv(dst, sem, cnt, after, lat):
+        return add(None, None, [dst], [], 0.0, lat, sem, cnt, after)
+
+    C = T.cores
+    nxt, prv = C[(rank + 1) % N], C[(rank - 1) % N]
+
+    def same(a, b):
+        return topo.chip(C[a % N]) == topo.chip(C[b % N])
+
+    def relayed(r):
+        return same(r, r + 1) and not same(r, r + 2)
+
+    def plan(r):
+        e1 = topo.engines(C[r % N], C[(r - 1) % N])
+        if relayed(r - 2):
+            return e1, None
+        e2 = topo.engines(C[r % N], C[(r - 2) % N])
+        if len(e1) > len(e2):
+            return [e for e in e1 if e not in e2], e2
+        if len(e2) > len(e1):
+            return e1, [e for e in e2 if e not in e1]
+        return e1[:len(e1) // 2], e2[len(e2) // 2:]
+
+    def small(r):
+        return topo.engines(C[r % N], C[(r + 1) % N])[:8]
+
+    au = ["au0", "au1", "au2"]
+    lni, spi, gui = ap("lni", 0, 256, 1, (0, 8)), ap("spi", 0, 256), ap("gui", 0, 256)
+    dma([(lambda: R(lni), lambda: T.lens[:])], [lni], [], 2.2, "S")
+    for h in range(2):
+        a = ap("au0", 2048 * h, 2048 * h + 2048)
+        dma([(lambda a=a: R(a), lambda h=h: T.aud[:, 2048 * h:2048 * h + 2048])], [a], [], 4.0 + 1.5 * h)
+    dma([(lambda: R(spi), lambda: T.spots[:])], [spi], [], 2.6, "S")
+    dma([(lambda: R(gui), lambda: T.gua[:])], [gui], [], 3.0, "S")
+    e1, e2 = plan(rank)
+    for h in range(2):
+        lo, hi = 2048 * h, 2048 * h + 2048
+        items = [(ap("au0", lo, hi), ap("au1", lo, hi), prv, e1, "a1h%d" % h)]
+        if e2 is not None:
+            items.append((ap("au0", lo, hi), ap("au2", lo, hi), C[(rank - 2) % N], e2, "a2h%d" % h))
+        s = send(items, 6.0)
+        recv(ap("au1", lo, hi), "a1h%d" % h, len(plan(rank + 1)[0]), [s], 2.0 + 3 * h)
+        if not relayed(rank):
+            recv(ap("au2", lo, hi), "a2h%d" % h, len(plan(rank + 2)[1]), [s], 6.0 + 3 * h)
+        else:
+            recv(ap("au2", lo, hi), "a2h%d" % h, len(topo.engines(nxt, core)), [s], 9.0 + 3 * h)
+    if relayed(rank - 1):
+        for h in range(2):
+            lo, hi = 2048 * h, 2048 * h + 2048
+            send([(ap("au1", lo, hi), ap("au2", lo, hi), prv, topo.engines(core, prv), "a2h%d" % h)], 4.0)
+
+    pi = iota(new("ri", 1), [[0, 1]], 0, 1)
+    JB = iota(new("rf", 128), [[1, 8], [0, 16]], 0, 0)
+    RAMPE = iota(new("rf", 384), [[0, 24], [8192, 16]], 0, 0)
+    J = iota(new("rf", 256), [[1, 256]], 0, 0)
+    PCR = iota(new("rf", 1024), [[8192, 1024]], 8192, 0)
+    J16, J128 = sub(J, 0, 16), sub(J, 0, 128)
+    FL = ap("fl", 0, 4352)
+    ZERO = ms(new("rb", 384), 0.0)
+    pcol = cp("wf", pi)
+    B8 = sub(new("rf", 128), 0, 128, 1, (0, 8))
+    ts(B8, sub(JB, 0, 128, 1, (0, 8)), sub(pcol, 0, 1, 1, (0, 8)), ALU.is_equal)
+    ii = ts("ri", pi, 15, ALU.bitwise_and)
+    gi = ts("ri", pi, 4, ALU.arith_shift_right)
+    icol, gcol = cp("wf", ii), cp("wf", gi)
+    i8k = ts("wf", ii, 8192.0, ALU.mult)
+    AM = ts("rf", RAMPE, i8k, ALU.is_equal, BIG, ALU.mult)
+    C16 = ts("wf", J16, 16.0, ALU.mult, icol, ALU.add)
+    DUM = lin_("wf", C16, 1.0, 4096.0)
+    ms(FL, 1.0)
+    IF = ts("rf", J128, pcol, ALU.is_equal)
+    BO = ts("rf", JB, gcol, ALU.is_equal)
+    BOS = lin_("rf", BO, 1.0 / BIG, 0.0)
+    BOP = lin_("rb", BO, 0.25, 0.0)
+    BON = lin_("rb", BO, -0.25, 0.0)
+    NBO = lin_("rf", BO, -1.0, 0.0)
+    UI, US = new("rf", 128), new("rf", 128)
+    add("G", lambda g: g.affine_select(R(UI), R(NBO), [[-1, 128]], ALU.is_ge, 0.0, 0, 1), [UI], [NBO], 0.44)
+    add("G", lambda g: g.affine_select(R(US), R(NBO), [[-1, 128]], ALU.is_gt, 0.0, 0, 1), [US], [NBO], 0.44)
+    S15 = lin_("rf", BO, ts("wf", icol, 15.0, ALU.is_equal), 0.0)
+    Z = ms(new("rb", 144), 0.0)
+    ts(sub(Z, 15, 143, 16), sub(J, 0, 8), gcol, ALU.is_equal)
+    SEL = [sub(Z, 15 - a, 143 - a) for a in range(16)]
+    ni8k = lin_("wf", icol, -8192.0, 0.0)
+    i256 = lin_("wf", icol, -256.0, 0.5)
+    i256p = lin_("wf", icol, -256.0, -255.5)
+    POS8 = lin_("rf", J, -131072.0, ni8k)
+    RB = lin_("rb", sub(RAMPE, 0, 256), 0.25, 0.0)
+    PT = lin_("wf", ts("wf", J16, icol, ALU.is_le), -2 * BIG - 8192.0, 8192.0)
+    JO = cp("wu", J16)
+    JV = lin_("wf", C16, 16.0, 16.0)
+    C400 = lin_("wf", C16, 1.0, 400.0)
+    C656 = lin_("wf", C16, 1.0, 656.0)
+    C272 = lin_("wf", C16, 1.0, 272.0)
+    DUM2 = lin_("wf", C16, 1.0, 4352.0)
+    C16K = lin_("wf", C16, 16384.0, 4608.0)
+    L255 = new("wf", 32)
+    ts(sub(L255, 0, 16), C16, 255.0, ALU.is_equal, 4096.0, ALU.mult)
+    lin_(sub(L255, 16, 32), C16, 0.0, 0.0)
+    JW = new("wf", 24)
+    lin_(sub(JW, 0, 16), C16, 1.0, 0.0)
+    for k in range(3):
+        if k:
+            ms(ap(au[k], 4096, 4104), float(1 << 21))
+        if k == 2:
+            ms(ap(au[k], 4104, 4112), 0.0)
+        lin_(ap("nm", GB[k] + 384, GB[k] + 400), J16, 0.0, 4096.0)
+    lin_(ap("nm", NONE, NONE + 16), J16, 0.0, 4096.0)
+    lin_(ap("xa", 4096, 4352), J, 0.0, 0.0)
+    lin_(ap("xb", 4096, 4352), J, 0.0, 0.0)
+    END, WX, CODE = new("rf", 257), new("rf", 257), new("rf", 257)
+    T1, T2 = new("rb", 272), new("rb", 272)
+    HI = new("rf", 257)
+    for b in (END, WX):
+        lin_(sub(b, 0, 1), icol, 0.0, 0.0)
+    lin_(sub(CODE, 0, 1), icol, 0.0, BIG)
+    lin_(sub(HI, 256, 257), icol, 0.0, 0.0)
+    lin_(sub(T1, 0, 16), J16, 0.0, 0.0)
+    ZP = lin_("wf", J16, 0.0, 0.0)
+    pc, pd, pv, pw, pe, pq, pa, pb = [ap("p%d" % k, 0, 512) for k in range(8)]
+
+    def blk(a, b, step=1):
+        return raw("p2", 16 * a, 16 * b, lambda t: t[:, a:b:step, :], 16 * len(range(a, b, step)))
+
+    def wrap(out, row):
+        n = count(row)
+        scan(sub(out, 0, n), sub(AM, 0, n), row, 0.0, ALU.add, ALU.min)
+        return sub(out, 15, n, 16)
+
+    def unwrap(out, w, mx, ps):
+        tt(mx, ind(w, JO), sub(AM, 0, 256), ALU.mult)
+        mm(ps, [(BOS, mx)])
+        return act(out, ps, AF.Copy)
+
+    def count16(ps, row):
+        return mm(ps, [(SEL[a], sub(row, a, 256, 16)) for a in range(16)])
+
+    SPU = cp("wu", spi)
+    lnf = cp(sub(new("rf", 256), 0, 256, 1, (0, 8)), lni)
+    pn = mm(sub(pa, 0, 256), [(B8, lnf)])
+    scan(sub(END, 1, 257), pn, sub(ZERO, 0, 256), 0.0, ALU.add, ALU.add)
+    WA, WB, WC, WD = new("rf", 384), new("rf", 384), new("rf", 256), new("rf", 256)
+    cum0 = new("wf", 32)
+    endw = cp(sub(cum0, 0, 16), wrap(WA, sub(END, 1, 257)))
+    begw = cp(sub(cum0, 16, 32), wrap(WB, sub(END, 0, 256)))
+    SO = cp("wu", tt("wf", tt("wf", tt("wf", endw, begw, ALU.is_equal), DUM, ALU.mult), begw, ALU.max))
+    NG = ts("rf", gui, -1.0, ALU.mult)
+    cp(ind(FL, SO), sub(ZERO, 0, 256))
+    UO = cp("wu", ts("ri", cp("ri", endw), 255, ALU.bitwise_and))
+    LT = act("rb", END, AF.Sign, i256p)
+    GE = act("rb", sub(END, 1, 257), AF.Sign, i256)
+    EQ = tt("rb", GE, sub(LT, 1, 257), ALU.subtract)
+    nw0 = tt("wf", endw, begw, ALU.subtract)
+    beg16 = lin_("wf", begw, 1.0, 16.0)
+    begm = lin_("wf", begw, 1.0, -1.0)
+    SG1, SGN = new("rb", 256), new("rb", 256)
+    act(SG1, NG, AF.Sign, 0.5)
+    zw = ts("wf", count16(sub(pe, 0, 16), SG1), -1.0, ALU.is_lt)
+    stat = tt("wf", lin_("wf", nw0, -0.5, ni8k), zw, ALU.subtract)
+    act(ap("da", 4096, 4352), NG, AF.Copy)
+    act(ap("db", 4096, 4352), NG, AF.Copy)
+
+    SPF = cp("rf", spi)
+    for h in range(2):
+        o = sub(pb, 128 * h, 128 * h + 128)
+        i_ = sub(SPF, h, 256, 2)
+        add("P", lambda g, o=o, i_=i_: g.tensor.transpose(R(o), R(i_), R(IF)), [o], [i_, IF], 0.45, 0.5)
+        act(raw("st3", 0, 256, lambda t, h=h: t[:, :, h, :], 128), o, AF.Copy)
+    lin = ap("lin", 0, 4128)
+    zp8 = sub(ZP, 0, 16, 1, (0, 8))
+    pairs = [(lambda g_=g_: T.lin[g_, 16:4112], lambda g_=g_: T.st3[:, g_, :, :]) for g_ in range(8)]
+    pairs += [(lambda: T.lin[:, 0:16], lambda: R(zp8)), (lambda: T.lin[:, 4112:4128], lambda: R(zp8))]
+    dma(pairs, [lin], [ap("st3", 0, 256), zp8], 4.0)
+    dma([(lambda i=i: T.nm[i:128:16, NB:NB + 4096], lambda: T.lin[:, 16:4112]) for i in range(16)], [ap("nm", NB, NB + 4096)], [lin], 10.0)
+    WIN = ap("db", 0, 4112)
+
+    XS, SG2 = new("rf", 256), new("rb", 256)
+    NC, FIL, BKG, MX, MY, NA, NB2, EG = [new("rf", n) for n in (256, 384, 384, 256, 256, 256, 256, 256)]
+    BKR = [new("rf", 256), new("rf", 256)]
+    SND = new("rf", 384)
+    ZW = ap("zw", 0, 4608)
+    st = {"cum": cum0, "k": nw0, "l": nw0, "bk": sub(END, 1, 257), "m8": endw}
+
+    def heavy(t):
+        x, d = ["xa", "xb", "xa"][t], ["da", "db", "da"][t]
+        tab = ap(au[t], 0, 4096)
+        for k in range(8):
+            o, src = ap(x, 512 * k, 512 * k + 512), ind(tab, sub(SPU, 32 * k, 32 * k + 32))
+            if k >= 8 - VG[t]:
+                cp(o, src)
+            else:
+                act(o, src, AF.Copy)
+        act(XS, ind(ap(x, 0, 4352), SO), AF.Copy)
+        tt(ind(ap(x, 0, 4352), SO), XS, NG, ALU.add)
+        terms = []
+        for k in range(8):
+            lo, hi = 512 * k, 512 * k + 512
+            scan(ap(d, lo, hi), ap("fl", lo, hi), ap(x, lo, hi), 0.0 if k == 0 else ap(d, lo - 1, lo), ALU.mult, ALU.add)
+            act(ap("sg", lo, hi), ap(d, lo, hi), AF.Sign, 0.5)
+            terms += [(SEL[a], ap("sg", 256 * a, 256 * a + 256)) for a in range(2 * k, 2 * k + 2)]
+        mm(sub(pc, 0, 256), terms)
+        act(SG2, sub(pc, 0, 256), AF.Sign, 1.0)
+        scan(sub(WX, 1, 257), SG2, sub(ZERO, 0, 256), 0.0, ALU.add, ALU.add)
+        tt(sub(T1, 16, 272), ind(WX, UO), EQ, ALU.mult)
+        lin_(sub(T2, 15, 272), LT, sub(WX, 256, 257), 0.0)
+        mm(sub(pd, 0, 256), [(BOP, RB), (BOP, sub(T2, 16, 272)), (BON, sub(T2, 15, 271)), (BOP, sub(T1, 16, 272)), (BON, sub(T1, 15, 271))])
+        w = wrap(WC, sub(pd, 0, 256))
+        if t == 0:
+            return tt("wf", w, tt("wf", stat, nw0, ALU.add), ALU.add)
+        return tt("wf", w, stat, ALU.add)
+
+    def decode(n, jc, bk):
+        nw = wrap(WA, sub(FIL, 0, n))
+        cu = ts("wu", nw, 1.0 / 16384, ALU.mult)
+        act(sub(BKG, 0, n), ind(bk, cu), AF.Copy)
+        ci = ts("ri", nw, 1.0 / 16384, ALU.mult)
+        y = tt("wf", tt("wf", nw, jc, ALU.add), ts("wf", ci, -16384.0, ALU.mult, -4608.0, ALU.add), ALU.add)
+        return ci, y
+
+    def fill(n, offs, code):
+        lin_(sub(ZW, 0, n), sub(RAMPE, 0, n), 0.0, 0.0)
+        cp(ind(ZW, offs), code)
+        scan(sub(FIL, 0, n), sub(ZW, 0, n), sub(ZERO, 0, n), 0.0, ALU.max, ALU.max)
+
+    def light(t, d):
+        Gt = GB[t]
+        cum, k, l = st["cum"], st["k"], st["l"]
+        if t:
+            tab = ap(au[t], 0, 4112 if t == 2 else 4104)
+            mx = tt("wf", tt("wf", d, l, ALU.add), st["m1"], ALU.max)
+            na = lin_(NA, ind(ap(["da", "db", "da"][t], 0, 4352), st["VU"]), -1.0, 0.0)
+            if t == 2:
+                u = tt(NB2, ind(tab, st["OZ"]), na, ALU.subtract)
+                act(SG1, u, AF.Sign, 0.5)
+                io = ts("wf", count16(sub(pe, 16, 32), SG1), -1.0, ALU.is_lt)
+                mx = tt("wf", mx, tt("wf", io, st["mm"], ALU.mult), ALU.subtract)
+                na = lin_(NA, u, -1.0, 0.0)
+            tt(SGN, ind(tab, st["EW"]), na, ALU.is_lt)
+            inew = ts("wf", count16(sub(pq, 0, 16), SGN), 8.5, ALU.is_ge)
+            d = tt("wf", mx, inew, ALU.subtract)
+        x = new("wf", 32)
+        rel, sh = ts(sub(x, 0, 16), d, 0.0, ALU.max), ts(sub(x, 16, 32), d, 0.0, ALU.is_lt)
+        sc = scan("wf", x, sub(ZERO, 0, 32), 0.0, ALU.add, ALU.add)
+        mm(blk(0, 2), [(BO, sc), (US, x)])
+        code = tt("wf", st["m8"], blk(0, 1), ALU.subtract)
+        mm(sub(pw, 0, 2), [(BO, sub(sc, 15, 32, 16))])
+        ex = mm(blk(2, 4), [(BO, sc), (UI, x)])
+        rcx = blk(2, 3)
+        rt = cp("wf", sub(pw, 0, 2))
+        rcol, tot = sub(rt, 0, 1), sub(rt, 1, 2)
+        unwrap(NC, code, MX, sub(pa, 0, 256))
+        cs, cn = ap("cs", 4 * t, 4 * t + 1), ap("cn", 4 * t, 4 * t + 1)
+        ts(cs, ts("wf", rcol, 2.0, ALU.mult, tot, ALU.subtract), 0.0, ALU.max, 128.0, ALU.min)
+        s = send([(cs, cn, nxt, small(rank), "rc%d" % t)], 1.0)
+        recv(cn, "rc%d" % t, len(small(rank - 1)), [s], 1.5)
+        scol = tt("wf", tot, rcol, ALU.subtract)
+        c256 = ts("wf", scol, -1.0, ALU.mult, 256.0, ALU.add)
+        t2 = tt("wf", ts("wf", x, 0.0, ALU.is_equal, 8192.0, ALU.mult), ex, ALU.add)
+        p = tt("wf", ts("wf", rcx, scol, ALU.is_ge, c256, ALU.mult), sub(t2, 0, 16), ALU.add)
+        OU = cp("wu", tt("wf", p, DUM2, ALU.min))
+        lin_(sub(JW, 16, 24), sub(C16, 0, 8), 1.0, scol)
+        jcb = tt("wf", ts("wf", JW, rcol, ALU.is_ge, 8192.0, ALU.mult), JW, ALU.add)
+        fill(384, OU, NC)
+        w0 = [NB, E1, E2][t]
+        if t == 0:
+            off = tt("wf", wrap(WA, FIL), jcb, ALU.add)
+        else:
+            ci, y = decode(384, jcb, st["bk"])
+            neg = ts("wf", y, 0.0, ALU.is_lt)
+            base = tt("wf", tt("wf", y, ts("wf", y, 256.0, ALU.mult), ALU.max), ci, ALU.add)
+            h = ts("wf", ci, -1.0, ALU.mult, float(NB - w0), ALU.add)
+            off = tt("wf", tt("wf", tt("wf", wrap(WB, BKG), h, ALU.add), neg, ALU.mult), base, ALU.add)
+        RU = ts("wu", off, float(NONE - w0), ALU.min, 0.0, ALU.max)
+        snd, arr = sub(SND, 128 * t, 128 * t + 128), ap("nm", Gt + 256, Gt + 384)
+        act(snd, ind(ap("nm", w0, NONE + 16), sub(RU, 16, 24)), AF.Copy)
+        s = send([(snd, arr, nxt, small(rank), "rn%d" % t)], 1.2)
+        recv(arr, "rn%d" % t, len(small(rank - 1)), [s], 1.6)
+        act(ap("nm", Gt, Gt + 256), ind(ap("nm", w0, NONE + 16), sub(RU, 0, 16)), AF.Copy)
+        r2 = lin_("wf", rcol, 2.0, 0.0)
+        cr = lin_("wf", rcol, -1.0, 256.0)
+        tq = ts("wf", sub(t2, 16, 32), r2, ALU.is_ge, cr, ALU.mult)
+        idx = ts(sub(new("wf", 48), 32, 48), tt("wf", sub(t2, 16, 32), tq, ALU.add), rcol, ALU.subtract, 384.0, ALU.min)
+        t1 = tt("wf", cum, blk(0, 4, 2), ALU.subtract)
+        gp = ts("wf", blk(1, 4, 2), tt("wf", r2, cn, ALU.add), ALU.min, rcol, ALU.subtract)
+        cum = ts("wf", tt("wf", t1, gp, ALU.add), 4096.0, ALU.min)
+        l = tt("wf", sub(cum, 0, 16), sub(cum, 16, 32), ALU.subtract)
+        k = tt("wf", k, l, ALU.min)
+        bk = tt("wf", begw, k, ALU.add)
+        gw = ap("nm", Gt, Gt + 400 + 256 * t)
+        if t == 2:
+            return idx, cum, l, k, bk, gw
+        m = tt("wf", l, k, ALU.subtract)
+        if t == 0:
+            ix = tt("wf", ts("wf", m, 1.0, ALU.is_lt, 384.0, ALU.mult), idx, ALU.max)
+            EU = cp("wu", ix)
+            EN = EU
+        else:
+            mm_ = tt("wf", st["m"], m, ALU.min)
+            ex2 = new("wf", 32)
+            ix = tt(sub(ex2, 16, 32), lin_("wf", tt("wf", m, mm_, ALU.is_le), 384.0, 0.0), idx, ALU.max)
+            tt(sub(ex2, 0, 16), tt("wf", C400, mm_, ALU.mult), ix, ALU.max)
+            EU = cp("wu", ex2)
+            EN = sub(EU, 16, 32)
+            st["OZ"] = ts("wu", tt("wf", st["en"], mm_, ALU.mult), 4104.0, ALU.add)
+            st["mm"] = mm_
+        tt(EG, ind(gw, EN), sub(RAMPE, 0, 256), ALU.add)
+        ew = wrap(WD, EG)
+        st["EW"] = ts("wu", ew, i8k, ALU.subtract)
+        if t == 0:
+            st["en"] = ts("wf", ew, i8k, ALU.subtract, -4104.0, ALU.add)
+        act(ap("nm", [E1, E2][t], [E1, E2][t] + 256 * (t + 1)), ind(gw, EU), AF.Copy)
+        zz = tt("wf", ts("wf", k, 0.0, ALU.is_equal), DUM, ALU.mult)
+        st["VU"] = cp("wu", tt("wf", tt("wf", begm, k, ALU.add), zz, ALU.max))
+        st.update({"cum": cum, "k": k, "l": l, "m": m, "m1": lin_("wf", m, 1.0, -1.0), "m8": tt("wf", m, C16K, ALU.add),
+                   "bk": unwrap(BKR[t], bk, MY, sub(pb, 0, 256))})
+        return None
+
+    def final(idx, cum, l, k, bk, gw):
+        PC, PEN, PS = ap("xb", 0, 1024), ap("xb", 1024, 2048), ap("xb", 2048, 3072)
+        ex = ap("wf", idx[2] - 32, idx[3])
+        for s, cc in ((0, C400), (1, C656)):
+            tt(sub(ex, 16 * s, 16 * s + 16), tt("wf", ts("wf", st["m"], float(s + 1), ALU.is_ge), cc, ALU.mult), idx, ALU.max)
+        EU = cp("wu", ex)
+        cw, dw = sub(cum, 0, 16), sub(cum, 16, 32)
+        kw = tt("wf", dw, k, ALU.add)
+        unwrap(NC, tt("wf", C16K, kw, ALU.subtract), MX, sub(pa, 0, 256))
+        bkr = unwrap(NA, bk, MY, sub(pb, 0, 256))
+        q32 = ts("ri", tt("wf", cum, L255, ALU.add), 0.0625, ALU.mult, -0.46875, ALU.add)
+        pe_, pq_ = sub(q32, 0, 16), sub(q32, 16, 32)
+        OU = cp("wu", tt("wf", tt("wf", tt("wf", pq_, pe_, ALU.is_equal), C272, ALU.mult), pq_, ALU.max))
+        s4 = new("ri", 64)
+        cp(sub(s4, 0, 16), dw)
+        cp(sub(s4, 16, 32), kw)
+        for s in (1, 2):
+            tt(sub(s4, 16 + 16 * s, 32 + 16 * s), lin_("wf", kw, 1.0, float(s)), cw, ALU.min)
+        r4 = ts("ri", s4, 15, ALU.bitwise_and)
+        PU = cp("wu", r4)
+        BU = ts("wu", tt("wf", beg16, sub(r4, 0, 16), ALU.subtract), 4111.0, ALU.min)
+        fill(256, OU, NC)
+        ci, y = decode(256, JV, bkr)
+        GU = cp("wu", tt("wf", ts("wf", y, 0.0, ALU.max, 3.0, ALU.min), ts("wf", ci, 4.0, ALU.mult), ALU.add))
+        AU = ts("wu", tt("wf", wrap(WB, sub(BKG, 0, 256)), y, ALU.add), 16.0, ALU.add, 4111.0, ALU.min)
+        act(sub(HI, 0, 256), ind(PCR, GU), AF.Copy)
+        lin_(EG, ind(PCR, GU), 1.0, 4096.0)
+        hi = tt(MX, sub(HI, 1, 257), EG, ALU.subtract)
+        for s in range(4):
+            act(sub(PEN, s, 1024, 4), ind(PT, sub(PU, 16 * s, 16 * s + 16)), AF.Copy)
+        act(sub(PC, 0, 1024, 4), ind(WIN, BU), AF.Copy)
+        for s in range(3):
+            act(sub(PC, 1 + s, 1024, 4), ind(gw, sub(EU, 16 * s, 16 * s + 16)), AF.Copy)
+        scan(PS, PEN, PC, 0.0, ALU.add, ALU.max)
+        o = sub(pe, 128, 256, 1, (0, 16))
+        add("P", lambda g: g.tensor.transpose(R(o), R(l), R(IF)), [o], [l, IF], 0.45, 0.5)
+        yn = act(sub(NB2, 0, 128, 1, (0, 16)), o, AF.Copy)
+        dma([(lambda g_=g_: T.yn[g_, :], lambda g_=g_: R(sub(yn, 16 * g_, 16 * g_ + 16, 1, (0, 16)))) for g_ in range(8)], [], [yn], 2.5)
+        tcol = lin_("wf", mm(sub(pw, 8, 9), [(S15, sub(cw, 15, 16))]), 8192.0, -4096.0)
+        mk = ts(sub(pc, 0, 256), POS8, tcol, ALU.add, -1.0, ALU.max)
+        tt(sub(CODE, 1, 257), ind(WIN, AU), hi, ALU.add)
+        h3 = tt(gui, ind(PS, GU), sub(CODE, 0, 256), ALU.min)
+        v = ts(spi, h3, 4095, ALU.bitwise_and)
+        YO = tt(XS, v, mk, ALU.min)
+        dma([(lambda: T.yo[:], lambda: R(YO))], [], [YO], 2.5)
+
+    light(0, heavy(0))
+    light(1, heavy(1))
+    dma([(lambda i=i: T.db[i:128:16, 0:4112], lambda i=i: T.lin[:, i:i + 4112]) for i in range(16)], [WIN], [lin], 10.0)
+    final(*light(2, heavy(2)))
+    return ops
+
+
+def order(ops):
+    n = len(ops)
+    seen = {}
+    for i, o in enumerate(ops):
+        soft = set(o["after"])
+        hard = set()
+        for kind, regs in (("r", o["rd"]), ("w", o["wr"])):
+            for (b, lo, hi, sp) in regs:
+                ps = SCRATCH[b][0] == "psum"
+                for (j, k2, l2, h2, s2) in seen.get(b, []):
+                    hit = l2 < hi and lo < h2 and (kind == "w" or k2 == "w") and not (sp == s2 and (lo - l2) % sp)
+                    if ps and ops[j]["eng"] == "P" and o["eng"] == "P":
+                        soft.add(j)
+                    elif hit and kind == "w" and ops[j]["eng"] == o["eng"] and o["sem"] is None and ops[j]["sem"] is None:
+                        soft.add(j)
+                    elif hit or (ps and ops[j]["eng"] != o["eng"]):
+                        hard.add(j)
+        for kind, regs in (("r", o["rd"]), ("w", o["wr"])):
+            for (b, lo, hi, sp) in regs:
+                seen.setdefault(b, []).append((i, kind, lo, hi, sp))
+        o["deps"] = sorted(soft | hard)
+        o["hard"] = sorted(hard)
+    succ = [[] for _ in range(n)]
+    for i, o in enumerate(ops):
+        for j in o["deps"]:
+            succ[j].append(i)
+    lev = [0.0] * n
+    for i in range(n - 1, -1, -1):
+        lev[i] = ops[i]["lat"] + HOP + max([lev[s] for s in succ[i]] + [0.0])
+    cost = [max(o["cost"], 1e-3) for o in ops]
+    lag = {}
+    for i, o in enumerate(ops):
+        for j in o["deps"]:
+            soft = j not in o["hard"] and ops[j]["eng"] == o["eng"]
+            lag[j, i] = cost[j] if soft else max(ops[j]["lat"], cost[j]) + HOP
+
+    def place(key, back):
+        before = succ if back else [o["deps"] for o in ops]
+        after = [o["deps"] for o in ops] if back else succ
+        left = [len(b) for b in before]
+        cand = [i for i in range(n) if left[i] == 0]
+        at = [0.0] * n
+        used = {}
+        while cand:
+            i = min(cand, key=lambda c: (key[c], c))
+            cand.remove(i)
+            if back:
+                s = max([ops[i]["lat"] - cost[i]] + [at[k] + cost[k] + lag[i, k] - cost[i] for k in before[i]])
+            else:
+                s = max([0.0] + [at[j] + lag[j, i] for j in before[i]])
+            if ops[i]["eng"] is not None:
+                line = used.setdefault(ops[i]["eng"], [])
+                q = 0
+                while q < len(line) and line[q][0] < s + cost[i] - 1e-9:
+                    s = max(s, line[q][1])
+                    q += 1
+                line.insert(q, (s, s + cost[i]))
+            at[i] = s
+            for k in after[i]:
+                left[k] -= 1
+                if left[k] == 0:
+                    cand.append(k)
+        return at
+
+    best, key, seed = None, [-v for v in lev], 1
+    for it in range(ROUNDS):
+        at = place(key, False)
+        end = max(at[i] + ops[i]["lat"] for i in range(n))
+        if best is None or end < best[0]:
+            best = (end, at)
+        bk = place([-(at[i] + cost[i]) for i in range(n)], True)
+        key = []
+        for i in range(n):
+            seed = (seed * 1103515245 + 12345) % 2147483648
+            key.append(-(bk[i] + cost[i]) + JIT * seed / 2147483648.0)
+    for i in range(n):
+        ops[i]["t"] = best[1][i]
+    return sorted(range(n), key=lambda i: (best[1][i], i))
+
+
+ROUNDS, JIT = 40, 1.5
+
+
+def rank_program(g, core, T, topo):
+    rank = T.rank_of(core)
+    if rank is None:
+        return
+    ops = build(rank, core, T, topo)
+    seq = order(ops)
+    queue = {"V": g.vector, "S": g.scalar, "P": g.tensor, "G": g, "Y": g.sync}
+    pos = {i: k for k, i in enumerate(seq)}
+    marked = set()
+    known = {q: {} for q in queue}
+    keep = []
+    for i in seq:
+        last, own = {}, []
+        for j in ops[i]["hard"]:
+            if ops[j]["sem"] is not None:
+                own.append(j)
+            elif ops[j]["eng"] not in last or pos[j] > pos[last[ops[j]["eng"]]]:
+                last[ops[j]["eng"]] = j
+        e = ops[i]["eng"]
+        ws = []
+        if e is not None:
+            for j in own:
+                if known[e].get(ops[j]["sem"], -1) < 0:
+                    known[e][ops[j]["sem"]] = 1
+                    ws.append(j)
+            for e2, j in last.items():
+                if known[e].get("c" + e2, -1) < pos[j]:
+                    known[e]["c" + e2] = pos[j]
+                    ws.append(j)
+                    marked.add(j)
+        keep.append(ws)
+    val, total, waited = {}, {"V": 0, "S": 0, "P": 0, "G": 0}, set()
+    for i, ws in zip(seq, keep):
+        o = ops[i]
+        if o["eng"] is None:
+            continue
+        q = queue[o["eng"]]
+        for j in ws:
+            if ops[j]["sem"] is not None:
+                q.wait_ge(T.sem[ops[j]["sem"]], ops[j]["cnt"])
+                waited.add(j)
+            else:
+                q.wait_ge(T.sem["c" + ops[j]["eng"]], val[j])
+        ins = o["emit"](g)
+        if i in marked:
+            total[o["eng"]] += 1
+            val[i] = total[o["eng"]]
+            ins.then_inc(T.sem["c" + o["eng"]], 1)
+    for i in seq:
+        if ops[i]["sem"] is not None and i not in waited:
+            (g.sync if ops[i]["eng"] in ("Y", "S") else g).wait_ge(T.sem[ops[i]["sem"]], ops[i]["cnt"])

@@ -1,3 +1,4 @@
+import numpy as np
 from concourse.bass import DstId, RemoteDMATransfer
 from concourse.mybir import AluOpType as ALU, ActivationFunctionType as AF
 
@@ -5,7 +6,7 @@ N = 4
 F32, BF, I32, U16 = "float32", "bfloat16", "int32", "uint16"
 G2, E2, G1, E1, NB, NONE, G0, NMW = 0, 400, 912, 1312, 1568, 5664, 5680, 6080
 GB = [G0, G1, G2]
-RW, BW, IW, UW, WW = 10752, 4096, 640, 1024, 5120
+RW, BW, IW, UW, WW = 11520, 4096, 640, 1024, 5120
 SCRATCH = {
     "au0": ("sbuf", [128, 4112], BF), "au1": ("sbuf", [128, 4112], BF), "au2": ("sbuf", [128, 4112], BF),
     "xa": ("sbuf", [128, 4352], F32), "xb": ("sbuf", [128, 4352], F32),
@@ -23,8 +24,9 @@ for _k in range(8):
 SEMAPHORES = (["cV", "cS", "cP", "cG"] + ["d%d" % k for k in range(16)] + ["lo%d" % k for k in range(12)]
               + ["a1h0", "a1h1", "a2h0", "a2h1"] + ["rc%d" % t for t in range(3)] + ["rn%d" % t for t in range(3)])
 
-CY = 0.00104
-HOP = 0.10
+CUTS = [[0, 512, 1280, 2048, 2816, 3584, 3840, 4096], list(range(0, 4097, 512)), list(range(0, 4097, 512))]
+CY = 0.00092
+HOP = 0.13
 BIG = float(1 << 23)
 VG = [3, 3, 0]
 
@@ -279,7 +281,8 @@ def build(rank, core, T, topo):
     UI, US = new("rf", 128), new("rf", 128)
     add("G", lambda g: g.affine_select(R(UI), R(NBO), [[-1, 128]], ALU.is_ge, 0.0, 0, 1), [UI], [NBO], 0.44)
     add("G", lambda g: g.affine_select(R(US), R(NBO), [[-1, 128]], ALU.is_gt, 0.0, 0, 1), [US], [NBO], 0.44)
-    S15 = lin_("rf", BO, ts("wf", icol, 15.0, ALU.is_equal), 0.0)
+    i15 = act("wf", icol, AF.Relu, -14.0)
+    S15 = lin_("rf", BO, i15, 0.0)
     Z = ms(new("rb", 144), 0.0)
     ts(sub(Z, 15, 143, 16), sub(J, 0, 8), gcol, ALU.is_equal)
     SEL = [sub(Z, 15 - a, 143 - a) for a in range(16)]
@@ -295,7 +298,7 @@ def build(rank, core, T, topo):
     C656 = lin_("wf", C16, 1.0, 656.0)
     C272 = lin_("wf", C16, 1.0, 272.0)
     DUM2 = lin_("wf", C16, 1.0, 4352.0)
-    C16K = lin_("wf", C16, 16384.0, 4608.0)
+    C16K = lin_("wf", C16, 16384.0, 5632.0)
     L255 = new("wf", 32)
     ts(sub(L255, 0, 16), C16, 255.0, ALU.is_equal, 4096.0, ALU.mult)
     lin_(sub(L255, 16, 32), C16, 0.0, 0.0)
@@ -306,8 +309,8 @@ def build(rank, core, T, topo):
             ms(ap(au[k], 4096, 4104), float(1 << 21))
         if k == 2:
             ms(ap(au[k], 4104, 4112), 0.0)
-        lin_(ap("nm", GB[k] + 384, GB[k] + 400), J16, 0.0, 4096.0)
-    lin_(ap("nm", NONE, NONE + 16), J16, 0.0, 4096.0)
+        lin_(ap("nm", GB[k] + 384, GB[k] + 400), J16, 0.0, 4097.0)
+    lin_(ap("nm", NONE, NONE + 16), J16, 0.0, 4097.0)
     lin_(ap("xa", 4096, 4352), J, 0.0, 0.0)
     lin_(ap("xb", 4096, 4352), J, 0.0, 0.0)
     END, WX, CODE = new("rf", 257), new("rf", 257), new("rf", 257)
@@ -362,7 +365,12 @@ def build(rank, core, T, topo):
     act(ap("da", 4096, 4352), NG, AF.Copy)
     act(ap("db", 4096, 4352), NG, AF.Copy)
 
-    SPF = cp("rf", spi)
+    SPF = ts("rf", spi, 1.0, ALU.add)
+    u1 = new("rf", 256)
+    lin_(sub(u1, 0, 1), icol, 0.0, 1.0)
+    lin_(sub(u1, 1, 256), sub(AM, 0, 255), 8191.0 / BIG, 1.0)
+    AH = act("rf", mm(sub(pq, 256, 512), [(IF, u1), (lin_("rf", IF, -1.0 / BIG, 0.0), sub(AM, 0, 256))]), AF.Copy)
+    inv = lin_("wf", i15, 8191.0 / 8192, 1.0 / 8192)
     for h in range(2):
         o = sub(pb, 128 * h, 128 * h + 128)
         i_ = sub(SPF, h, 256, 2)
@@ -373,7 +381,7 @@ def build(rank, core, T, topo):
     pairs = [(lambda g_=g_: T.lin[g_, 16:4112], lambda g_=g_: T.st3[:, g_, :, :]) for g_ in range(8)]
     pairs += [(lambda: T.lin[:, 0:16], lambda: R(zp8)), (lambda: T.lin[:, 4112:4128], lambda: R(zp8))]
     dma(pairs, [lin], [ap("st3", 0, 256), zp8], 4.0)
-    dma([(lambda i=i: T.nm[i:128:16, NB:NB + 4096], lambda: T.lin[:, 16:4112]) for i in range(16)], [ap("nm", NB, NB + 4096)], [lin], 10.0)
+    dma([(lambda i=i: T.nm[i:128:16, NB:NB + 4096], lambda: T.lin[:, 16:4112]) for i in range(16)], [ap("nm", NB, NB + 4096)], [lin], 13.0)
     WIN = ap("db", 0, 4112)
 
     XS, SG2 = new("rf", 256), new("rb", 256)
@@ -395,11 +403,10 @@ def build(rank, core, T, topo):
         act(XS, ind(ap(x, 0, 4352), SO), AF.Copy)
         tt(ind(ap(x, 0, 4352), SO), XS, NG, ALU.add)
         terms = []
-        for k in range(8):
-            lo, hi = 512 * k, 512 * k + 512
-            scan(ap(d, lo, hi), ap("fl", lo, hi), ap(x, lo, hi), 0.0 if k == 0 else ap(d, lo - 1, lo), ALU.mult, ALU.add)
+        for lo, hi in zip(CUTS[t][:-1], CUTS[t][1:]):
+            scan(ap(d, lo, hi), ap("fl", lo, hi), ap(x, lo, hi), 0.0 if lo == 0 else ap(d, lo - 1, lo), ALU.mult, ALU.add)
             act(ap("sg", lo, hi), ap(d, lo, hi), AF.Sign, 0.5)
-            terms += [(SEL[a], ap("sg", 256 * a, 256 * a + 256)) for a in range(2 * k, 2 * k + 2)]
+            terms += [(SEL[a], ap("sg", 256 * a, 256 * a + 256)) for a in range(lo // 256, hi // 256)]
         mm(sub(pc, 0, 256), terms)
         act(SG2, sub(pc, 0, 256), AF.Sign, 1.0)
         scan(sub(WX, 1, 257), SG2, sub(ZERO, 0, 256), 0.0, ALU.add, ALU.add)
@@ -416,11 +423,11 @@ def build(rank, core, T, topo):
         cu = ts("wu", nw, 1.0 / 16384, ALU.mult)
         act(sub(BKG, 0, n), ind(bk, cu), AF.Copy)
         ci = ts("ri", nw, 1.0 / 16384, ALU.mult)
-        y = tt("wf", tt("wf", nw, jc, ALU.add), ts("wf", ci, -16384.0, ALU.mult, -4608.0, ALU.add), ALU.add)
+        y = tt("wf", tt("wf", nw, jc, ALU.add), ts("wf", ci, -16384.0, ALU.mult, -5632.0, ALU.add), ALU.add)
         return ci, y
 
     def fill(n, offs, code):
-        lin_(sub(ZW, 0, n), sub(RAMPE, 0, n), 0.0, 0.0)
+        iota(sub(ZW, 0, n), [[0, n]], 0, 0)
         cp(ind(ZW, offs), code)
         scan(sub(FIL, 0, n), sub(ZW, 0, n), sub(ZERO, 0, n), 0.0, ALU.max, ALU.max)
 
@@ -438,12 +445,24 @@ def build(rank, core, T, topo):
                 mx = tt("wf", mx, tt("wf", io, st["mm"], ALU.mult), ALU.subtract)
                 na = lin_(NA, u, -1.0, 0.0)
             tt(SGN, ind(tab, st["EW"]), na, ALU.is_lt)
-            inew = ts("wf", count16(sub(pq, 0, 16), SGN), 8.5, ALU.is_ge)
-            d = tt("wf", mx, inew, ALU.subtract)
-        x = new("wf", 32)
-        rel, sh = ts(sub(x, 0, 16), d, 0.0, ALU.max), ts(sub(x, 16, 32), d, 0.0, ALU.is_lt)
-        sc = scan("wf", x, sub(ZERO, 0, 32), 0.0, ALU.add, ALU.add)
-        mm(blk(0, 2), [(BO, sc), (US, x)])
+            xb, xj = new("wf", 32), new("wf", 32)
+            act(sub(xb, 0, 16), mx, AF.Relu, -1.0)
+            act(sub(xb, 16, 32), mx, AF.Relu, 0.0, -1.0)
+            th1 = ts("wf", mx, 1.0, ALU.is_ge, 8.5, ALU.mult)
+            th2 = ts("wf", mx, 90.0, ALU.mult, 8.5, ALU.max)
+            cnt = count16(sub(pq, 0, 16), SGN)
+            tt(sub(xj, 0, 16), cnt, th1, ALU.is_lt)
+            tt(sub(xj, 16, 32), cnt, th2, ALU.is_gt)
+            sc = scan("wf", xb, xj, 0.0, ALU.add, ALU.add)
+            x = tt("wf", xb, xj, ALU.add)
+            first = [(US, xb), (US, xj), (BO, sc)]
+        else:
+            x = new("wf", 32)
+            ts(sub(x, 0, 16), d, 0.0, ALU.max)
+            ts(sub(x, 16, 32), d, 0.0, ALU.is_lt)
+            sc = scan("wf", x, sub(ZERO, 0, 32), 0.0, ALU.add, ALU.add)
+            first = [(US, x), (BO, sc)]
+        mm(blk(0, 2), first)
         code = tt("wf", st["m8"], blk(0, 1), ALU.subtract)
         mm(sub(pw, 0, 2), [(BO, sub(sc, 15, 32, 16))])
         ex = mm(blk(2, 4), [(BO, sc), (UI, x)])
@@ -456,7 +475,7 @@ def build(rank, core, T, topo):
         s = send([(cs, cn, nxt, small(rank), "rc%d" % t)], 1.0)
         recv(cn, "rc%d" % t, len(small(rank - 1)), [s], 1.5)
         scol = tt("wf", tot, rcol, ALU.subtract)
-        c256 = ts("wf", scol, -1.0, ALU.mult, 256.0, ALU.add)
+        c256 = lin_("wf", scol, -1.0, 256.0) if t == 2 else ts("wf", scol, -1.0, ALU.mult, 256.0, ALU.add)
         t2 = tt("wf", ts("wf", x, 0.0, ALU.is_equal, 8192.0, ALU.mult), ex, ALU.add)
         p = tt("wf", ts("wf", rcx, scol, ALU.is_ge, c256, ALU.mult), sub(t2, 0, 16), ALU.add)
         OU = cp("wu", tt("wf", p, DUM2, ALU.min))
@@ -469,9 +488,10 @@ def build(rank, core, T, topo):
         else:
             ci, y = decode(384, jcb, st["bk"])
             neg = ts("wf", y, 0.0, ALU.is_lt)
-            base = tt("wf", tt("wf", y, ts("wf", y, 256.0, ALU.mult), ALU.max), ci, ALU.add)
+            base = tt("wf", tt("wf", y, lin_("wf", y, 256.0, 0.0) if t == 2 else ts("wf", y, 256.0, ALU.mult), ALU.max), ci, ALU.add)
             h = ts("wf", ci, -1.0, ALU.mult, float(NB - w0), ALU.add)
-            off = tt("wf", tt("wf", tt("wf", wrap(WB, BKG), h, ALU.add), neg, ALU.mult), base, ALU.add)
+            base = tt("wf", tt("wf", h, neg, ALU.mult), base, ALU.add)
+            off = tt("wf", tt("wf", wrap(WB, BKG), neg, ALU.mult), base, ALU.add)
         RU = ts("wu", off, float(NONE - w0), ALU.min, 0.0, ALU.max)
         snd, arr = sub(SND, 128 * t, 128 * t + 128), ap("nm", Gt + 256, Gt + 384)
         act(snd, ind(ap("nm", w0, NONE + 16), sub(RU, 16, 24)), AF.Copy)
@@ -487,37 +507,38 @@ def build(rank, core, T, topo):
         cum = ts("wf", tt("wf", t1, gp, ALU.add), 4096.0, ALU.min)
         l = tt("wf", sub(cum, 0, 16), sub(cum, 16, 32), ALU.subtract)
         k = tt("wf", k, l, ALU.min)
-        bk = tt("wf", begw, k, ALU.add)
         gw = ap("nm", Gt, Gt + 400 + 256 * t)
         if t == 2:
-            return idx, cum, l, k, bk, gw
+            return idx, cum, l, k, gw
+        bk = tt("wf", begw, k, ALU.add)
         m = tt("wf", l, k, ALU.subtract)
         if t == 0:
             ix = tt("wf", ts("wf", m, 1.0, ALU.is_lt, 384.0, ALU.mult), idx, ALU.max)
             EU = cp("wu", ix)
-            EN = EU
+            EN, en = EU, ap("nm", E1, E1 + 256)
         else:
             mm_ = tt("wf", st["m"], m, ALU.min)
             ex2 = new("wf", 32)
             ix = tt(sub(ex2, 16, 32), lin_("wf", tt("wf", m, mm_, ALU.is_le), 384.0, 0.0), idx, ALU.max)
             tt(sub(ex2, 0, 16), tt("wf", C400, mm_, ALU.mult), ix, ALU.max)
             EU = cp("wu", ex2)
-            EN = sub(EU, 16, 32)
+            EN, en = sub(EU, 16, 32), ap("nm", E2 + 256, E2 + 512)
+            act(ap("nm", E2, E2 + 256), ind(gw, sub(EU, 0, 16)), AF.Copy)
             st["OZ"] = ts("wu", tt("wf", st["en"], mm_, ALU.mult), 4104.0, ALU.add)
             st["mm"] = mm_
-        tt(EG, ind(gw, EN), sub(RAMPE, 0, 256), ALU.add)
-        ew = wrap(WD, EG)
-        st["EW"] = ts("wu", ew, i8k, ALU.subtract)
+        act(en, ind(gw, EN), AF.Copy)
+        scan(WD, AH, en, 0.0, ALU.mult, ALU.max)
+        ew = sub(WD, 15, 256, 16)
+        st["EW"] = ts("wu", ew, inv, ALU.mult, -1.0, ALU.add)
         if t == 0:
-            st["en"] = ts("wf", ew, i8k, ALU.subtract, -4104.0, ALU.add)
-        act(ap("nm", [E1, E2][t], [E1, E2][t] + 256 * (t + 1)), ind(gw, EU), AF.Copy)
+            st["en"] = ts("wf", ew, inv, ALU.mult, -4105.0, ALU.add)
         zz = tt("wf", ts("wf", k, 0.0, ALU.is_equal), DUM, ALU.mult)
         st["VU"] = cp("wu", tt("wf", tt("wf", begm, k, ALU.add), zz, ALU.max))
         st.update({"cum": cum, "k": k, "l": l, "m": m, "m1": lin_("wf", m, 1.0, -1.0), "m8": tt("wf", m, C16K, ALU.add),
                    "bk": unwrap(BKR[t], bk, MY, sub(pb, 0, 256))})
         return None
 
-    def final(idx, cum, l, k, bk, gw):
+    def final(idx, cum, l, k, gw):
         PC, PEN, PS = ap("xb", 0, 1024), ap("xb", 1024, 2048), ap("xb", 2048, 3072)
         ex = ap("wf", idx[2] - 32, idx[3])
         for s, cc in ((0, C400), (1, C656)):
@@ -525,8 +546,8 @@ def build(rank, core, T, topo):
         EU = cp("wu", ex)
         cw, dw = sub(cum, 0, 16), sub(cum, 16, 32)
         kw = tt("wf", dw, k, ALU.add)
-        unwrap(NC, tt("wf", C16K, kw, ALU.subtract), MX, sub(pa, 0, 256))
-        bkr = unwrap(NA, bk, MY, sub(pb, 0, 256))
+        unwrap(NC, tt("wf", tt("wf", C16K, st["k"], ALU.subtract), dw, ALU.subtract), MX, sub(pa, 0, 256))
+        bkr = st["bk"]
         q32 = ts("ri", tt("wf", cum, L255, ALU.add), 0.0625, ALU.mult, -0.46875, ALU.add)
         pe_, pq_ = sub(q32, 0, 16), sub(q32, 16, 32)
         OU = cp("wu", tt("wf", tt("wf", tt("wf", pq_, pe_, ALU.is_equal), C272, ALU.mult), pq_, ALU.max))
@@ -543,20 +564,20 @@ def build(rank, core, T, topo):
         GU = cp("wu", tt("wf", ts("wf", y, 0.0, ALU.max, 3.0, ALU.min), ts("wf", ci, 4.0, ALU.mult), ALU.add))
         AU = ts("wu", tt("wf", wrap(WB, sub(BKG, 0, 256)), y, ALU.add), 16.0, ALU.add, 4111.0, ALU.min)
         act(sub(HI, 0, 256), ind(PCR, GU), AF.Copy)
-        lin_(EG, ind(PCR, GU), 1.0, 4096.0)
+        lin_(EG, ind(PCR, GU), 1.0, 4097.0)
         hi = tt(MX, sub(HI, 1, 257), EG, ALU.subtract)
         for s in range(4):
             act(sub(PEN, s, 1024, 4), ind(PT, sub(PU, 16 * s, 16 * s + 16)), AF.Copy)
-        act(sub(PC, 0, 1024, 4), ind(WIN, BU), AF.Copy)
+        lin_(sub(PC, 0, 1024, 4), ind(WIN, BU), 1.0, -1.0)
         for s in range(3):
-            act(sub(PC, 1 + s, 1024, 4), ind(gw, sub(EU, 16 * s, 16 * s + 16)), AF.Copy)
+            lin_(sub(PC, 1 + s, 1024, 4), ind(gw, sub(EU, 16 * s, 16 * s + 16)), 1.0, -1.0)
         scan(PS, PEN, PC, 0.0, ALU.add, ALU.max)
         o = sub(pe, 128, 256, 1, (0, 16))
         add("P", lambda g: g.tensor.transpose(R(o), R(l), R(IF)), [o], [l, IF], 0.45, 0.5)
         yn = act(sub(NB2, 0, 128, 1, (0, 16)), o, AF.Copy)
         dma([(lambda g_=g_: T.yn[g_, :], lambda g_=g_: R(sub(yn, 16 * g_, 16 * g_ + 16, 1, (0, 16)))) for g_ in range(8)], [], [yn], 2.5)
         tcol = lin_("wf", mm(sub(pw, 8, 9), [(S15, sub(cw, 15, 16))]), 8192.0, -4096.0)
-        mk = ts(sub(pc, 0, 256), POS8, tcol, ALU.add, -1.0, ALU.max)
+        mk = lin_(sub(pc, 0, 256), act(NA, POS8, AF.Relu, tcol), 1.0, -1.0)
         tt(sub(CODE, 1, 257), ind(WIN, AU), hi, ALU.add)
         h3 = tt(gui, ind(PS, GU), sub(CODE, 0, 256), ALU.min)
         v = ts(spi, h3, 4095, ALU.bitwise_and)
@@ -565,7 +586,7 @@ def build(rank, core, T, topo):
 
     light(0, heavy(0))
     light(1, heavy(1))
-    dma([(lambda i=i: T.db[i:128:16, 0:4112], lambda i=i: T.lin[:, i:i + 4112]) for i in range(16)], [WIN], [lin], 10.0)
+    dma([(lambda i=i: T.db[i:128:16, 0:4112], lambda i=i: T.lin[:, i:i + 4112]) for i in range(16)], [WIN], [lin], 13.0)
     final(*light(2, heavy(2)))
     return ops
 
@@ -606,51 +627,63 @@ def order(ops):
             soft = j not in o["hard"] and ops[j]["eng"] == o["eng"]
             lag[j, i] = cost[j] if soft else max(ops[j]["lat"], cost[j]) + HOP
 
+    pre = [[(j, lag[j, i]) for j in ops[i]["deps"]] for i in range(n)]
+    post = [[(k, cost[k] + lag[i, k] - cost[i]) for k in succ[i]] for i in range(n)]
+    tail = [ops[i]["lat"] - cost[i] for i in range(n)]
+    eng = [o["eng"] for o in ops]
+
     def place(key, back):
-        before = succ if back else [o["deps"] for o in ops]
-        after = [o["deps"] for o in ops] if back else succ
-        left = [len(b) for b in before]
-        cand = [i for i in range(n) if left[i] == 0]
+        before = post if back else pre
+        key = list(key)
+        for i in (range(n - 1, -1, -1) if back else range(n)):
+            for j, _w in before[i]:
+                if key[i] <= key[j]:
+                    key[i] = key[j] + 1e-6
         at = [0.0] * n
-        used = {}
-        while cand:
-            i = min(cand, key=lambda c: (key[c], c))
-            cand.remove(i)
-            if back:
-                s = max([ops[i]["lat"] - cost[i]] + [at[k] + cost[k] + lag[i, k] - cost[i] for k in before[i]])
-            else:
-                s = max([0.0] + [at[j] + lag[j, i] for j in before[i]])
-            if ops[i]["eng"] is not None:
-                line = used.setdefault(ops[i]["eng"], [])
-                q = 0
-                while q < len(line) and line[q][0] < s + cost[i] - 1e-9:
-                    s = max(s, line[q][1])
+        used = {e: ([], []) for e in eng}
+        for i in sorted(range(n), key=lambda c: key[c]):
+            s = tail[i] if back else 0.0
+            for j, w in before[i]:
+                if at[j] + w > s:
+                    s = at[j] + w
+            if eng[i] is not None:
+                lo, hi = used[eng[i]]
+                q = len(lo)
+                while q and hi[q - 1] > s + 1e-9:
+                    q -= 1
+                while q < len(lo) and lo[q] < s + cost[i] - 1e-9:
+                    s = max(s, hi[q])
                     q += 1
-                line.insert(q, (s, s + cost[i]))
+                lo.insert(q, s)
+                hi.insert(q, s + cost[i])
             at[i] = s
-            for k in after[i]:
-                left[k] -= 1
-                if left[k] == 0:
-                    cand.append(k)
         return at
 
-    best, key, seed = None, [-v for v in lev], 1
-    for it in range(ROUNDS):
-        at = place(key, False)
-        end = max(at[i] + ops[i]["lat"] for i in range(n))
-        if best is None or end < best[0]:
-            best = (end, at)
-        bk = place([-(at[i] + cost[i]) for i in range(n)], True)
-        key = []
-        for i in range(n):
-            seed = (seed * 1103515245 + 12345) % 2147483648
-            key.append(-(bk[i] + cost[i]) + JIT * seed / 2147483648.0)
+    def span(at):
+        return max(at[i] + ops[i]["lat"] for i in range(n))
+
+    shape = (n, ROUNDS, round(sum(lev), 3))
+    if shape not in KNOWN:
+        rng = np.random.default_rng(1)
+        at = place([-v for v in lev], False)
+        best = (span(at), at)
+        for it in range(ROUNDS):
+            mid, half, amp = rng.random() * best[0], 2 + 12 * rng.random(), JIT * rng.random()
+            noise = rng.random(n) * amp
+            at = place([t + (noise[i] if abs(t - mid) < half else 0.5 * amp) for i, t in enumerate(best[1])], False)
+            bk = place([-(at[i] + cost[i]) for i in range(n)], True)
+            at = place([-(bk[i] + cost[i]) for i in range(n)], False)
+            end = span(at)
+            if end <= best[0] + 0.02:
+                best = (end, at)
+        KNOWN[shape] = best[1]
     for i in range(n):
-        ops[i]["t"] = best[1][i]
-    return sorted(range(n), key=lambda i: (best[1][i], i))
+        ops[i]["t"] = KNOWN[shape][i]
+    return sorted(range(n), key=lambda i: (KNOWN[shape][i], i))
 
 
-ROUNDS, JIT = 40, 1.5
+KNOWN = {}
+ROUNDS, JIT = 3000, 4.0
 
 
 def rank_program(g, core, T, topo):

@@ -4,15 +4,18 @@ from concourse.mybir import AluOpType as ALU, ActivationFunctionType as AF
 
 N = 4
 F32, BF, I32, U16 = "float32", "bfloat16", "int32", "uint16"
-G2, E2, G1, E1, NB, NONE, G0, NMW = 0, 400, 912, 1312, 1568, 5664, 5680, 6080
+NB, E1, G1, E2A, G0, XA, ST = 0, 4112, 4368, 4768, 5024, 5424, 9776
+E2B = E2A + 8192
+G2 = E2B + 256
+NMW = G2 + 400
 GB = [G0, G1, G2]
-RW, BW, IW, UW, WW = 11520, 4096, 640, 1024, 5120
+RW, BW, IW, UW, WW = 7680, 4608, 640, 1024, 4608
 SCRATCH = {
     "au0": ("sbuf", [128, 4112], BF), "au1": ("sbuf", [128, 4112], BF), "au2": ("sbuf", [128, 4112], BF),
-    "xa": ("sbuf", [128, 4352], F32), "xb": ("sbuf", [128, 4352], F32),
+    "xb": ("sbuf", [128, 4352], F32),
     "da": ("sbuf", [128, 4352], F32), "db": ("sbuf", [128, 4352], F32),
     "fl": ("sbuf", [128, 4352], BF), "sg": ("sbuf", [128, 4096], BF),
-    "nm": ("sbuf", [128, NMW], F32), "zw": ("sbuf", [128, 4608], F32),
+    "nm": ("sbuf", [128, NMW], F32), "zw": ("sbuf", [128, 768 + 9024], BF),
     "rf": ("sbuf", [128, RW], F32), "rb": ("sbuf", [128, BW], BF), "ri": ("sbuf", [128, IW], I32),
     "wu": ("sbuf", [128, UW], U16), "wf": ("sbuf", [128, WW], F32),
     "spi": ("sbuf", [128, 256], I32), "gui": ("sbuf", [128, 256], I32), "lni": ("sbuf", [128, 256], I32),
@@ -28,7 +31,8 @@ CUTS = [[0, 512, 1280, 2048, 2816, 3584, 3840, 4096], list(range(0, 4097, 512)),
 CY = 0.00092
 HOP = 0.13
 BIG = float(1 << 23)
-VG = [3, 3, 0]
+HOLD = float(1 << 24)
+VG = [4, 4, 2]
 
 
 def ap(name, lo, hi, step=1, parts=None):
@@ -73,7 +77,7 @@ def in_psum(a):
 
 def build(rank, core, T, topo):
     ops = []
-    free = {"rf": 0, "rb": 0, "ri": 0, "wu": 0, "wf": 0}
+    free = {"rf": 0, "rb": 0, "ri": 0, "wu": 0, "wf": 0, "nm": ST}
 
     def R(a):
         if not isinstance(a, tuple):
@@ -89,7 +93,7 @@ def build(rank, core, T, topo):
     def new(buf, n):
         lo = free[buf]
         free[buf] = lo + (n + 15) // 16 * 16
-        assert free[buf] <= SCRATCH[buf][1][1], buf
+        assert free[buf] <= (E2B if buf == "nm" else SCRATCH[buf][1][1]), buf
         return ap(buf, lo, lo + n)
 
     def add(eng, emit, outs, ins, cost, lat=None, sem=None, cnt=0, after=()):
@@ -254,71 +258,76 @@ def build(rank, core, T, topo):
             send([(ap("au1", lo, hi), ap("au2", lo, hi), prv, topo.engines(core, prv), "a2h%d" % h)], 4.0)
 
     pi = iota(new("ri", 1), [[0, 1]], 0, 1)
-    JB = iota(new("rf", 128), [[1, 8], [0, 16]], 0, 0)
-    RAMPE = iota(new("rf", 384), [[0, 24], [8192, 16]], 0, 0)
-    J = iota(new("rf", 256), [[1, 256]], 0, 0)
-    PCR = iota(new("rf", 1024), [[8192, 1024]], 8192, 0)
+    JB = iota(new("nm", 128), [[1, 8], [0, 16]], 0, 0)
+    RB = iota(new("rb", 384), [[0, 24], [2048, 16]], 0, 0)
+    J = iota(new("nm", 368), [[1, 368]], 0, 0)
+    PCR = iota(new("nm", 1024), [[8192, 1024]], 8192, 0)
+    CROW = iota(new("rb", 256), [[1, 256]], 1, 0)
+    iota(ap("zw", 256, 1152), [[0, 896]], 0, 0)
+    iota(ap("nm", XA + 4096, XA + 4352), [[0, 256]], 0, 0)
+    iota(ap("xb", 4096, 4352), [[0, 256]], 0, 0)
     J16, J128 = sub(J, 0, 16), sub(J, 0, 128)
     FL = ap("fl", 0, 4352)
-    ZERO = ms(new("rb", 384), 0.0)
+    ZERO = ms(ap("zw", 0, 256), 0.0)
     pcol = cp("wf", pi)
     B8 = sub(new("rf", 128), 0, 128, 1, (0, 8))
     ts(B8, sub(JB, 0, 128, 1, (0, 8)), sub(pcol, 0, 1, 1, (0, 8)), ALU.is_equal)
     ii = ts("ri", pi, 15, ALU.bitwise_and)
     gi = ts("ri", pi, 4, ALU.arith_shift_right)
     icol, gcol = cp("wf", ii), cp("wf", gi)
-    i8k = ts("wf", ii, 8192.0, ALU.mult)
-    AM = ts("rf", RAMPE, i8k, ALU.is_equal, BIG, ALU.mult)
-    C16 = ts("wf", J16, 16.0, ALU.mult, icol, ALU.add)
+    i2k = ts("wf", ii, 2048.0, ALU.mult)
+    AM = ts("rb", RB, i2k, ALU.is_equal, BIG, ALU.mult)
+    JJ = lin_("wf", sub(J, 0, 24), 16.0, icol)
+    C16 = sub(JJ, 0, 16)
     DUM = lin_("wf", C16, 1.0, 4096.0)
     ms(FL, 1.0)
-    IF = ts("rf", J128, pcol, ALU.is_equal)
-    BO = ts("rf", JB, gcol, ALU.is_equal)
-    BOS = lin_("rf", BO, 1.0 / BIG, 0.0)
+    IF = ts("nm", J128, pcol, ALU.is_equal)
+    BO = ts("nm", JB, gcol, ALU.is_equal)
+    BOS = lin_("nm", BO, 1.0 / BIG, 0.0)
     BOP = lin_("rb", BO, 0.25, 0.0)
     BON = lin_("rb", BO, -0.25, 0.0)
-    NBO = lin_("rf", BO, -1.0, 0.0)
-    UI, US = new("rf", 128), new("rf", 128)
+    NBO = lin_("nm", BO, -1.0, 0.0)
+    UI, US = new("nm", 128), new("nm", 128)
     add("G", lambda g: g.affine_select(R(UI), R(NBO), [[-1, 128]], ALU.is_ge, 0.0, 0, 1), [UI], [NBO], 0.44)
     add("G", lambda g: g.affine_select(R(US), R(NBO), [[-1, 128]], ALU.is_gt, 0.0, 0, 1), [US], [NBO], 0.44)
     i15 = act("wf", icol, AF.Relu, -14.0)
-    S15 = lin_("rf", BO, i15, 0.0)
-    Z = ms(new("rb", 144), 0.0)
-    ts(sub(Z, 15, 143, 16), sub(J, 0, 8), gcol, ALU.is_equal)
+    S15 = lin_("nm", BO, i15, 0.0)
+    Z = iota(new("rb", 144), [[0, 144]], 0, 0)
+    ts(sub(Z, 15, 143, 16), sub(J, 0, 8), gcol, ALU.is_equal, 1.0 / 32, ALU.mult)
     SEL = [sub(Z, 15 - a, 143 - a) for a in range(16)]
     ni8k = lin_("wf", icol, -8192.0, 0.0)
-    i256 = lin_("wf", icol, -256.0, 0.5)
+    i256 = lin_("wf", icol, -256.0, -127.5)
     i256p = lin_("wf", icol, -256.0, -255.5)
-    POS8 = lin_("rf", J, -131072.0, ni8k)
-    RB = lin_("rb", sub(RAMPE, 0, 256), 0.25, 0.0)
+    POS8 = lin_("nm", sub(J, 0, 256), -131072.0, ni8k)
     PT = lin_("wf", ts("wf", J16, icol, ALU.is_le), -2 * BIG - 8192.0, 8192.0)
     JO = cp("wu", J16)
     JV = lin_("wf", C16, 16.0, 16.0)
-    C400 = lin_("wf", C16, 1.0, 400.0)
-    C656 = lin_("wf", C16, 1.0, 656.0)
-    C272 = lin_("wf", C16, 1.0, 272.0)
-    DUM2 = lin_("wf", C16, 1.0, 4352.0)
+    CE = new("wf", 32)
+    lin_(sub(CE, 0, 16), C16, 1.0, float(E2A - G2))
+    CM = lin_(sub(CE, 16, 32), C16, 1.0, float(E2B - G2))
+    C272 = tt("wf", lin_("wf", C16, 1.0, 272.0), act("wf", C16, AF.Sign, 255.0, -1.0), ALU.mult)
+    CD = lin_("wf", C16, 1.0, 4400.0)
     C16K = lin_("wf", C16, 16384.0, 5632.0)
-    L255 = new("wf", 32)
-    ts(sub(L255, 0, 16), C16, 255.0, ALU.is_equal, 4096.0, ALU.mult)
-    lin_(sub(L255, 16, 32), C16, 0.0, 0.0)
-    JW = new("wf", 24)
-    lin_(sub(JW, 0, 16), C16, 1.0, 0.0)
+    RST = act("wf", sub(J, 0, 32), AF.Sign, -16.0)
+    RST = act("wf", RST, AF.Square)
+    T2B = new("wf", 32)
+    lin_(sub(T2B, 16, 32), J16, 0.0, 0.0)
+    AH16 = tt("wf", ts("wf", J16, icol, ALU.not_equal), ts("wf", J16, lin_("wf", icol, 1.0, 1.0), ALU.is_equal, HOLD - 1, ALU.mult), ALU.add)
+    AH = act("rb", ind(AH16, ts("wu", sub(ZERO, 0, 24), icol, ALU.add)), AF.Copy)
+    inv = lin_("wf", i15, 1.0 - 1.0 / HOLD, 1.0 / HOLD)
     for k in range(3):
         if k:
-            ms(ap(au[k], 4096, 4104), float(1 << 21))
+            lin_(ap(au[k], 4096, 4104), sub(J, 0, 8), 0.0, float(1 << 21))
         if k == 2:
-            ms(ap(au[k], 4104, 4112), 0.0)
+            lin_(ap(au[k], 4104, 4112), sub(J, 0, 8), 0.0, 0.0)
         lin_(ap("nm", GB[k] + 384, GB[k] + 400), J16, 0.0, 4097.0)
-    lin_(ap("nm", NONE, NONE + 16), J16, 0.0, 4097.0)
-    lin_(ap("xa", 4096, 4352), J, 0.0, 0.0)
-    lin_(ap("xb", 4096, 4352), J, 0.0, 0.0)
-    END, WX, CODE = new("rf", 257), new("rf", 257), new("rf", 257)
+    END, WX, CODE, NC = new("rf", 257), new("rf", 257), new("rf", 257), new("rf", 257)
     T1, T2 = new("rb", 272), new("rb", 272)
     HI = new("rf", 257)
     for b in (END, WX):
         lin_(sub(b, 0, 1), icol, 0.0, 0.0)
     lin_(sub(CODE, 0, 1), icol, 0.0, BIG)
+    lin_(sub(NC, 0, 1), icol, 0.0, 8192001.0)
     lin_(sub(HI, 256, 257), icol, 0.0, 0.0)
     lin_(sub(T1, 0, 16), J16, 0.0, 0.0)
     ZP = lin_("wf", J16, 0.0, 0.0)
@@ -332,45 +341,45 @@ def build(rank, core, T, topo):
         scan(sub(out, 0, n), sub(AM, 0, n), row, 0.0, ALU.add, ALU.min)
         return sub(out, 15, n, 16)
 
+    def hold(out, row):
+        n = count(row)
+        scan(sub(out, 0, n), sub(AH, 0, n), row, 0.0, ALU.mult, ALU.max)
+        return sub(out, 15, n, 16)
+
     def unwrap(out, w, mx, ps):
         tt(mx, ind(w, JO), sub(AM, 0, 256), ALU.mult)
         mm(ps, [(BOS, mx)])
         return act(out, ps, AF.Copy)
 
-    def count16(ps, row):
-        return mm(ps, [(SEL[a], sub(row, a, 256, 16)) for a in range(16)])
+    def pick(row):
+        return [(SEL[a], sub(row, a, 256, 16)) for a in range(16)]
 
     SPU = cp("wu", spi)
     lnf = cp(sub(new("rf", 256), 0, 256, 1, (0, 8)), lni)
     pn = mm(sub(pa, 0, 256), [(B8, lnf)])
-    scan(sub(END, 1, 257), pn, sub(ZERO, 0, 256), 0.0, ALU.add, ALU.add)
+    scan(sub(END, 1, 257), pn, ZERO, 0.0, ALU.add, ALU.add)
+    W0 = new("nm", 512)
+    endw = wrap(sub(W0, 0, 256), sub(END, 1, 257))
+    begw = wrap(sub(W0, 256, 512), sub(END, 0, 256))
+    cum0 = sub(W0, 15, 512, 16)
     WA, WB, WC, WD = new("rf", 384), new("rf", 384), new("rf", 256), new("rf", 256)
-    cum0 = new("wf", 32)
-    endw = cp(sub(cum0, 0, 16), wrap(WA, sub(END, 1, 257)))
-    begw = cp(sub(cum0, 16, 32), wrap(WB, sub(END, 0, 256)))
     SO = cp("wu", tt("wf", tt("wf", tt("wf", endw, begw, ALU.is_equal), DUM, ALU.mult), begw, ALU.max))
-    NG = ts("rf", gui, -1.0, ALU.mult)
-    cp(ind(FL, SO), sub(ZERO, 0, 256))
+    NG = ts(ap("da", 4096, 4352), gui, -1.0, ALU.mult)
+    cp(ind(FL, SO), ZERO)
     UO = cp("wu", ts("ri", cp("ri", endw), 255, ALU.bitwise_and))
     LT = act("rb", END, AF.Sign, i256p)
-    GE = act("rb", sub(END, 1, 257), AF.Sign, i256)
-    EQ = tt("rb", GE, sub(LT, 1, 257), ALU.subtract)
+    EQ = ts("rb", act("rf", sub(END, 1, 257), AF.Abs, i256), 128.0, ALU.is_lt, 2.0, ALU.mult)
     nw0 = tt("wf", endw, begw, ALU.subtract)
     beg16 = lin_("wf", begw, 1.0, 16.0)
-    begm = lin_("wf", begw, 1.0, -1.0)
+    begO = lin_("wf", begw, 1.0, 16896.0)
+    DUMO = lin_("wf", C16, 1.0, 4096.0 + 16897.0)
     SG1, SGN = new("rb", 256), new("rb", 256)
     act(SG1, NG, AF.Sign, 0.5)
-    zw = ts("wf", count16(sub(pe, 0, 16), SG1), -1.0, ALU.is_lt)
+    zw = ts("wf", mm(sub(pe, 0, 16), pick(SG1)), -1.0 / 32, ALU.is_lt)
     stat = tt("wf", lin_("wf", nw0, -0.5, ni8k), zw, ALU.subtract)
-    act(ap("da", 4096, 4352), NG, AF.Copy)
     act(ap("db", 4096, 4352), NG, AF.Copy)
 
     SPF = ts("rf", spi, 1.0, ALU.add)
-    u1 = new("rf", 256)
-    lin_(sub(u1, 0, 1), icol, 0.0, 1.0)
-    lin_(sub(u1, 1, 256), sub(AM, 0, 255), 8191.0 / BIG, 1.0)
-    AH = act("rf", mm(sub(pq, 256, 512), [(IF, u1), (lin_("rf", IF, -1.0 / BIG, 0.0), sub(AM, 0, 256))]), AF.Copy)
-    inv = lin_("wf", i15, 8191.0 / 8192, 1.0 / 8192)
     for h in range(2):
         o = sub(pb, 128 * h, 128 * h + 128)
         i_ = sub(SPF, h, 256, 2)
@@ -381,191 +390,180 @@ def build(rank, core, T, topo):
     pairs = [(lambda g_=g_: T.lin[g_, 16:4112], lambda g_=g_: T.st3[:, g_, :, :]) for g_ in range(8)]
     pairs += [(lambda: T.lin[:, 0:16], lambda: R(zp8)), (lambda: T.lin[:, 4112:4128], lambda: R(zp8))]
     dma(pairs, [lin], [ap("st3", 0, 256), zp8], 4.0)
-    dma([(lambda i=i: T.nm[i:128:16, NB:NB + 4096], lambda: T.lin[:, 16:4112]) for i in range(16)], [ap("nm", NB, NB + 4096)], [lin], 13.0)
+    dma([(lambda i=i: T.nm[i:128:16, NB:NB + 4112], lambda: T.lin[:, 16:4128]) for i in range(16)], [ap("nm", NB, NB + 4112)], [lin], 13.0)
     WIN = ap("db", 0, 4112)
+    assert free["nm"] == E2B
 
     XS, SG2 = new("rf", 256), new("rb", 256)
-    NC, FIL, BKG, MX, MY, NA, NB2, EG = [new("rf", n) for n in (256, 384, 384, 256, 256, 256, 256, 256)]
-    BKR = [new("rf", 256), new("rf", 256)]
+    FIL, BKG, MX, NA, NB2, BKR = [new("rf", n) for n in (256, 384, 256, 256, 256, 256)]
+    FIB, WAB = new("rb", 384), new("rb", 384)
     SND = new("rf", 384)
-    ZW = ap("zw", 0, 4608)
-    st = {"cum": cum0, "k": nw0, "l": nw0, "bk": sub(END, 1, 257), "m8": endw}
+    ZF = new("rf", 528)
+    iota(sub(ZF, 0, 256), [[0, 256]], 0, 0)
+    st = {"cum": cum0, "k": nw0, "l": nw0}
 
     def heavy(t):
-        x, d = ["xa", "xb", "xa"][t], ["da", "db", "da"][t]
+        x = [ap("nm", XA, XA + 4352), ap("xb", 0, 4352)][t % 2]
+        d = ap(["da", "db"][t % 2], 0, 4352)
         tab = ap(au[t], 0, 4096)
         for k in range(8):
-            o, src = ap(x, 512 * k, 512 * k + 512), ind(tab, sub(SPU, 32 * k, 32 * k + 32))
+            o, src = sub(x, 512 * k, 512 * k + 512), ind(tab, sub(SPU, 32 * k, 32 * k + 32))
             if k >= 8 - VG[t]:
                 cp(o, src)
             else:
                 act(o, src, AF.Copy)
-        act(XS, ind(ap(x, 0, 4352), SO), AF.Copy)
-        tt(ind(ap(x, 0, 4352), SO), XS, NG, ALU.add)
+        act(XS, ind(x, SO), AF.Copy)
+        tt(ind(x, SO), XS, NG, ALU.add)
         terms = []
         for lo, hi in zip(CUTS[t][:-1], CUTS[t][1:]):
-            scan(ap(d, lo, hi), ap("fl", lo, hi), ap(x, lo, hi), 0.0 if lo == 0 else ap(d, lo - 1, lo), ALU.mult, ALU.add)
-            act(ap("sg", lo, hi), ap(d, lo, hi), AF.Sign, 0.5)
+            scan(sub(d, lo, hi), ap("fl", lo, hi), sub(x, lo, hi), 0.0 if lo == 0 else sub(d, lo - 1, lo), ALU.mult, ALU.add)
+            act(ap("sg", lo, hi), sub(d, lo, hi), AF.Sign, 0.5)
             terms += [(SEL[a], ap("sg", 256 * a, 256 * a + 256)) for a in range(lo // 256, hi // 256)]
         mm(sub(pc, 0, 256), terms)
-        act(SG2, sub(pc, 0, 256), AF.Sign, 1.0)
-        scan(sub(WX, 1, 257), SG2, sub(ZERO, 0, 256), 0.0, ALU.add, ALU.add)
+        act(SG2, sub(pc, 0, 256), AF.Sign, 1.0 / 32)
+        scan(sub(WX, 1, 257), SG2, ZERO, 0.0, ALU.add, ALU.add)
         tt(sub(T1, 16, 272), ind(WX, UO), EQ, ALU.mult)
         lin_(sub(T2, 15, 272), LT, sub(WX, 256, 257), 0.0)
-        mm(sub(pd, 0, 256), [(BOP, RB), (BOP, sub(T2, 16, 272)), (BON, sub(T2, 15, 271)), (BOP, sub(T1, 16, 272)), (BON, sub(T1, 15, 271))])
-        w = wrap(WC, sub(pd, 0, 256))
-        if t == 0:
-            return tt("wf", w, tt("wf", stat, nw0, ALU.add), ALU.add)
-        return tt("wf", w, stat, ALU.add)
-
-    def decode(n, jc, bk):
-        nw = wrap(WA, sub(FIL, 0, n))
-        cu = ts("wu", nw, 1.0 / 16384, ALU.mult)
-        act(sub(BKG, 0, n), ind(bk, cu), AF.Copy)
-        ci = ts("ri", nw, 1.0 / 16384, ALU.mult)
-        y = tt("wf", tt("wf", nw, jc, ALU.add), ts("wf", ci, -16384.0, ALU.mult, -5632.0, ALU.add), ALU.add)
-        return ci, y
-
-    def fill(n, offs, code):
-        iota(sub(ZW, 0, n), [[0, n]], 0, 0)
-        cp(ind(ZW, offs), code)
-        scan(sub(FIL, 0, n), sub(ZW, 0, n), sub(ZERO, 0, n), 0.0, ALU.max, ALU.max)
+        mm(sub(pd, 0, 256), [(BOP, sub(RB, 0, 256)), (BOP, sub(T2, 16, 272)), (BON, sub(T2, 15, 271)), (BOP, sub(T1, 16, 272)), (BON, sub(T1, 15, 271))])
+        return tt("wf", wrap(WC, sub(pd, 0, 256)), tt("wf", stat, st["l"], ALU.add), ALU.add)
 
     def light(t, d):
         Gt = GB[t]
-        cum, k, l = st["cum"], st["k"], st["l"]
+        cum, k = st["cum"], st["k"]
+        x = new("wf", 32)
+        x0, x1 = sub(x, 0, 16), sub(x, 16, 32)
         if t:
             tab = ap(au[t], 0, 4112 if t == 2 else 4104)
-            mx = tt("wf", tt("wf", d, l, ALU.add), st["m1"], ALU.max)
-            na = lin_(NA, ind(ap(["da", "db", "da"][t], 0, 4352), st["VU"]), -1.0, 0.0)
+            terms = [(IF, tt("wf", d, st["mq"], ALU.max))]
+            dk = ind(ap(["da", "db"][t % 2], 0, 4352), st["VU"])
             if t == 2:
-                u = tt(NB2, ind(tab, st["OZ"]), na, ALU.subtract)
+                u = tt(NB2, ind(tab, st["OZ"]), act(NA, dk, AF.Copy), ALU.add)
                 act(SG1, u, AF.Sign, 0.5)
-                io = ts("wf", count16(sub(pe, 16, 32), SG1), -1.0, ALU.is_lt)
-                mx = tt("wf", mx, tt("wf", io, st["mm"], ALU.mult), ALU.subtract)
+                terms.append((IF, ts("wf", mm(sub(pe, 16, 32), pick(SG1)), -1.0 / 32, ALU.is_gt)))
                 na = lin_(NA, u, -1.0, 0.0)
-            tt(SGN, ind(tab, st["EW"]), na, ALU.is_lt)
-            xb, xj = new("wf", 32), new("wf", 32)
-            act(sub(xb, 0, 16), mx, AF.Relu, -1.0)
-            act(sub(xb, 16, 32), mx, AF.Relu, 0.0, -1.0)
-            th1 = ts("wf", mx, 1.0, ALU.is_ge, 8.5, ALU.mult)
-            th2 = ts("wf", mx, 90.0, ALU.mult, 8.5, ALU.max)
-            cnt = count16(sub(pq, 0, 16), SGN)
-            tt(sub(xj, 0, 16), cnt, th1, ALU.is_lt)
-            tt(sub(xj, 16, 32), cnt, th2, ALU.is_gt)
-            sc = scan("wf", xb, xj, 0.0, ALU.add, ALU.add)
-            x = tt("wf", xb, xj, ALU.add)
-            first = [(US, xb), (US, xj), (BO, sc)]
+            else:
+                na = lin_(NA, dk, -1.0, 0.0)
+            tt(SGN, ind(tab, st["EW"]), na, ALU.is_ge)
+            v = mm(sub(pq, 0, 16), terms + pick(SGN))
+            c0 = 23.5 / 32 + (t - 1)
+            d = ts("ri", v, -c0, ALU.add)
+            ts(x1, v, c0 - 0.5, ALU.is_lt)
+            e = ts("wf", v, c0 + 0.5, ALU.is_lt)
         else:
-            x = new("wf", 32)
-            ts(sub(x, 0, 16), d, 0.0, ALU.max)
-            ts(sub(x, 16, 32), d, 0.0, ALU.is_lt)
-            sc = scan("wf", x, sub(ZERO, 0, 32), 0.0, ALU.add, ALU.add)
-            first = [(US, x), (BO, sc)]
-        mm(blk(0, 2), first)
-        code = tt("wf", st["m8"], blk(0, 1), ALU.subtract)
+            ts(x1, d, 0.0, ALU.is_lt)
+            e = ts("wf", d, 0.5, ALU.is_lt)
+        ts(x0, d, 0.0, ALU.max)
+        tt(sub(T2B, 0, 16), e, CD, ALU.mult)
+        sc = scan("wf", RST, x, 0.0, ALU.mult, ALU.add)
         mm(sub(pw, 0, 2), [(BO, sub(sc, 15, 32, 16))])
-        ex = mm(blk(2, 4), [(BO, sc), (UI, x)])
-        rcx = blk(2, 3)
-        rt = cp("wf", sub(pw, 0, 2))
-        rcol, tot = sub(rt, 0, 1), sub(rt, 1, 2)
-        unwrap(NC, code, MX, sub(pa, 0, 256))
+        ex = mm(sub(pb, 0, 32), [(UI, x), (IF, T2B), (BO, sc)])
+        mm(blk(0, 2), [(US, x), (BO, sc)])
+        mm(blk(2, 4), [(UI, x), (BO, sc)])
+        mn = ts("wf", sub(pw, 0, 1), sub(pw, 1, 2), ALU.min, -256.0, ALU.add)
         cs, cn = ap("cs", 4 * t, 4 * t + 1), ap("cn", 4 * t, 4 * t + 1)
-        ts(cs, ts("wf", rcol, 2.0, ALU.mult, tot, ALU.subtract), 0.0, ALU.max, 128.0, ALU.min)
+        OU = ts("wu", sub(ex, 0, 16), mn, ALU.subtract)
+        ts(cs, sub(pw, 0, 1), mn, ALU.subtract, 384.0, ALU.min)
         s = send([(cs, cn, nxt, small(rank), "rc%d" % t)], 1.0)
         recv(cn, "rc%d" % t, len(small(rank - 1)), [s], 1.5)
-        scol = tt("wf", tot, rcol, ALU.subtract)
-        c256 = lin_("wf", scol, -1.0, 256.0) if t == 2 else ts("wf", scol, -1.0, ALU.mult, 256.0, ALU.add)
-        t2 = tt("wf", ts("wf", x, 0.0, ALU.is_equal, 8192.0, ALU.mult), ex, ALU.add)
-        p = tt("wf", ts("wf", rcx, scol, ALU.is_ge, c256, ALU.mult), sub(t2, 0, 16), ALU.add)
-        OU = cp("wu", tt("wf", p, DUM2, ALU.min))
-        lin_(sub(JW, 16, 24), sub(C16, 0, 8), 1.0, scol)
-        jcb = tt("wf", ts("wf", JW, rcol, ALU.is_ge, 8192.0, ALU.mult), JW, ALU.add)
-        fill(384, OU, NC)
-        w0 = [NB, E1, E2][t]
+        jj = lin_("wf", JJ, 1.0, mn)
         if t == 0:
-            off = tt("wf", wrap(WA, FIL), jcb, ALU.add)
+            pay = tt("wf", tt("wf", endw, x0, ALU.subtract), sub(ex, 0, 16), ALU.subtract)
         else:
-            ci, y = decode(384, jcb, st["bk"])
-            neg = ts("wf", y, 0.0, ALU.is_lt)
-            base = tt("wf", tt("wf", y, lin_("wf", y, 256.0, 0.0) if t == 2 else ts("wf", y, 256.0, ALU.mult), ALU.max), ci, ALU.add)
-            h = ts("wf", ci, -1.0, ALU.mult, float(NB - w0), ALU.add)
-            base = tt("wf", tt("wf", h, neg, ALU.mult), base, ALU.add)
-            off = tt("wf", tt("wf", wrap(WB, BKG), neg, ALU.mult), base, ALU.add)
-        RU = ts("wu", off, float(NONE - w0), ALU.min, 0.0, ALU.max)
+            rm = tt("wf", x0, st["m"], ALU.subtract)
+            off = tt("wf", tt("wf", st["bk"], rm, ALU.subtract), ts("wf", rm, 512.0, ALU.min, 8192.0, ALU.mult), ALU.add)
+            pay = tt("wf", ts("wf", sub(ex, 0, 16), 8191.0, ALU.mult), off, ALU.add)
+        idx = ts(sub(new("wf", 48), 32, 48), sub(ex, 16, 32), mn, ALU.subtract, 384.0, ALU.min)
+        unwrap(sub(NC, 1, 257), pay, MX, sub(pa, 0, 256))
+        zo = 768 - 384 * t
+        cp(ind(ap("zw", zo, 768 + 9024), OU), CROW)
+        scan(FIB, ap("zw", zo, zo + 384), ap("zw", zo, zo + 384), 0.0, ALU.max, ALU.max)
+        c1 = wrap(WAB, FIB)
+        act(BKG, ind(NC, cp("wu", c1)), AF.Copy)
+        top = [4112, E1 + 256, E2B + 256][t]
+        if t == 0:
+            RU = ts("wu", tt("wf", wrap(WA, BKG), jj, ALU.add), top - 1.0, ALU.min)
+        else:
+            cj = tt("wf", c1, lin_("wf", jj, 8192.0, 16384.0 + 511.0 + [0, E1, E2A][t]), ALU.add)
+            p = ts("ri", hold(WA, BKG), inv, ALU.mult)
+            far = tt("wf", tt("wf", cj, p, ALU.subtract), jj, ALU.max)
+            RU = ts("wu", tt("wf", far, ts("ri", p, 8191, ALU.bitwise_and), ALU.add), -512.0, ALU.add, top - 1.0, ALU.min)
         snd, arr = sub(SND, 128 * t, 128 * t + 128), ap("nm", Gt + 256, Gt + 384)
-        act(snd, ind(ap("nm", w0, NONE + 16), sub(RU, 16, 24)), AF.Copy)
+        act(snd, ind(ap("nm", NB, top), sub(RU, 16, 24)), AF.Copy)
         s = send([(snd, arr, nxt, small(rank), "rn%d" % t)], 1.2)
         recv(arr, "rn%d" % t, len(small(rank - 1)), [s], 1.6)
-        act(ap("nm", Gt, Gt + 256), ind(ap("nm", w0, NONE + 16), sub(RU, 0, 16)), AF.Copy)
-        r2 = lin_("wf", rcol, 2.0, 0.0)
-        cr = lin_("wf", rcol, -1.0, 256.0)
-        tq = ts("wf", sub(t2, 16, 32), r2, ALU.is_ge, cr, ALU.mult)
-        idx = ts(sub(new("wf", 48), 32, 48), tt("wf", sub(t2, 16, 32), tq, ALU.add), rcol, ALU.subtract, 384.0, ALU.min)
+        act(ap("nm", Gt, Gt + 256), ind(ap("nm", NB, top), sub(RU, 0, 16)), AF.Copy)
         t1 = tt("wf", cum, blk(0, 4, 2), ALU.subtract)
-        gp = ts("wf", blk(1, 4, 2), tt("wf", r2, cn, ALU.add), ALU.min, rcol, ALU.subtract)
-        cum = ts("wf", tt("wf", t1, gp, ALU.add), 4096.0, ALU.min)
+        gp = ts("wf", blk(1, 4, 2), mn, ALU.subtract, cn, ALU.min)
+        cum = ts(sub(new("wf", 80), 0, 32), tt("wf", t1, gp, ALU.add), mn, ALU.add, 4096.0, ALU.min)
         l = tt("wf", sub(cum, 0, 16), sub(cum, 16, 32), ALU.subtract)
         k = tt("wf", k, l, ALU.min)
-        gw = ap("nm", Gt, Gt + 400 + 256 * t)
         if t == 2:
-            return idx, cum, l, k, gw
-        bk = tt("wf", begw, k, ALU.add)
+            return idx, cum, l, k
+        bk = tt("wf", begO, k, ALU.add)
         m = tt("wf", l, k, ALU.subtract)
         if t == 0:
-            ix = tt("wf", ts("wf", m, 1.0, ALU.is_lt, 384.0, ALU.mult), idx, ALU.max)
-            EU = cp("wu", ix)
-            EN, en = EU, ap("nm", E1, E1 + 256)
+            gw = ap("nm", G0, G0 + 400)
+            EN = cp("wu", tt("wf", ts("wf", m, 1.0, ALU.is_lt, 384.0, ALU.mult), idx, ALU.max))
+            en = ap("nm", E1, E1 + 256)
+            st["mq"] = lin_("wf", m, 1.0, -1.0)
         else:
+            gw = ap("nm", E1, G1 + 400)
             mm_ = tt("wf", st["m"], m, ALU.min)
+            nf = tt("wf", m, mm_, ALU.subtract)
             ex2 = new("wf", 32)
-            ix = tt(sub(ex2, 16, 32), lin_("wf", tt("wf", m, mm_, ALU.is_le), 384.0, 0.0), idx, ALU.max)
-            tt(sub(ex2, 0, 16), tt("wf", C400, mm_, ALU.mult), ix, ALU.max)
-            EU = cp("wu", ex2)
-            EN, en = sub(EU, 16, 32), ap("nm", E2 + 256, E2 + 512)
-            act(ap("nm", E2, E2 + 256), ind(gw, sub(EU, 0, 16)), AF.Copy)
+            ix = tt(sub(ex2, 16, 32), ts("wf", nf, -384.0, ALU.mult, 384.0, ALU.add), idx, ALU.max)
+            tt(sub(ex2, 0, 16), tt("wf", CM, lin_("wf", mm_, -16384.0, 16384.0), ALU.add), ix, ALU.min)
+            EU = ts("wu", ex2, 256.0, ALU.add)
+            EN, en = sub(EU, 16, 32), ap("nm", E2B, E2B + 256)
+            act(ap("nm", E2A, E2A + 256), ind(gw, sub(EU, 0, 16)), AF.Copy)
             st["OZ"] = ts("wu", tt("wf", st["en"], mm_, ALU.mult), 4104.0, ALU.add)
-            st["mm"] = mm_
+            st["mq"] = nf
+            unwrap(BKR, bk, MX, sub(pa, 0, 256))
+            f = new("wf", 32)
+            act(sub(f, 0, 16), m, AF.Relu, 16384.0, -16384.0)
+            act(sub(f, 16, 32), m, AF.Relu, 32768.0, -16384.0)
+            st["old"] = tt("wf", f, CE, ALU.add)
+            st["ck"] = tt("wf", C16K, k, ALU.subtract)
         act(en, ind(gw, EN), AF.Copy)
-        scan(WD, AH, en, 0.0, ALU.mult, ALU.max)
-        ew = sub(WD, 15, 256, 16)
+        ew = hold(WD, en)
         st["EW"] = ts("wu", ew, inv, ALU.mult, -1.0, ALU.add)
         if t == 0:
             st["en"] = ts("wf", ew, inv, ALU.mult, -4105.0, ALU.add)
-        zz = tt("wf", ts("wf", k, 0.0, ALU.is_equal), DUM, ALU.mult)
-        st["VU"] = cp("wu", tt("wf", tt("wf", begm, k, ALU.add), zz, ALU.max))
-        st.update({"cum": cum, "k": k, "l": l, "m": m, "m1": lin_("wf", m, 1.0, -1.0), "m8": tt("wf", m, C16K, ALU.add),
-                   "bk": unwrap(BKR[t], bk, MY, sub(pb, 0, 256))})
+        zz = tt("wf", act("wf", k, AF.Relu, 1.0, -1.0), DUMO, ALU.mult)
+        st["VU"] = ts("wu", tt("wf", bk, zz, ALU.max), -16897.0, ALU.add)
+        st.update({"cum": cum, "k": k, "l": l, "m": m, "bk": bk})
         return None
 
-    def final(idx, cum, l, k, gw):
+    def final(idx, cum, l, k):
         PC, PEN, PS = ap("xb", 0, 1024), ap("xb", 1024, 2048), ap("xb", 2048, 3072)
+        gw = ap("nm", E2A, G2 + 400)
         ex = ap("wf", idx[2] - 32, idx[3])
-        for s, cc in ((0, C400), (1, C656)):
-            tt(sub(ex, 16 * s, 16 * s + 16), tt("wf", ts("wf", st["m"], float(s + 1), ALU.is_ge), cc, ALU.mult), idx, ALU.max)
-        EU = cp("wu", ex)
+        for s in range(2):
+            tt(sub(ex, 16 * s, 16 * s + 16), sub(st["old"], 16 * s, 16 * s + 16), idx, ALU.min)
+        EU = ts("wu", ex, float(G2 - E2A), ALU.add)
         cw, dw = sub(cum, 0, 16), sub(cum, 16, 32)
-        kw = tt("wf", dw, k, ALU.add)
-        unwrap(NC, tt("wf", tt("wf", C16K, st["k"], ALU.subtract), dw, ALU.subtract), MX, sub(pa, 0, 256))
-        bkr = st["bk"]
-        q32 = ts("ri", tt("wf", cum, L255, ALU.add), 0.0625, ALU.mult, -0.46875, ALU.add)
+        kw = tt(sub(cum, 32, 48), dw, k, ALU.add)
+        code = unwrap(sub(NC, 1, 257), tt("wf", st["ck"], dw, ALU.subtract), MX, sub(pa, 0, 256))
+        q32 = ts("ri", cum, 0.0625, ALU.mult, -0.46875, ALU.add)
         pe_, pq_ = sub(q32, 0, 16), sub(q32, 16, 32)
         OU = cp("wu", tt("wf", tt("wf", tt("wf", pq_, pe_, ALU.is_equal), C272, ALU.mult), pq_, ALU.max))
-        s4 = new("ri", 64)
-        cp(sub(s4, 0, 16), dw)
-        cp(sub(s4, 16, 32), kw)
         for s in (1, 2):
-            tt(sub(s4, 16 + 16 * s, 32 + 16 * s), lin_("wf", kw, 1.0, float(s)), cw, ALU.min)
-        r4 = ts("ri", s4, 15, ALU.bitwise_and)
+            tt(sub(cum, 32 + 16 * s, 48 + 16 * s), lin_("wf", kw, 1.0, float(s)), cw, ALU.min)
+        r4 = ts("ri", cp("ri", sub(cum, 16, 80)), 15, ALU.bitwise_and)
         PU = cp("wu", r4)
         BU = ts("wu", tt("wf", beg16, sub(r4, 0, 16), ALU.subtract), 4111.0, ALU.min)
-        fill(256, OU, NC)
-        ci, y = decode(256, JV, bkr)
-        GU = cp("wu", tt("wf", ts("wf", y, 0.0, ALU.max, 3.0, ALU.min), ts("wf", ci, 4.0, ALU.mult), ALU.add))
-        AU = ts("wu", tt("wf", wrap(WB, sub(BKG, 0, 256)), y, ALU.add), 16.0, ALU.add, 4111.0, ALU.min)
+        cp(ind(ZF, OU), code)
+        scan(FIL, sub(ZF, 0, 256), sub(ZF, 0, 256), 0.0, ALU.max, ALU.max)
+        nw = wrap(WA, FIL)
+        act(sub(BKG, 0, 256), ind(BKR, ts("wu", nw, 1.0 / 16384, ALU.mult)), AF.Copy)
+        a = tt("ri", nw, JV, ALU.add)
+        y5 = ts("ri", a, 16383, ALU.bitwise_and)
+        c4 = ts("ri", a, 12, ALU.arith_shift_right, 1020, ALU.bitwise_and)
+        GU = ts("wu", tt("wf", ts("wf", y5, 5632.0, ALU.max, 5635.0, ALU.min), c4, ALU.add), -5632.0, ALU.add)
+        AU = ts("wu", tt("wf", wrap(WB, sub(BKG, 0, 256)), y5, ALU.add), 16.0 - 5632.0 - 16896.0, ALU.add, 4111.0, ALU.min)
         act(sub(HI, 0, 256), ind(PCR, GU), AF.Copy)
-        lin_(EG, ind(PCR, GU), 1.0, 4097.0)
-        hi = tt(MX, sub(HI, 1, 257), EG, ALU.subtract)
+        eg = lin_(sub(pd, 0, 256), sub(HI, 0, 256), 1.0, 4097.0)
+        hi = tt(MX, sub(HI, 1, 257), eg, ALU.subtract)
         for s in range(4):
             act(sub(PEN, s, 1024, 4), ind(PT, sub(PU, 16 * s, 16 * s + 16)), AF.Copy)
         lin_(sub(PC, 0, 1024, 4), ind(WIN, BU), 1.0, -1.0)
@@ -604,7 +602,7 @@ def order(ops):
                     hit = l2 < hi and lo < h2 and (kind == "w" or k2 == "w") and not (sp == s2 and (lo - l2) % sp)
                     if ps and ops[j]["eng"] == "P" and o["eng"] == "P":
                         soft.add(j)
-                    elif hit and kind == "w" and ops[j]["eng"] == o["eng"] and o["sem"] is None and ops[j]["sem"] is None:
+                    elif hit and kind == "w" and k2 == "r" and ops[j]["eng"] == o["eng"] and o["sem"] is None and ops[j]["sem"] is None:
                         soft.add(j)
                     elif hit or (ps and ops[j]["eng"] != o["eng"]):
                         hard.add(j)

@@ -1,3 +1,4 @@
+import math
 import numpy as np
 from concourse.bass import DstId, RemoteDMATransfer
 from concourse.mybir import AluOpType as ALU, ActivationFunctionType as AF
@@ -9,13 +10,13 @@ E2B = E2A + 8192
 G2 = E2B + 256
 NMW = G2 + 400
 GB = [G0, G1, G2]
-RW, BW, IW, UW, WW = 7680, 4608, 640, 1024, 4608
+RW, BW, IW, UW, WW = 6400, 4736, 640, 1024, 3840
 SCRATCH = {
     "au0": ("sbuf", [128, 4112], BF), "au1": ("sbuf", [128, 4112], BF), "au2": ("sbuf", [128, 4112], BF),
     "xb": ("sbuf", [128, 4352], F32),
     "da": ("sbuf", [128, 4352], F32), "db": ("sbuf", [128, 4352], F32),
     "fl": ("sbuf", [128, 4352], BF), "sg": ("sbuf", [128, 4096], BF),
-    "nm": ("sbuf", [128, NMW], F32), "zw": ("sbuf", [128, 768 + 9024], BF),
+    "nm": ("sbuf", [128, NMW], F32), "zw": ("sbuf", [128, 384 + 4864], BF), "zf": ("sbuf", [128, 256 + 4864], F32),
     "rf": ("sbuf", [128, RW], F32), "rb": ("sbuf", [128, BW], BF), "ri": ("sbuf", [128, IW], I32),
     "wu": ("sbuf", [128, UW], U16), "wf": ("sbuf", [128, WW], F32),
     "spi": ("sbuf", [128, 256], I32), "gui": ("sbuf", [128, 256], I32), "lni": ("sbuf", [128, 256], I32),
@@ -25,13 +26,16 @@ SCRATCH = {
 for _k in range(8):
     SCRATCH["p%d" % _k] = ("psum", [128, 32, 16] if _k == 2 else [128, 512], F32)
 SEMAPHORES = (["cV", "cS", "cP", "cG"] + ["d%d" % k for k in range(16)] + ["lo%d" % k for k in range(12)]
-              + ["a1h0", "a1h1", "a2h0", "a2h1"] + ["rc%d" % t for t in range(3)] + ["rn%d" % t for t in range(3)])
+              + ["a1h0", "a1h1", "a1h2", "a1h3", "a2h0"] + ["rc%d" % t for t in range(3)] + ["rn%d" % t for t in range(3)])
 
 CUTS = [[0, 512, 1280, 2048, 2816, 3584, 3840, 4096], list(range(0, 4097, 512)), list(range(0, 4097, 512))]
 CY = 0.00092
 HOP = 0.13
 BIG = float(1 << 23)
 HOLD = float(1 << 24)
+RND = float(3 << 22)
+C0 = [0.0, 23.5 / 32, 1 + 23.5 / 32]
+VIA = [0, 2]
 VG = [4, 4, 2]
 
 
@@ -75,6 +79,26 @@ def in_psum(a):
     return a[0] != "ind" and SCRATCH[a[1]][0] == "psum"
 
 
+def helper(r, T, topo):
+    src, dst = T.cores[r % N], T.cores[(r - 1) % N]
+    if topo.chip(src) == topo.chip(dst):
+        return None
+    return [c for c in topo.cores_of(src) if c not in T.cores and topo.die(c) != topo.die(src) and topo.may_write(c, dst)][0]
+
+
+def hand_on(g, core, T, topo):
+    for r in range(N):
+        if helper(r, T, topo) == core:
+            dst = T.cores[(r - 1) % N]
+            rid, pid, _se = topo.addr(dst)
+            into = [e for e in topo.engines(T.cores[r], core) if e not in topo.engines(T.cores[r], dst)]
+            for h in VIA:
+                g.wait_ge(T.sem["a1h%d" % h], len(into))
+                g.remote_dma(T.au1[:, 1024 * h:1024 * h + 1024], T.au0[:, 1024 * h:1024 * h + 1024], T.sem["a1h%d" % h], T.sem["lo0"],
+                             pid, rid, topo.mask(core, dst))
+            g.wait_ge(T.sem["lo0"], len(VIA) * len(topo.engines(core, dst)))
+
+
 def build(rank, core, T, topo):
     ops = []
     free = {"rf": 0, "rb": 0, "ri": 0, "wu": 0, "wf": 0, "nm": ST}
@@ -107,7 +131,8 @@ def build(rank, core, T, topo):
             else:
                 wr += regions(a)
         ops.append({"eng": eng, "emit": emit, "rd": rd, "wr": wr, "cost": cost, "lat": cost if lat is None else lat,
-                    "sem": sem, "cnt": cnt, "after": list(after)})
+                    "sem": sem, "cnt": cnt, "after": list(after),
+                    "kind": "s" if any(a[0] == "ind" for a in outs) else "g" if any(isinstance(a, tuple) and a[0] == "ind" for a in ins) else ""})
         return len(ops) - 1
 
     def vcost(out, ins, two=False):
@@ -167,11 +192,11 @@ def build(rank, core, T, topo):
             add("P", lambda g, l=l, r=r, k=k: g.tensor.matmul(R(out), R(l), R(r), k == 0, k == len(terms) - 1), [out], [l, r], c, c + 0.06)
         return out
 
-    def iota(out, pat, base, cm):
+    def iota(out, pat, base, cm, after=()):
         if SCRATCH[out[1]][2] == I32:
             add("G", lambda g: g.iota(R(out), pat, base, cm), [out], [], 0.13 + 2 * count(out) * CY)
         else:
-            add("G", lambda g: g.iota(R(out), pat, base, cm, allow_small_or_imprecise_dtypes=True), [out], [], 0.13 + 2 * count(out) * CY)
+            add("G", lambda g: g.iota(R(out), pat, base, cm, allow_small_or_imprecise_dtypes=True), [out], [], 0.13 + 2 * count(out) * CY, after=after)
         return out
 
     nd = [0]
@@ -188,7 +213,7 @@ def build(rank, core, T, topo):
 
     nl = [0]
 
-    def send(items, lat):
+    def send(items, lat, gate=(), after=()):
         s = "lo%d" % nl[0]
         nl[0] += 1
 
@@ -204,7 +229,7 @@ def build(rank, core, T, topo):
                     tr.append(RemoteDMATransfer(dst_ids=[DstId(rid=rid, pnc=pid)], dma_engine_mask=sum(1 << e for e in es),
                                                 remote_sem=T.sem[rs], src=R(src), dst=R(dst)))
                 g.remote_dma_fused(tr, local_sem=T.sem[s])
-        return add("G", emit, [], [it[0] for it in items], 0.6, lat, s, sum(len(it[3]) for it in items))
+        return add("G", emit, [], [it[0] for it in items] + list(gate), 0.6, lat, s, sum(len(it[3]) for it in items), after)
 
     def recv(dst, sem, cnt, after, lat):
         return add(None, None, [dst], [], 0.0, lat, sem, cnt, after)
@@ -218,54 +243,37 @@ def build(rank, core, T, topo):
     def relayed(r):
         return same(r, r + 1) and not same(r, r + 2)
 
-    def plan(r):
-        e1 = topo.engines(C[r % N], C[(r - 1) % N])
-        if relayed(r - 2):
-            return e1, None
-        e2 = topo.engines(C[r % N], C[(r - 2) % N])
-        if len(e1) > len(e2):
-            return [e for e in e1 if e not in e2], e2
-        if len(e2) > len(e1):
-            return e1, [e for e in e2 if e not in e1]
-        return e1[:len(e1) // 2], e2[len(e2) // 2:]
-
     def small(r):
         return topo.engines(C[r % N], C[(r + 1) % N])[:8]
 
     au = ["au0", "au1", "au2"]
     lni, spi, gui = ap("lni", 0, 256, 1, (0, 8)), ap("spi", 0, 256), ap("gui", 0, 256)
     dma([(lambda: R(lni), lambda: T.lens[:])], [lni], [], 2.2, "S")
-    for h in range(2):
-        a = ap("au0", 2048 * h, 2048 * h + 2048)
-        dma([(lambda a=a: R(a), lambda h=h: T.aud[:, 2048 * h:2048 * h + 2048])], [a], [], 4.0 + 1.5 * h)
+    for h in range(4):
+        a = ap("au0", 1024 * h, 1024 * h + 1024)
+        dma([(lambda a=a: R(a), lambda h=h: T.aud[:, 1024 * h:1024 * h + 1024])], [a], [], OPT["aud"][0] + OPT["aud"][1] * h)
     dma([(lambda: R(spi), lambda: T.spots[:])], [spi], [], 2.6, "S")
-    dma([(lambda: R(gui), lambda: T.gua[:])], [gui], [], 3.0, "S")
-    e1, e2 = plan(rank)
-    for h in range(2):
-        lo, hi = 2048 * h, 2048 * h + 2048
-        items = [(ap("au0", lo, hi), ap("au1", lo, hi), prv, e1, "a1h%d" % h)]
-        if e2 is not None:
-            items.append((ap("au0", lo, hi), ap("au2", lo, hi), C[(rank - 2) % N], e2, "a2h%d" % h))
-        s = send(items, 6.0)
-        recv(ap("au1", lo, hi), "a1h%d" % h, len(plan(rank + 1)[0]), [s], 2.0 + 3 * h)
-        if not relayed(rank):
-            recv(ap("au2", lo, hi), "a2h%d" % h, len(plan(rank + 2)[1]), [s], 6.0 + 3 * h)
+    dma([(lambda: R(gui), lambda: T.gua[:])], [gui], [], *OPT["gua"])
+    mine, theirs = helper(rank, T, topo), helper(rank + 1, T, topo)
+    s = None
+    for h in range(4):
+        a0, a1 = ap("au0", 1024 * h, 1024 * h + 1024), ap("au1", 1024 * h, 1024 * h + 1024)
+        if mine is not None and h in VIA:
+            item = (a0, a0, mine, [e for e in topo.engines(core, mine) if e not in topo.engines(core, prv)], "a1h%d" % h)
         else:
-            recv(ap("au2", lo, hi), "a2h%d" % h, len(topo.engines(nxt, core)), [s], 9.0 + 3 * h)
-    if relayed(rank - 1):
-        for h in range(2):
-            lo, hi = 2048 * h, 2048 * h + 2048
-            send([(ap("au1", lo, hi), ap("au2", lo, hi), prv, topo.engines(core, prv), "a2h%d" % h)], 4.0)
+            item = (a0, a1, prv, topo.engines(core, prv), "a1h%d" % h)
+        s = send([item], OPT["l0"], after=[] if s is None else [s])
+        recv(a1, "a1h%d" % h, len(topo.engines(theirs if theirs is not None and h in VIA else nxt, core)), [s], OPT["l1"] + OPT["aud"][1] * (3 - h))
 
     pi = iota(new("ri", 1), [[0, 1]], 0, 1)
     JB = iota(new("nm", 128), [[1, 8], [0, 16]], 0, 0)
     RB = iota(new("rb", 384), [[0, 24], [2048, 16]], 0, 0)
-    J = iota(new("nm", 368), [[1, 368]], 0, 0)
-    PCR = iota(new("nm", 1024), [[8192, 1024]], 8192, 0)
-    CROW = iota(new("rb", 256), [[1, 256]], 1, 0)
-    iota(ap("zw", 256, 1152), [[0, 896]], 0, 0)
-    iota(ap("nm", XA + 4096, XA + 4352), [[0, 256]], 0, 0)
-    iota(ap("xb", 4096, 4352), [[0, 256]], 0, 0)
+    J = iota(new("nm", 128), [[1, 128]], 0, 0)
+    s1 = s
+    JH, PCR, CROW = new("nm", 240), new("nm", 1024), new("rb", 256)
+    iota(ap("nm", XA + 4096, XA + 4352), [[0, 256]], 0, 0, [s])
+    iota(ap("xb", 4096, 4352), [[0, 256]], 0, 0, [s])
+    iota(ap("zf", 256, 640), [[0, 384]], 0, 0, [s])
     J16, J128 = sub(J, 0, 16), sub(J, 0, 128)
     FL = ap("fl", 0, 4352)
     ZERO = ms(ap("zw", 0, 256), 0.0)
@@ -280,7 +288,13 @@ def build(rank, core, T, topo):
     JJ = lin_("wf", sub(J, 0, 24), 16.0, icol)
     C16 = sub(JJ, 0, 16)
     DUM = lin_("wf", C16, 1.0, 4096.0)
-    ms(FL, 1.0)
+    fs, fg = OPT["fl"]
+    ms(sub(FL, 0, fs), 1.0)
+    act(sub(FL, fs, 2 * fs), sub(FL, 0, fs), AF.Copy)
+    iota(sub(FL, 2 * fs, 2 * fs + fg), [[0, fg]], 1, 0)
+    fm = (2 * fs + fg + 4352) // 2
+    ms(sub(FL, 2 * fs + fg, fm), 1.0)
+    ms(sub(FL, fm, 4352), 1.0)
     IF = ts("nm", J128, pcol, ALU.is_equal)
     BO = ts("nm", JB, gcol, ALU.is_equal)
     BOS = lin_("nm", BO, 1.0 / BIG, 0.0)
@@ -288,8 +302,8 @@ def build(rank, core, T, topo):
     BON = lin_("rb", BO, -0.25, 0.0)
     NBO = lin_("nm", BO, -1.0, 0.0)
     UI, US = new("nm", 128), new("nm", 128)
-    add("G", lambda g: g.affine_select(R(UI), R(NBO), [[-1, 128]], ALU.is_ge, 0.0, 0, 1), [UI], [NBO], 0.44)
-    add("G", lambda g: g.affine_select(R(US), R(NBO), [[-1, 128]], ALU.is_gt, 0.0, 0, 1), [US], [NBO], 0.44)
+    add("G", lambda g: g.affine_select(R(UI), R(NBO), [[-1, 128]], ALU.is_ge, 0.0, 0, 1), [UI], [NBO], 0.44, after=[s])
+    add("G", lambda g: g.affine_select(R(US), R(NBO), [[-1, 128]], ALU.is_gt, 0.0, 0, 1), [US], [NBO], 0.44, after=[s])
     i15 = act("wf", icol, AF.Relu, -14.0)
     S15 = lin_("nm", BO, i15, 0.0)
     Z = iota(new("rb", 144), [[0, 144]], 0, 0)
@@ -298,7 +312,7 @@ def build(rank, core, T, topo):
     ni8k = lin_("wf", icol, -8192.0, 0.0)
     i256 = lin_("wf", icol, -256.0, -127.5)
     i256p = lin_("wf", icol, -256.0, -255.5)
-    POS8 = lin_("nm", sub(J, 0, 256), -131072.0, ni8k)
+    POS8 = new("nm", 256)
     PT = lin_("wf", ts("wf", J16, icol, ALU.is_le), -2 * BIG - 8192.0, 8192.0)
     JO = cp("wu", J16)
     JV = lin_("wf", C16, 16.0, 16.0)
@@ -306,7 +320,7 @@ def build(rank, core, T, topo):
     lin_(sub(CE, 0, 16), C16, 1.0, float(E2A - G2))
     CM = lin_(sub(CE, 16, 32), C16, 1.0, float(E2B - G2))
     C272 = tt("wf", lin_("wf", C16, 1.0, 272.0), act("wf", C16, AF.Sign, 255.0, -1.0), ALU.mult)
-    CD = lin_("wf", C16, 1.0, 4400.0)
+    DUM2 = lin_("wf", C16, 1.0, 4352.0)
     C16K = lin_("wf", C16, 16384.0, 5632.0)
     RST = act("wf", sub(J, 0, 32), AF.Sign, -16.0)
     RST = act("wf", RST, AF.Square)
@@ -323,14 +337,10 @@ def build(rank, core, T, topo):
         lin_(ap("nm", GB[k] + 384, GB[k] + 400), J16, 0.0, 4097.0)
     END, WX, CODE, NC = new("rf", 257), new("rf", 257), new("rf", 257), new("rf", 257)
     T1, T2 = new("rb", 272), new("rb", 272)
-    HI = new("rf", 257)
-    for b in (END, WX):
-        lin_(sub(b, 0, 1), icol, 0.0, 0.0)
-    lin_(sub(CODE, 0, 1), icol, 0.0, BIG)
-    lin_(sub(NC, 0, 1), icol, 0.0, 8192001.0)
-    lin_(sub(HI, 256, 257), icol, 0.0, 0.0)
+    lin_(sub(END, 0, 544, 272), sub(J, 0, 2), 0.0, 0.0)
+    lin_(sub(CODE, 0, 544, 272), sub(J, 0, 2), 0.0, 8192001.0)
     lin_(sub(T1, 0, 16), J16, 0.0, 0.0)
-    ZP = lin_("wf", J16, 0.0, 0.0)
+    ZP = sub(T2B, 16, 32)
     pc, pd, pv, pw, pe, pq, pa, pb = [ap("p%d" % k, 0, 512) for k in range(8)]
 
     def blk(a, b, step=1):
@@ -389,8 +399,23 @@ def build(rank, core, T, topo):
     zp8 = sub(ZP, 0, 16, 1, (0, 8))
     pairs = [(lambda g_=g_: T.lin[g_, 16:4112], lambda g_=g_: T.st3[:, g_, :, :]) for g_ in range(8)]
     pairs += [(lambda: T.lin[:, 0:16], lambda: R(zp8)), (lambda: T.lin[:, 4112:4128], lambda: R(zp8))]
-    dma(pairs, [lin], [ap("st3", 0, 256), zp8], 4.0)
-    dma([(lambda i=i: T.nm[i:128:16, NB:NB + 4112], lambda: T.lin[:, 16:4128]) for i in range(16)], [ap("nm", NB, NB + 4112)], [lin], 13.0)
+    s = dma(pairs, [lin], [ap("st3", 0, 256), zp8], 4.0)
+    dma([(lambda i=i: T.nm[i:128:16, NB:NB + 4112], lambda: T.lin[:, 16:4128]) for i in range(16)], [ap("nm", NB, NB + 4112)], [lin], OPT["nm"])
+    far2, got = C[(rank - 2) % N], ap("au1", 0, 4096)
+    lo = 0 if relayed(rank - 1) else 2048
+    out = [send([(ap("au1", lo, 4096), ap("au2", lo, 4096), prv, topo.engines(core, prv), "a2h0")], 1.0, [lin, got])]
+    if not relayed(rank - 2):
+        out.append(send([(ap("au0", 0, 2048), ap("au2", 0, 2048), far2, topo.engines(core, far2), "a2h0")], 1.0, [lin, got]))
+        ops[out[1]]["more"] = True
+    recv(ap("au2", 0, 4096), "a2h0", len(topo.engines(nxt, core)) + (0 if relayed(rank) else len(topo.engines(C[(rank + 2) % N], core))),
+         out, OPT["l2"])
+    out = [s1] + out
+    iota(JH, [[1, 240]], 128, 0, out[:1])
+    lin_(POS8, sub(J, 0, 256), -131072.0, ni8k)
+    iota(CROW, [[1, 256]], 1, 0, out[:1])
+    iota(ap("zw", 256, 768), [[0, 512]], 0, 0, out[:1])
+    iota(ap("zf", 0, 256), [[0, 256]], 0, 0, out)
+    iota(PCR, [[8192, 1024]], 8192, 0, out)
     WIN = ap("db", 0, 4112)
     assert free["nm"] == E2B
 
@@ -398,8 +423,7 @@ def build(rank, core, T, topo):
     FIL, BKG, MX, NA, NB2, BKR = [new("rf", n) for n in (256, 384, 256, 256, 256, 256)]
     FIB, WAB = new("rb", 384), new("rb", 384)
     SND = new("rf", 384)
-    ZF = new("rf", 528)
-    iota(sub(ZF, 0, 256), [[0, 256]], 0, 0)
+    ZF = ap("zf", 0, 528)
     st = {"cum": cum0, "k": nw0, "l": nw0}
 
     def heavy(t):
@@ -425,7 +449,7 @@ def build(rank, core, T, topo):
         tt(sub(T1, 16, 272), ind(WX, UO), EQ, ALU.mult)
         lin_(sub(T2, 15, 272), LT, sub(WX, 256, 257), 0.0)
         mm(sub(pd, 0, 256), [(BOP, sub(RB, 0, 256)), (BOP, sub(T2, 16, 272)), (BON, sub(T2, 15, 271)), (BOP, sub(T1, 16, 272)), (BON, sub(T1, 15, 271))])
-        return tt("wf", wrap(WC, sub(pd, 0, 256)), tt("wf", stat, st["l"], ALU.add), ALU.add)
+        return tt("wf", wrap(WC, sub(pd, 0, 256)), tt("wf", lin_("wf", stat, 1.0, -C0[t]) if t else stat, st["l"], ALU.add), ALU.add)
 
     def light(t, d):
         Gt = GB[t]
@@ -444,16 +468,21 @@ def build(rank, core, T, topo):
             else:
                 na = lin_(NA, dk, -1.0, 0.0)
             tt(SGN, ind(tab, st["EW"]), na, ALU.is_ge)
-            v = mm(sub(pq, 0, 16), terms + pick(SGN))
-            c0 = 23.5 / 32 + (t - 1)
-            d = ts("ri", v, -c0, ALU.add)
-            ts(x1, v, c0 - 0.5, ALU.is_lt)
-            e = ts("wf", v, c0 + 0.5, ALU.is_lt)
+            v = mm(sub(pq, 0, 16), pick(SGN) + terms[::-1] if OPT["mxl"][t] else terms + pick(SGN))
+        e8 = sub(T2B, 0, 16)
+        if OPT["xs"][t]:
+            m0 = RND if t else 0.0
+            if t:
+                d = lin_("wf", v, 1.0, RND)
+            act(x0, d, AF.Relu, -m0)
+            act(x1, d, AF.Relu, m0, -1.0)
+            act(e8, d, AF.Relu, 8192.0 * (m0 + 1), -8192.0)
         else:
-            ts(x1, d, 0.0, ALU.is_lt)
-            e = ts("wf", d, 0.5, ALU.is_lt)
-        ts(x0, d, 0.0, ALU.max)
-        tt(sub(T2B, 0, 16), e, CD, ALU.mult)
+            if t:
+                d = cp("ri", v)
+            ts(x1, v if t else d, -0.5, ALU.is_lt)
+            ts(e8, v if t else d, 0.5, ALU.is_lt, 8192.0, ALU.mult)
+            ts(x0, d, 0.0, ALU.max)
         sc = scan("wf", RST, x, 0.0, ALU.mult, ALU.add)
         mm(sub(pw, 0, 2), [(BO, sub(sc, 15, 32, 16))])
         ex = mm(sub(pb, 0, 32), [(UI, x), (IF, T2B), (BO, sc)])
@@ -461,31 +490,35 @@ def build(rank, core, T, topo):
         mm(blk(2, 4), [(UI, x), (BO, sc)])
         mn = ts("wf", sub(pw, 0, 1), sub(pw, 1, 2), ALU.min, -256.0, ALU.add)
         cs, cn = ap("cs", 4 * t, 4 * t + 1), ap("cn", 4 * t, 4 * t + 1)
-        OU = ts("wu", sub(ex, 0, 16), mn, ALU.subtract)
+        OU = ts("wu", tt("wf", sub(ex, 0, 16), DUM2, ALU.min), mn, ALU.subtract)
         ts(cs, sub(pw, 0, 1), mn, ALU.subtract, 384.0, ALU.min)
         s = send([(cs, cn, nxt, small(rank), "rc%d" % t)], 1.0)
         recv(cn, "rc%d" % t, len(small(rank - 1)), [s], 1.5)
         jj = lin_("wf", JJ, 1.0, mn)
+        idx = ts(sub(new("wf", 48), 32, 48), sub(ex, 16, 32), mn, ALU.subtract, 384.0, ALU.min)
+        top = [4112, E1 + 256, E2B + 256][t]
         if t == 0:
-            pay = tt("wf", tt("wf", endw, x0, ALU.subtract), sub(ex, 0, 16), ALU.subtract)
+            tt(MX, ind(tt("wf", nw0, x0, ALU.subtract), JO), sub(AM, 0, 256), ALU.mult)
+            kept = scan(sub(NC, 1, 257), mm(sub(pa, 0, 256), [(BOS, MX)]), ZERO, 0.0, ALU.add, ALU.add)
+            cp(ind(ap("zf", 256, 256 + 4864), OU), kept)
+            scan(BKG, ap("zf", 256, 640), ap("zf", 256, 640), 0.0, ALU.max, ALU.max)
+            RU = ts("wu", tt("wf", wrap(WA, BKG), jj, ALU.add), top - 1.0, ALU.min)
         else:
             rm = tt("wf", x0, st["m"], ALU.subtract)
             off = tt("wf", tt("wf", st["bk"], rm, ALU.subtract), ts("wf", rm, 512.0, ALU.min, 8192.0, ALU.mult), ALU.add)
-            pay = tt("wf", ts("wf", sub(ex, 0, 16), 8191.0, ALU.mult), off, ALU.add)
-        idx = ts(sub(new("wf", 48), 32, 48), sub(ex, 16, 32), mn, ALU.subtract, 384.0, ALU.min)
-        unwrap(sub(NC, 1, 257), pay, MX, sub(pa, 0, 256))
-        zo = 768 - 384 * t
-        cp(ind(ap("zw", zo, 768 + 9024), OU), CROW)
-        scan(FIB, ap("zw", zo, zo + 384), ap("zw", zo, zo + 384), 0.0, ALU.max, ALU.max)
-        c1 = wrap(WAB, FIB)
-        act(BKG, ind(NC, cp("wu", c1)), AF.Copy)
-        top = [4112, E1 + 256, E2B + 256][t]
-        if t == 0:
-            RU = ts("wu", tt("wf", wrap(WA, BKG), jj, ALU.add), top - 1.0, ALU.min)
-        else:
+            unwrap(sub(NC, 1, 257), tt("wf", ts("wf", sub(ex, 0, 16), 8191.0, ALU.mult), off, ALU.add), MX, sub(pa, 0, 256))
+            zo = 768 - 384 * t
+            cp(ind(ap("zw", zo, 384 + 4864), OU), CROW)
+            scan(FIB, ap("zw", zo, zo + 384), ap("zw", zo, zo + 384), 0.0, ALU.max, ALU.max)
+            c1 = wrap(WAB, FIB)
+            act(BKG, ind(NC, cp("wu", c1)), AF.Copy)
             cj = tt("wf", c1, lin_("wf", jj, 8192.0, 16384.0 + 511.0 + [0, E1, E2A][t]), ALU.add)
-            p = ts("ri", hold(WA, BKG), inv, ALU.mult)
-            far = tt("wf", tt("wf", cj, p, ALU.subtract), jj, ALU.max)
+            if t == 1:
+                pf = wrap(WA, BKG)
+                p = cp("ri", pf)
+            else:
+                pf = p = ts("ri", hold(WA, BKG), inv, ALU.mult)
+            far = tt("wf", tt("wf", cj, pf, ALU.subtract), jj, ALU.max)
             RU = ts("wu", tt("wf", far, ts("ri", p, 8191, ALU.bitwise_and), ALU.add), -512.0, ALU.add, top - 1.0, ALU.min)
         snd, arr = sub(SND, 128 * t, 128 * t + 128), ap("nm", Gt + 256, Gt + 384)
         act(snd, ind(ap("nm", NB, top), sub(RU, 16, 24)), AF.Copy)
@@ -505,7 +538,7 @@ def build(rank, core, T, topo):
             gw = ap("nm", G0, G0 + 400)
             EN = cp("wu", tt("wf", ts("wf", m, 1.0, ALU.is_lt, 384.0, ALU.mult), idx, ALU.max))
             en = ap("nm", E1, E1 + 256)
-            st["mq"] = lin_("wf", m, 1.0, -1.0)
+            st["mq"] = lin_("wf", m, 1.0, -1.0 - C0[1])
         else:
             gw = ap("nm", E1, G1 + 400)
             mm_ = tt("wf", st["m"], m, ALU.min)
@@ -517,7 +550,7 @@ def build(rank, core, T, topo):
             EN, en = sub(EU, 16, 32), ap("nm", E2B, E2B + 256)
             act(ap("nm", E2A, E2A + 256), ind(gw, sub(EU, 0, 16)), AF.Copy)
             st["OZ"] = ts("wu", tt("wf", st["en"], mm_, ALU.mult), 4104.0, ALU.add)
-            st["mq"] = nf
+            st["mq"] = lin_("wf", nf, 1.0, -C0[2])
             unwrap(BKR, bk, MX, sub(pa, 0, 256))
             f = new("wf", 32)
             act(sub(f, 0, 16), m, AF.Relu, 16384.0, -16384.0)
@@ -561,25 +594,33 @@ def build(rank, core, T, topo):
         c4 = ts("ri", a, 12, ALU.arith_shift_right, 1020, ALU.bitwise_and)
         GU = ts("wu", tt("wf", ts("wf", y5, 5632.0, ALU.max, 5635.0, ALU.min), c4, ALU.add), -5632.0, ALU.add)
         AU = ts("wu", tt("wf", wrap(WB, sub(BKG, 0, 256)), y5, ALU.add), 16.0 - 5632.0 - 16896.0, ALU.add, 4111.0, ALU.min)
-        act(sub(HI, 0, 256), ind(PCR, GU), AF.Copy)
-        eg = lin_(sub(pd, 0, 256), sub(HI, 0, 256), 1.0, 4097.0)
-        hi = tt(MX, sub(HI, 1, 257), eg, ALU.subtract)
+        HJ = lin_(MX, ind(PCR, GU), 1.0, 4097.0)
         for s in range(4):
-            act(sub(PEN, s, 1024, 4), ind(PT, sub(PU, 16 * s, 16 * s + 16)), AF.Copy)
-        lin_(sub(PC, 0, 1024, 4), ind(WIN, BU), 1.0, -1.0)
+            o, i_ = sub(PEN, s, 1024, 4), ind(PT, sub(PU, 16 * s, 16 * s + 16))
+            if s < OPT["pen"]:
+                cp(o, i_)
+            else:
+                act(o, i_, AF.Copy)
+        lin_(sub(PC, 0, 1024, 4), ind(WIN, BU), 1.0, 4096.0)
         for s in range(3):
-            lin_(sub(PC, 1 + s, 1024, 4), ind(gw, sub(EU, 16 * s, 16 * s + 16)), 1.0, -1.0)
-        scan(PS, PEN, PC, 0.0, ALU.add, ALU.max)
+            if s < OPT["pc"]:
+                ts(sub(PC, 1 + s, 1024, 4), ind(gw, sub(EU, 16 * s, 16 * s + 16)), 4096.0, ALU.add)
+            else:
+                lin_(sub(PC, 1 + s, 1024, 4), ind(gw, sub(EU, 16 * s, 16 * s + 16)), 1.0, 4096.0)
+        scan(PS, PEN, PC, 8192.0, ALU.add, ALU.max)
         o = sub(pe, 128, 256, 1, (0, 16))
         add("P", lambda g: g.tensor.transpose(R(o), R(l), R(IF)), [o], [l, IF], 0.45, 0.5)
         yn = act(sub(NB2, 0, 128, 1, (0, 16)), o, AF.Copy)
         dma([(lambda g_=g_: T.yn[g_, :], lambda g_=g_: R(sub(yn, 16 * g_, 16 * g_ + 16, 1, (0, 16)))) for g_ in range(8)], [], [yn], 2.5)
         tcol = lin_("wf", mm(sub(pw, 8, 9), [(S15, sub(cw, 15, 16))]), 8192.0, -4096.0)
         mk = lin_(sub(pc, 0, 256), act(NA, POS8, AF.Relu, tcol), 1.0, -1.0)
-        tt(sub(CODE, 1, 257), ind(WIN, AU), hi, ALU.add)
-        h3 = tt(gui, ind(PS, GU), sub(CODE, 0, 256), ALU.min)
-        v = ts(spi, h3, 4095, ALU.bitwise_and)
-        YO = tt(XS, v, mk, ALU.min)
+        tt(sub(CODE, 1, 257), ind(WIN, AU), HJ, ALU.subtract)
+        tt(FIL, ind(PS, GU), HJ, ALU.subtract)
+        YO = XS
+        for lo in range(0, 256, OPT["last"]):
+            hi = lo + OPT["last"]
+            h3 = tt(sub(gui, lo, hi), sub(FIL, lo, hi), sub(CODE, lo, hi), ALU.min)
+            tt(sub(YO, lo, hi), ts(sub(spi, lo, hi), h3, 4095, ALU.bitwise_and), sub(mk, lo, hi), ALU.min)
         dma([(lambda: T.yo[:], lambda: R(YO))], [], [YO], 2.5)
 
     light(0, heavy(0))
@@ -660,13 +701,12 @@ def order(ops):
     def span(at):
         return max(at[i] + ops[i]["lat"] for i in range(n))
 
-    shape = (n, ROUNDS, round(sum(lev), 3))
-    if shape not in KNOWN:
+    if "t" not in KNOWN:
         rng = np.random.default_rng(1)
         at = place([-v for v in lev], False)
         best = (span(at), at)
-        for it in range(ROUNDS):
-            mid, half, amp = rng.random() * best[0], 2 + 12 * rng.random(), JIT * rng.random()
+        for it in range(ROUNDS // 300):
+            mid, half, amp = rng.random() * best[0], 2 + 12 * rng.random(), 4 * rng.random()
             noise = rng.random(n) * amp
             at = place([t + (noise[i] if abs(t - mid) < half else 0.5 * amp) for i, t in enumerate(best[1])], False)
             bk = place([-(at[i] + cost[i]) for i in range(n)], True)
@@ -674,20 +714,120 @@ def order(ops):
             end = span(at)
             if end <= best[0] + 0.02:
                 best = (end, at)
-        KNOWN[shape] = best[1]
+        KNOWN["t"] = improve(ops, pre, cost, best[1], rng)
+        KNOWN["few"] = [t for t, o in zip(KNOWN["t"], ops) if "more" not in o]
+    at = KNOWN["t" if n == len(KNOWN["t"]) else "few"]
+    assert len(at) == n
     for i in range(n):
-        ops[i]["t"] = KNOWN[shape][i]
-    return sorted(range(n), key=lambda i: (KNOWN[shape][i], i))
+        ops[i]["t"] = at[i]
+    return sorted(range(n), key=lambda i: (at[i], i))
+
+
+def improve(ops, pre, cost, at, rng):
+    n = len(ops)
+    eng = [o["eng"] for o in ops]
+    anc, lean = [0] * n, []
+    for i in range(n):
+        far = 0
+        for j, _w in pre[i]:
+            far |= anc[j]
+            anc[i] |= anc[j] | (1 << j)
+        lean.append([j for j, _w in pre[i] if not (far >> j & 1) or ops[j]["sem"] is not None])
+    cases = []
+    for gather, scatter, slow, hop, dma in CASES:
+        cost = [max(o["cost"], 1e-3) if o["sem"] else slow * (0.04 + (o["cost"] - 0.04) * {"g": gather, "s": scatter, "": 1.0}[o["kind"]]) for o in ops]
+        lat = [o["lat"] * dma if o["sem"] else c + o["lat"] - o["cost"] for o, c in zip(ops, cost)]
+        cases.append(([[(j, cost[j] if j not in o["hard"] and eng[j] == o["eng"] else max(lat[j], cost[j]) + hop) for j in lean[i]]
+                       for i, o in enumerate(ops)], cost, lat))
+
+    def run(seq, case):
+        before, cost, lat = case
+        t, by, free = [0.0] * n, [-1] * n, {}
+        end, last = 0.0, -1
+        for i in seq:
+            s, b = 0.0, -1
+            for j, w in before[i]:
+                if t[j] + w > s:
+                    s, b = t[j] + w, j
+            e = eng[i]
+            if e is not None:
+                p = free.get(e)
+                if p is not None and t[p] + cost[p] > s:
+                    s, b = t[p] + cost[p], -2 - p
+                free[e] = i
+            t[i], by[i] = s, b
+            if s + lat[i] > end:
+                end, last = s + lat[i], i
+        return end + 0.3 * sum(t) / n, t, by, last, end
+
+    seq = sorted(range(n), key=lambda i: (at[i], i))
+    now = [run(seq, c) for c in cases]
+    weight = [66.0 / r[4] / len(cases) for r in now]
+    val = sum(w * r[0] for w, r in zip(weight, now))
+    best = (val, seq)
+    for it, r in enumerate(rng.random((ROUNDS, 7)).tolist()):
+        slack = 0.12 * (0.015 / 0.12) ** (it / ROUNDS)
+        _v, _t, by, last, _e = now[int(r[6] * len(cases))]
+        pairs, i = [], last if r[0] < 0.7 else int(r[1] * n)
+        while i != -1:
+            if by[i] <= -2:
+                pairs.append((-2 - by[i], i))
+            i = -2 - by[i] if by[i] <= -2 else by[i]
+        if not pairs:
+            continue
+        p, i = pairs[int(r[2] * len(pairs))]
+        a, b = seq.index(p), seq.index(i)
+        more = int(-math.log2(1 - r[3]))
+        if r[5] < 0.5:
+            for _k in range(more):
+                c = a - 1
+                while c >= 0 and eng[seq[c]] != eng[i]:
+                    c -= 1
+                if c < 0 or anc[i] >> seq[c] & 1:
+                    break
+                a = c
+            if anc[i] >> seq[a] & 1:
+                continue
+            mid = seq[a:b]
+            new = seq[:a] + [j for j in mid if anc[i] >> j & 1] + [i] + [j for j in mid if not anc[i] >> j & 1] + seq[b + 1:]
+        else:
+            for _k in range(more):
+                c = b + 1
+                while c < n and eng[seq[c]] != eng[p]:
+                    c += 1
+                if c >= n or anc[seq[c]] >> p & 1:
+                    break
+                b = c
+            if anc[seq[b]] >> p & 1:
+                continue
+            mid = seq[a + 1:b + 1]
+            new = seq[:a] + [j for j in mid if not anc[j] >> p & 1] + [p] + [j for j in mid if anc[j] >> p & 1] + seq[b + 1:]
+        got = [run(new, c) for c in cases]
+        v = sum(w * q[0] for w, q in zip(weight, got))
+        if v <= val or r[4] < math.exp((val - v) / slack):
+            val, now = v, got
+            seq = sorted(new, key=lambda j: got[0][1][j])
+            if val < best[0]:
+                best = (val, seq)
+    OPT["ends"] = [round(run(best[1], c)[4], 1) for c in cases]
+    t = run(best[1], cases[0])[1]
+    for k, i in enumerate(best[1]):
+        t[i] += 1e-7 * k
+    return t
 
 
 KNOWN = {}
-ROUNDS, JIT = 3000, 4.0
+ROUNDS = 180000
+CASES = [(1.0, 1.0, 1.0, 0.13, 1.0)]
+OPT = {"fl": [1280, 480], "aud": [3.1, 0.8], "gua": [3.0, "S"], "l0": 3.0, "l1": 4.0, "l2": 8.0, "nm": 16.0, "pc": 1, "pen": 0, "last": 128, "xs": [0, 1, 1], "mxl": [0, 1, 1]}
 
 
 def rank_program(g, core, T, topo):
     rank = T.rank_of(core)
     if rank is None:
-        return
+        return hand_on(g, core, T, topo)
+    if "t" not in KNOWN:
+        order(max((build(r, c, T, topo) for r, c in enumerate(T.cores)), key=len))
     ops = build(rank, core, T, topo)
     seq = order(ops)
     queue = {"V": g.vector, "S": g.scalar, "P": g.tensor, "G": g, "Y": g.sync}

@@ -10,13 +10,13 @@ E2B = E2A + 8192
 G2 = E2B + 256
 NMW = G2 + 400
 GB = [G0, G1, G2]
-RW, BW, IW, UW, WW = 6400, 4736, 640, 1024, 3840
+RW, BW, IW, UW, WW = 6912, 5376, 768, 1024, 3840
 SCRATCH = {
     "au0": ("sbuf", [128, 4112], BF), "au1": ("sbuf", [128, 4112], BF), "au2": ("sbuf", [128, 4112], BF),
-    "xb": ("sbuf", [128, 4352], F32),
+    "xb": ("sbuf", [128, 384 + 4864], F32),
     "da": ("sbuf", [128, 4352], F32), "db": ("sbuf", [128, 4352], F32),
     "fl": ("sbuf", [128, 4352], BF), "sg": ("sbuf", [128, 4096], BF),
-    "nm": ("sbuf", [128, NMW], F32), "zw": ("sbuf", [128, 384 + 4864], BF), "zf": ("sbuf", [128, 256 + 4864], F32),
+    "nm": ("sbuf", [128, NMW], F32), "zf": ("sbuf", [128, 256 + 4864], F32),
     "rf": ("sbuf", [128, RW], F32), "rb": ("sbuf", [128, BW], BF), "ri": ("sbuf", [128, IW], I32),
     "wu": ("sbuf", [128, UW], U16), "wf": ("sbuf", [128, WW], F32),
     "spi": ("sbuf", [128, 256], I32), "gui": ("sbuf", [128, 256], I32), "lni": ("sbuf", [128, 256], I32),
@@ -25,7 +25,7 @@ SCRATCH = {
 }
 for _k in range(8):
     SCRATCH["p%d" % _k] = ("psum", [128, 32, 16] if _k == 2 else [128, 512], F32)
-SEMAPHORES = (["cV", "cS", "cP", "cG"] + ["d%d" % k for k in range(16)] + ["lo%d" % k for k in range(12)]
+SEMAPHORES = (["cV", "cS", "cP", "cG"] + ["d%d" % k for k in range(20)] + ["lo%d" % k for k in range(12)]
               + ["a1h0", "a1h1", "a1h2", "a1h3", "a2h0"] + ["rc%d" % t for t in range(3)] + ["rn%d" % t for t in range(3)])
 
 CUTS = [[0, 512, 1280, 2048, 2816, 3584, 3840, 4096], list(range(0, 4097, 512)), list(range(0, 4097, 512))]
@@ -34,7 +34,7 @@ HOP = 0.13
 BIG = float(1 << 23)
 HOLD = float(1 << 24)
 RND = float(3 << 22)
-C0 = [0.0, 23.5 / 32, 1 + 23.5 / 32]
+C0 = 23.5 / 32
 VIA = [0, 2]
 VG = [4, 4, 2]
 
@@ -177,10 +177,14 @@ def build(rank, core, T, topo):
         add("V", lambda g: g.vector.memset(R(out), v), [out], [], vcost(out, [out]))
         return out
 
-    def act(out, a, func, bias=0.0, scale=1.0):
+    def act(out, a, func, bias=0.0, scale=1.0, total=None):
         out = room(out, a)
         c = max(count(a) * (1.56 if a[0] == "ind" else 1), 64) * CY + 0.05
-        add("S", lambda g: g.scalar.activation(R(out), R(a), func, bias=R(bias), scale=R(scale)), [out], [a, bias, scale], c)
+        if total is None:
+            add("S", lambda g: g.scalar.activation(R(out), R(a), func, bias=R(bias), scale=R(scale)), [out], [a, bias, scale], c)
+        else:
+            add("S", lambda g: g.scalar.activation(R(out), R(a), func, bias=R(bias), scale=R(scale), accum_out=R(total)),
+                [out, total], [a, bias, scale], c + 0.02)
         return out
 
     def lin_(out, a, scale, bias):
@@ -248,12 +252,13 @@ def build(rank, core, T, topo):
 
     au = ["au0", "au1", "au2"]
     lni, spi, gui = ap("lni", 0, 256, 1, (0, 8)), ap("spi", 0, 256), ap("gui", 0, 256)
-    dma([(lambda: R(lni), lambda: T.lens[:])], [lni], [], 2.2, "S")
+    dma([(lambda: R(lni), lambda: T.lens[:])], [lni], [], 1.6, "S")
     for h in range(4):
         a = ap("au0", 1024 * h, 1024 * h + 1024)
-        dma([(lambda a=a: R(a), lambda h=h: T.aud[:, 1024 * h:1024 * h + 1024])], [a], [], OPT["aud"][0] + OPT["aud"][1] * h)
-    dma([(lambda: R(spi), lambda: T.spots[:])], [spi], [], 2.6, "S")
-    dma([(lambda: R(gui), lambda: T.gua[:])], [gui], [], *OPT["gua"])
+        s = dma([(lambda a=a: R(a), lambda h=h: T.aud[:, 1024 * h:1024 * h + 1024])], [a], [], OPT["aud"][0] + OPT["aud"][1] * h)
+        ops[s]["after"] = [s - 1] if h else []
+    dma([(lambda: R(spi), lambda: T.spots[:])], [spi], [], 2.0, "S")
+    ops[dma([(lambda: R(gui), lambda: T.gua[:])], [gui], [], OPT["aud"][0] + 3 * OPT["aud"][1] + 0.4)]["after"] = [s]
     mine, theirs = helper(rank, T, topo), helper(rank + 1, T, topo)
     s = None
     for h in range(4):
@@ -270,13 +275,13 @@ def build(rank, core, T, topo):
     RB = iota(new("rb", 384), [[0, 24], [2048, 16]], 0, 0)
     J = iota(new("nm", 128), [[1, 128]], 0, 0)
     s1 = s
-    JH, PCR, CROW = new("nm", 240), new("nm", 1024), new("rb", 256)
+    JH, PCR, CROW = new("nm", 240), new("nm", 1024), new("rf", 256)
     iota(ap("nm", XA + 4096, XA + 4352), [[0, 256]], 0, 0, [s])
     iota(ap("xb", 4096, 4352), [[0, 256]], 0, 0, [s])
     iota(ap("zf", 256, 640), [[0, 384]], 0, 0, [s])
     J16, J128 = sub(J, 0, 16), sub(J, 0, 128)
     FL = ap("fl", 0, 4352)
-    ZERO = ms(ap("zw", 0, 256), 0.0)
+    ZERO = ms(new("rb", 256), 0.0)
     pcol = cp("wf", pi)
     B8 = sub(new("rf", 128), 0, 128, 1, (0, 8))
     ts(B8, sub(JB, 0, 128, 1, (0, 8)), sub(pcol, 0, 1, 1, (0, 8)), ALU.is_equal)
@@ -321,19 +326,24 @@ def build(rank, core, T, topo):
     CM = lin_(sub(CE, 16, 32), C16, 1.0, float(E2B - G2))
     C272 = tt("wf", lin_("wf", C16, 1.0, 272.0), act("wf", C16, AF.Sign, 255.0, -1.0), ALU.mult)
     DUM2 = lin_("wf", C16, 1.0, 4352.0)
+    I16 = lin_("rb", IF, 1.0 / 16, 0.0)
     C16K = lin_("wf", C16, 16384.0, 5632.0)
-    RST = act("wf", sub(J, 0, 32), AF.Sign, -16.0)
-    RST = act("wf", RST, AF.Square)
+    RST = iota(new("wf", 32), [[0, 32]], 1, 0, [s])
+    iota(sub(RST, 16, 17), [[0, 1]], 0, 0, [s])
     T2B = new("wf", 32)
     lin_(sub(T2B, 16, 32), J16, 0.0, 0.0)
-    AH16 = tt("wf", ts("wf", J16, icol, ALU.not_equal), ts("wf", J16, lin_("wf", icol, 1.0, 1.0), ALU.is_equal, HOLD - 1, ALU.mult), ALU.add)
-    AH = act("rb", ind(AH16, ts("wu", sub(ZERO, 0, 24), icol, ALU.add)), AF.Copy)
+    AH = new("rb", 384)
+    AH16 = tt(sub(AH, 0, 16), ts("wf", J16, icol, ALU.not_equal), ts("wf", J16, lin_("wf", icol, 1.0, 1.0), ALU.is_equal, HOLD - 1, ALU.mult), ALU.add)
+    for lo, k in ((16, 3), (64, 5)):
+        dma([(lambda a=a, lo=lo: R(sub(AH, a, a + lo)), lambda lo=lo: R(sub(AH, 0, lo))) for a in range(lo, lo + k * lo, lo)],
+            [sub(AH, lo, lo + k * lo)], [sub(AH, 0, lo)], 4.0)
     inv = lin_("wf", i15, 1.0 - 1.0 / HOLD, 1.0 / HOLD)
     for k in range(3):
         if k:
             lin_(ap(au[k], 4096, 4104), sub(J, 0, 8), 0.0, float(1 << 21))
         if k == 2:
-            lin_(ap(au[k], 4104, 4112), sub(J, 0, 8), 0.0, 0.0)
+            Z8 = act(ap(au[k], 4104, 4112), sub(JB, 0, 8), AF.Silu, 0.0, 0.0)
+            ops[-1]["cost"] = ops[-1]["lat"] = 1.4
         lin_(ap("nm", GB[k] + 384, GB[k] + 400), J16, 0.0, 4097.0)
     END, WX, CODE, NC = new("rf", 257), new("rf", 257), new("rf", 257), new("rf", 257)
     T1, T2 = new("rb", 272), new("rb", 272)
@@ -361,6 +371,17 @@ def build(rank, core, T, topo):
         mm(ps, [(BOS, mx)])
         return act(out, ps, AF.Copy)
 
+    def strew(w, row, t):
+        if OPT["sil"][t]:
+            add("S", lambda g: g.scalar.activation(R(w), R(row), AF.Silu), [w], [row, Z8], 0.97)
+        else:
+            cp(w, row)
+
+    def fill(w, n, offs, t):
+        strew(ind(w, offs), CROW, t)
+        scan(sub(FIB, 0, n), sub(w, 0, n), sub(w, 0, n), 0.0, ALU.max, ALU.max)
+        return wrap(WAB, sub(FIB, 0, n))
+
     def pick(row):
         return [(SEL[a], sub(row, a, 256, 16)) for a in range(16)]
 
@@ -387,7 +408,12 @@ def build(rank, core, T, topo):
     act(SG1, NG, AF.Sign, 0.5)
     zw = ts("wf", mm(sub(pe, 0, 16), pick(SG1)), -1.0 / 32, ALU.is_lt)
     stat = tt("wf", lin_("wf", nw0, -0.5, ni8k), zw, ALU.subtract)
-    act(ap("db", 4096, 4352), NG, AF.Copy)
+    if not all(OPT["wd"][1:]):
+        stat1 = lin_("wf", stat, 1.0, -C0)
+    if any(OPT["wd"]):
+        stat2 = lin_("wf", stat, 1.0, lin_("wf", icol, 8192.0, -C0))
+        ZU, ZD = lin_("rb", Z, 8.0, 0.0), lin_("rb", Z, -8.0, 0.0)
+    dma([(lambda: T.db[:, 4096:4352], lambda: R(NG))], [ap("db", 4096, 4352)], [NG], 4.0)
 
     SPF = ts("rf", spi, 1.0, ALU.add)
     for h in range(2):
@@ -400,23 +426,23 @@ def build(rank, core, T, topo):
     pairs = [(lambda g_=g_: T.lin[g_, 16:4112], lambda g_=g_: T.st3[:, g_, :, :]) for g_ in range(8)]
     pairs += [(lambda: T.lin[:, 0:16], lambda: R(zp8)), (lambda: T.lin[:, 4112:4128], lambda: R(zp8))]
     s = dma(pairs, [lin], [ap("st3", 0, 256), zp8], 4.0)
-    dma([(lambda i=i: T.nm[i:128:16, NB:NB + 4112], lambda: T.lin[:, 16:4128]) for i in range(16)], [ap("nm", NB, NB + 4112)], [lin], OPT["nm"])
-    far2, got = C[(rank - 2) % N], ap("au1", 0, 4096)
+    dma([(lambda i=i: T.nm[i:128:16, NB:NB + 4112], lambda: T.lin[:, 16:4128]) for i in range(8)], [ap("nm", NB, NB + 4112, 2)], [lin], OPT["nm"])
+    far2, got, turn = C[(rank - 2) % N], ap("au1", 0, 4096), ap("cs", 1, 2)
     lo = 0 if relayed(rank - 1) else 2048
-    out = [send([(ap("au1", lo, 4096), ap("au2", lo, 4096), prv, topo.engines(core, prv), "a2h0")], 1.0, [lin, got])]
+    out = [send([(ap("au1", lo, 4096), ap("au2", lo, 4096), prv, topo.engines(core, prv), "a2h0")], 4.5, [turn, got])]
     if not relayed(rank - 2):
-        out.append(send([(ap("au0", 0, 2048), ap("au2", 0, 2048), far2, topo.engines(core, far2), "a2h0")], 1.0, [lin, got]))
+        out.append(send([(ap("au0", 0, 2048), ap("au2", 0, 2048), far2, topo.engines(core, far2), "a2h0")], 4.5, [turn, got]))
         ops[out[1]]["more"] = True
+    dma([(lambda i=i: T.nm[i:128:16, NB:NB + 4112], lambda: T.lin[:, 16:4128]) for i in range(8, 16)], [ap("nm", NB + 1, NB + 4112, 2), turn], [lin], OPT["nm"])
     recv(ap("au2", 0, 4096), "a2h0", len(topo.engines(nxt, core)) + (0 if relayed(rank) else len(topo.engines(C[(rank + 2) % N], core))),
          out, OPT["l2"])
     out = [s1] + out
     iota(JH, [[1, 240]], 128, 0, out[:1])
     lin_(POS8, sub(J, 0, 256), -131072.0, ni8k)
-    iota(CROW, [[1, 256]], 1, 0, out[:1])
-    iota(ap("zw", 256, 768), [[0, 512]], 0, 0, out[:1])
+    iota(CROW, [[16, 256]], 16, 0, out[:1])
     iota(ap("zf", 0, 256), [[0, 256]], 0, 0, out)
     iota(PCR, [[8192, 1024]], 8192, 0, out)
-    WIN = ap("db", 0, 4112)
+    WIN = ap("zf", 544, 4656)
     assert free["nm"] == E2B
 
     XS, SG2 = new("rf", 256), new("rb", 256)
@@ -430,8 +456,9 @@ def build(rank, core, T, topo):
         x = [ap("nm", XA, XA + 4352), ap("xb", 0, 4352)][t % 2]
         d = ap(["da", "db"][t % 2], 0, 4352)
         tab = ap(au[t], 0, 4096)
-        for k in range(8):
-            o, src = sub(x, 512 * k, 512 * k + 512), ind(tab, sub(SPU, 32 * k, 32 * k + 32))
+        w = 2 if t == 0 else 1
+        for k in range(0, 8, w):
+            o, src = sub(x, 512 * k, 512 * (k + w)), ind(tab, sub(SPU, 32 * k, 32 * (k + w)))
             if k >= 8 - VG[t]:
                 cp(o, src)
             else:
@@ -448,8 +475,11 @@ def build(rank, core, T, topo):
         scan(sub(WX, 1, 257), SG2, ZERO, 0.0, ALU.add, ALU.add)
         tt(sub(T1, 16, 272), ind(WX, UO), EQ, ALU.mult)
         lin_(sub(T2, 15, 272), LT, sub(WX, 256, 257), 0.0)
+        if OPT["wd"][t]:
+            return mm(sub(pd, 0, 16), [(IF, stat2)] + [(sub(z, 15 - a, 143 - a), sub(row, o + a, o + 256, 16))
+                                                       for row in (T2, T1) for z, o in ((ZU, 16), (ZD, 15)) for a in range(16)] + [(IF, st["l"])])
         mm(sub(pd, 0, 256), [(BOP, sub(RB, 0, 256)), (BOP, sub(T2, 16, 272)), (BON, sub(T2, 15, 271)), (BOP, sub(T1, 16, 272)), (BON, sub(T1, 15, 271))])
-        return tt("wf", wrap(WC, sub(pd, 0, 256)), tt("wf", lin_("wf", stat, 1.0, -C0[t]) if t else stat, st["l"], ALU.add), ALU.add)
+        return tt("wf", wrap(WC, sub(pd, 0, 256)), tt("wf", stat1 if t else stat, st["l"], ALU.add), ALU.add)
 
     def light(t, d):
         Gt = GB[t]
@@ -463,7 +493,7 @@ def build(rank, core, T, topo):
             if t == 2:
                 u = tt(NB2, ind(tab, st["OZ"]), act(NA, dk, AF.Copy), ALU.add)
                 act(SG1, u, AF.Sign, 0.5)
-                terms.append((IF, ts("wf", mm(sub(pe, 16, 32), pick(SG1)), -1.0 / 32, ALU.is_gt)))
+                terms.append((IF, ts("wf", mm(sub(pe, 16, 32), pick(SG1)), -1.0 / 32, ALU.is_lt, -1.0, ALU.mult)))
                 na = lin_(NA, u, -1.0, 0.0)
             else:
                 na = lin_(NA, dk, -1.0, 0.0)
@@ -474,8 +504,9 @@ def build(rank, core, T, topo):
             m0 = RND if t else 0.0
             if t:
                 d = lin_("wf", v, 1.0, RND)
-            act(x0, d, AF.Relu, -m0)
-            act(x1, d, AF.Relu, m0, -1.0)
+            rs = new("wf", 2)
+            act(x0, d, AF.Relu, -m0, 1.0, sub(rs, 0, 1))
+            act(x1, d, AF.Relu, m0, -1.0, sub(rs, 1, 2))
             act(e8, d, AF.Relu, 8192.0 * (m0 + 1), -8192.0)
         else:
             if t:
@@ -484,7 +515,7 @@ def build(rank, core, T, topo):
             ts(e8, v if t else d, 0.5, ALU.is_lt, 8192.0, ALU.mult)
             ts(x0, d, 0.0, ALU.max)
         sc = scan("wf", RST, x, 0.0, ALU.mult, ALU.add)
-        mm(sub(pw, 0, 2), [(BO, sub(sc, 15, 32, 16))])
+        mm(sub(pw, 0, 2), [(BO, rs if OPT["xs"][t] else sub(sc, 15, 32, 16))])
         ex = mm(sub(pb, 0, 32), [(UI, x), (IF, T2B), (BO, sc)])
         mm(blk(0, 2), [(US, x), (BO, sc)])
         mm(blk(2, 4), [(UI, x), (BO, sc)])
@@ -492,38 +523,48 @@ def build(rank, core, T, topo):
         cs, cn = ap("cs", 4 * t, 4 * t + 1), ap("cn", 4 * t, 4 * t + 1)
         OU = ts("wu", tt("wf", sub(ex, 0, 16), DUM2, ALU.min), mn, ALU.subtract)
         ts(cs, sub(pw, 0, 1), mn, ALU.subtract, 384.0, ALU.min)
-        s = send([(cs, cn, nxt, small(rank), "rc%d" % t)], 1.0)
-        recv(cn, "rc%d" % t, len(small(rank - 1)), [s], 1.5)
+        s = send([(cs, cn, nxt, small(rank), "rc%d" % t)], 0.65)
+        recv(cn, "rc%d" % t, len(small(rank - 1)), [s], OPT["hop"])
         jj = lin_("wf", JJ, 1.0, mn)
         idx = ts(sub(new("wf", 48), 32, 48), sub(ex, 16, 32), mn, ALU.subtract, 384.0, ALU.min)
         top = [4112, E1 + 256, E2B + 256][t]
+        RU, parts = new("wu", 24), ((16, 24), (0, 16)) if OPT["split"][t] else ((0, 24),)
         if t == 0:
             tt(MX, ind(tt("wf", nw0, x0, ALU.subtract), JO), sub(AM, 0, 256), ALU.mult)
-            kept = scan(sub(NC, 1, 257), mm(sub(pa, 0, 256), [(BOS, MX)]), ZERO, 0.0, ALU.add, ALU.add)
-            cp(ind(ap("zf", 256, 256 + 4864), OU), kept)
+            kept = scan(sub(NC, 1, 257), mm(sub(pa, 0, 256), [(BOS, MX)]), ZERO, 32.0, ALU.add, ALU.add)
+            strew(ind(ap("zf", 256, 256 + 4864), OU), kept, 0)
             scan(BKG, ap("zf", 256, 640), ap("zf", 256, 640), 0.0, ALU.max, ALU.max)
-            RU = ts("wu", tt("wf", wrap(WA, BKG), jj, ALU.add), top - 1.0, ALU.min)
+            for lo, hi in parts:
+                w = wrap(sub(WA, 16 * lo, 16 * hi), sub(BKG, 16 * lo, 16 * hi))
+                ts(sub(RU, lo, hi), tt("wf", w, sub(jj, lo, hi), ALU.add), -32.0, ALU.add, top - 1.0, ALU.min)
         else:
-            rm = tt("wf", x0, st["m"], ALU.subtract)
-            off = tt("wf", tt("wf", st["bk"], rm, ALU.subtract), ts("wf", rm, 512.0, ALU.min, 8192.0, ALU.mult), ALU.add)
+            rm = tt("wf", st["m"], x0, ALU.subtract)
+            rc = ts("wf", rm, -512.0, ALU.max, -8192.0, ALU.mult)
+            if OPT["po"][t]:
+                off = mm(sub(pa, 256, 272), [(IF, st["bk"]), (IF, rm), (IF, rc)])
+            else:
+                off = tt("wf", tt("wf", st["bk"], rm, ALU.add), rc, ALU.add)
             unwrap(sub(NC, 1, 257), tt("wf", ts("wf", sub(ex, 0, 16), 8191.0, ALU.mult), off, ALU.add), MX, sub(pa, 0, 256))
             zo = 768 - 384 * t
-            cp(ind(ap("zw", zo, 384 + 4864), OU), CROW)
-            scan(FIB, ap("zw", zo, zo + 384), ap("zw", zo, zo + 384), 0.0, ALU.max, ALU.max)
-            c1 = wrap(WAB, FIB)
-            act(BKG, ind(NC, cp("wu", c1)), AF.Copy)
-            cj = tt("wf", c1, lin_("wf", jj, 8192.0, 16384.0 + 511.0 + [0, E1, E2A][t]), ALU.add)
             if t == 1:
-                pf = wrap(WA, BKG)
-                p = cp("ri", pf)
-            else:
-                pf = p = ts("ri", hold(WA, BKG), inv, ALU.mult)
-            far = tt("wf", tt("wf", cj, pf, ALU.subtract), jj, ALU.max)
-            RU = ts("wu", tt("wf", far, ts("ri", p, 8191, ALU.bitwise_and), ALU.add), -512.0, ALU.add, top - 1.0, ALU.min)
+                iota(ap("xb", 384, 768), [[0, 384]], 0, 0)
+                iota(ap("xb", 0, 384), [[0, 384]], 0, 0)
+            c1 = fill(ap("xb", zo, 384 + 4864), 384, OU, t)
+            cu = ts("wu", c1, 1.0 / 16, ALU.mult)
+            cj = mm(sub(pw, 16, 40), [(IF, lin_("wf", jj, 8192.0, 16384.0 + 511.0 + [0, E1, E2A][t])), (I16, c1)])
+            for lo, hi in parts:
+                row, wa = act(sub(BKG, 16 * lo, 16 * hi), ind(NC, sub(cu, lo, hi)), AF.Copy), sub(WA, 16 * lo, 16 * hi)
+                if t == 1:
+                    pf = wrap(wa, row)
+                    p = cp("ri", pf)
+                else:
+                    pf = p = ts("ri", hold(wa, row), inv, ALU.mult)
+                far = tt("wf", tt("wf", sub(cj, lo, hi), pf, ALU.subtract), sub(jj, lo, hi), ALU.max)
+                ts(sub(RU, lo, hi), tt("wf", far, ts("ri", p, 8191, ALU.bitwise_and), ALU.add), -512.0, ALU.add, top - 1.0, ALU.min)
         snd, arr = sub(SND, 128 * t, 128 * t + 128), ap("nm", Gt + 256, Gt + 384)
         act(snd, ind(ap("nm", NB, top), sub(RU, 16, 24)), AF.Copy)
-        s = send([(snd, arr, nxt, small(rank), "rn%d" % t)], 1.2)
-        recv(arr, "rn%d" % t, len(small(rank - 1)), [s], 1.6)
+        s = send([(snd, arr, nxt, small(rank), "rn%d" % t)], 0.8)
+        recv(arr, "rn%d" % t, len(small(rank - 1)), [s], OPT["hop"])
         act(ap("nm", Gt, Gt + 256), ind(ap("nm", NB, top), sub(RU, 0, 16)), AF.Copy)
         t1 = tt("wf", cum, blk(0, 4, 2), ALU.subtract)
         gp = ts("wf", blk(1, 4, 2), mn, ALU.subtract, cn, ALU.min)
@@ -538,19 +579,20 @@ def build(rank, core, T, topo):
             gw = ap("nm", G0, G0 + 400)
             EN = cp("wu", tt("wf", ts("wf", m, 1.0, ALU.is_lt, 384.0, ALU.mult), idx, ALU.max))
             en = ap("nm", E1, E1 + 256)
-            st["mq"] = lin_("wf", m, 1.0, -1.0 - C0[1])
+            st["mq"] = lin_("wf", m, 1.0, -1.0 - C0)
         else:
             gw = ap("nm", E1, G1 + 400)
             mm_ = tt("wf", st["m"], m, ALU.min)
             nf = tt("wf", m, mm_, ALU.subtract)
             ex2 = new("wf", 32)
             ix = tt(sub(ex2, 16, 32), ts("wf", nf, -384.0, ALU.mult, 384.0, ALU.add), idx, ALU.max)
-            tt(sub(ex2, 0, 16), tt("wf", CM, lin_("wf", mm_, -16384.0, 16384.0), ALU.add), ix, ALU.min)
+            gone = lin_("wf", mm_, -16384.0, 16384.0)
+            tt(sub(ex2, 0, 16), mm(sub(pw, 64, 80), [(IF, CM), (IF, gone)]) if OPT["po"][0] else tt("wf", CM, gone, ALU.add), ix, ALU.min)
             EU = ts("wu", ex2, 256.0, ALU.add)
             EN, en = sub(EU, 16, 32), ap("nm", E2B, E2B + 256)
             act(ap("nm", E2A, E2A + 256), ind(gw, sub(EU, 0, 16)), AF.Copy)
             st["OZ"] = ts("wu", tt("wf", st["en"], mm_, ALU.mult), 4104.0, ALU.add)
-            st["mq"] = lin_("wf", nf, 1.0, -C0[2])
+            st["mq"] = lin_("wf", nf, 1.0, -C0)
             unwrap(BKR, bk, MX, sub(pa, 0, 256))
             f = new("wf", 32)
             act(sub(f, 0, 16), m, AF.Relu, 16384.0, -16384.0)
@@ -576,7 +618,7 @@ def build(rank, core, T, topo):
         EU = ts("wu", ex, float(G2 - E2A), ALU.add)
         cw, dw = sub(cum, 0, 16), sub(cum, 16, 32)
         kw = tt(sub(cum, 32, 48), dw, k, ALU.add)
-        code = unwrap(sub(NC, 1, 257), tt("wf", st["ck"], dw, ALU.subtract), MX, sub(pa, 0, 256))
+        code = unwrap(NB2, tt("wf", st["ck"], dw, ALU.subtract), MX, sub(pa, 0, 256))
         q32 = ts("ri", cum, 0.0625, ALU.mult, -0.46875, ALU.add)
         pe_, pq_ = sub(q32, 0, 16), sub(q32, 16, 32)
         OU = cp("wu", tt("wf", tt("wf", tt("wf", pq_, pe_, ALU.is_equal), C272, ALU.mult), pq_, ALU.max))
@@ -585,13 +627,21 @@ def build(rank, core, T, topo):
         r4 = ts("ri", cp("ri", sub(cum, 16, 80)), 15, ALU.bitwise_and)
         PU = cp("wu", r4)
         BU = ts("wu", tt("wf", beg16, sub(r4, 0, 16), ALU.subtract), 4111.0, ALU.min)
-        cp(ind(ZF, OU), code)
-        scan(FIL, sub(ZF, 0, 256), sub(ZF, 0, 256), 0.0, ALU.max, ALU.max)
-        nw = wrap(WA, FIL)
-        act(sub(BKG, 0, 256), ind(BKR, ts("wu", nw, 1.0 / 16384, ALU.mult)), AF.Copy)
-        a = tt("ri", nw, JV, ALU.add)
-        y5 = ts("ri", a, 16383, ALU.bitwise_and)
-        c4 = ts("ri", a, 12, ALU.arith_shift_right, 1020, ALU.bitwise_and)
+        if OPT["sil"][3]:
+            c1 = fill(ZF, 256, OU, 3)
+            cu = ts("wu", c1, 1.0 / 16, ALU.mult, -1.0, ALU.add)
+            nw = wrap(WA, act(FIL, ind(code, cu), AF.Copy))
+            act(sub(BKG, 0, 256), ind(BKR, cu), AF.Copy)
+            y5 = ts("ri", tt("ri", nw, JV, ALU.add), 16383, ALU.bitwise_and)
+            c4 = lin_("wf", c1, 0.25, -4.0)
+        else:
+            cp(ind(ZF, OU), code)
+            scan(FIL, sub(ZF, 0, 256), sub(ZF, 0, 256), 0.0, ALU.max, ALU.max)
+            nw = wrap(WA, FIL)
+            act(sub(BKG, 0, 256), ind(BKR, ts("wu", nw, 1.0 / 16384, ALU.mult)), AF.Copy)
+            a = tt("ri", nw, JV, ALU.add)
+            y5 = ts("ri", a, 16383, ALU.bitwise_and)
+            c4 = ts("ri", a, 12, ALU.arith_shift_right, 1020, ALU.bitwise_and)
         GU = ts("wu", tt("wf", ts("wf", y5, 5632.0, ALU.max, 5635.0, ALU.min), c4, ALU.add), -5632.0, ALU.add)
         AU = ts("wu", tt("wf", wrap(WB, sub(BKG, 0, 256)), y5, ALU.add), 16.0 - 5632.0 - 16896.0, ALU.add, 4111.0, ALU.min)
         HJ = lin_(MX, ind(PCR, GU), 1.0, 4097.0)
@@ -610,7 +660,7 @@ def build(rank, core, T, topo):
         scan(PS, PEN, PC, 8192.0, ALU.add, ALU.max)
         o = sub(pe, 128, 256, 1, (0, 16))
         add("P", lambda g: g.tensor.transpose(R(o), R(l), R(IF)), [o], [l, IF], 0.45, 0.5)
-        yn = act(sub(NB2, 0, 128, 1, (0, 16)), o, AF.Copy)
+        yn = act(sub(WD, 0, 128, 1, (0, 16)), o, AF.Copy)
         dma([(lambda g_=g_: T.yn[g_, :], lambda g_=g_: R(sub(yn, 16 * g_, 16 * g_ + 16, 1, (0, 16)))) for g_ in range(8)], [], [yn], 2.5)
         tcol = lin_("wf", mm(sub(pw, 8, 9), [(S15, sub(cw, 15, 16))]), 8192.0, -4096.0)
         mk = lin_(sub(pc, 0, 256), act(NA, POS8, AF.Relu, tcol), 1.0, -1.0)
@@ -621,11 +671,11 @@ def build(rank, core, T, topo):
             hi = lo + OPT["last"]
             h3 = tt(sub(gui, lo, hi), sub(FIL, lo, hi), sub(CODE, lo, hi), ALU.min)
             tt(sub(YO, lo, hi), ts(sub(spi, lo, hi), h3, 4095, ALU.bitwise_and), sub(mk, lo, hi), ALU.min)
-        dma([(lambda: T.yo[:], lambda: R(YO))], [], [YO], 2.5)
+            dma([(lambda lo=lo, hi=hi: T.yo[:, lo:hi], lambda lo=lo, hi=hi: R(sub(YO, lo, hi)))], [], [sub(YO, lo, hi)], 2.3, "Y" if lo else "S")
 
     light(0, heavy(0))
+    dma([(lambda i=i: T.zf[i:128:16, 544:4656], lambda i=i: T.lin[:, i:i + 4112]) for i in range(16)], [WIN, sub(SND, 0, 128)], [lin], 13.0)
     light(1, heavy(1))
-    dma([(lambda i=i: T.db[i:128:16, 0:4112], lambda i=i: T.lin[:, i:i + 4112]) for i in range(16)], [WIN], [lin], 13.0)
     final(*light(2, heavy(2)))
     return ops
 
@@ -702,7 +752,7 @@ def order(ops):
         return max(at[i] + ops[i]["lat"] for i in range(n))
 
     if "t" not in KNOWN:
-        rng = np.random.default_rng(1)
+        rng = np.random.default_rng(OPT["seed"])
         at = place([-v for v in lev], False)
         best = (span(at), at)
         for it in range(ROUNDS // 300):
@@ -740,11 +790,12 @@ def improve(ops, pre, cost, at, rng):
         cases.append(([[(j, cost[j] if j not in o["hard"] and eng[j] == o["eng"] else max(lat[j], cost[j]) + hop) for j in lean[i]]
                        for i, o in enumerate(ops)], cost, lat))
 
-    def run(seq, case):
+    def run(seq, case, a=0, old=None):
         before, cost, lat = case
-        t, by, free = [0.0] * n, [-1] * n, {}
+        t, by = (old[1][:], old[2][:]) if a else ([0.0] * n, [-1] * n)
+        free = {eng[i]: i for i in seq[:a]}
         end, last = 0.0, -1
-        for i in seq:
+        for i in seq[a:]:
             s, b = 0.0, -1
             for j, w in before[i]:
                 if t[j] + w > s:
@@ -766,7 +817,7 @@ def improve(ops, pre, cost, at, rng):
     val = sum(w * r[0] for w, r in zip(weight, now))
     best = (val, seq)
     for it, r in enumerate(rng.random((ROUNDS, 7)).tolist()):
-        slack = 0.12 * (0.015 / 0.12) ** (it / ROUNDS)
+        slack = OPT["hot"] * (0.015 / OPT["hot"]) ** (it / ROUNDS)
         _v, _t, by, last, _e = now[int(r[6] * len(cases))]
         pairs, i = [], last if r[0] < 0.7 else int(r[1] * n)
         while i != -1:
@@ -802,7 +853,8 @@ def improve(ops, pre, cost, at, rng):
                 continue
             mid = seq[a + 1:b + 1]
             new = seq[:a] + [j for j in mid if not anc[j] >> p & 1] + [p] + [j for j in mid if anc[j] >> p & 1] + seq[b + 1:]
-        got = [run(new, c) for c in cases]
+        a = min(a, n - 40)
+        got = [run(new, c, a, q) for c, q in zip(cases, now)]
         v = sum(w * q[0] for w, q in zip(weight, got))
         if v <= val or r[4] < math.exp((val - v) / slack):
             val, now = v, got
@@ -817,9 +869,9 @@ def improve(ops, pre, cost, at, rng):
 
 
 KNOWN = {}
-ROUNDS = 180000
-CASES = [(1.0, 1.0, 1.0, 0.13, 1.0)]
-OPT = {"fl": [1280, 480], "aud": [3.1, 0.8], "gua": [3.0, "S"], "l0": 3.0, "l1": 4.0, "l2": 8.0, "nm": 16.0, "pc": 1, "pen": 0, "last": 128, "xs": [0, 1, 1], "mxl": [0, 1, 1]}
+ROUNDS = 270000
+CASES = [(1, 1, 1.05, 0.13, 1.0)]
+OPT = {"hop": 0.7, "seed": 1, "hot": 0.12, "wd": [0, 0, 0], "po": [0, 0, 0], "split": [1, 0, 0], "sil": [1, 1, 1, 0], "fl": [800, 480], "aud": [2.3, 0.7], "l0": 3.0, "l1": 3.5, "l2": 2.5, "nm": 7.0, "pc": 1, "pen": 1, "last": 128, "xs": [1, 1, 1], "mxl": [0, 1, 1]}
 
 
 def rank_program(g, core, T, topo):

@@ -3,20 +3,17 @@ import numpy as np
 from concourse.bass import DstId, RemoteDMATransfer
 from concourse.mybir import AluOpType as ALU, ActivationFunctionType as AF
 
-N = 4
+N, CORES = 4, 48
 F32, BF, I32, U16 = "float32", "bfloat16", "int32", "uint16"
-NB, E1, G1, E2A, G0, XA, ST = 0, 4112, 4368, 4768, 5024, 5424, 9776
-E2B = E2A + 8192
-G2 = E2B + 256
-NMW = G2 + 400
+NB, PCB, E1, G1, G0, G2, NMW = 0, 4112, 5136, 5392, 5920, 6448, 6976
 GB = [G0, G1, G2]
-RW, BW, IW, UW, WW = 6912, 5376, 768, 1024, 3840
+CW, RW, BW, IW, UW, WW = 3328, 5376, 6144, 640, 1024, 3584
 SCRATCH = {
     "au0": ("sbuf", [128, 4112], BF), "au1": ("sbuf", [128, 4112], BF), "au2": ("sbuf", [128, 4112], BF),
-    "xb": ("sbuf", [128, 384 + 4864], F32),
+    "xa": ("sbuf", [128, 4352], F32), "xb": ("sbuf", [128, 384 + 4864], F32),
     "da": ("sbuf", [128, 4352], F32), "db": ("sbuf", [128, 4352], F32),
     "fl": ("sbuf", [128, 4352], BF), "sg": ("sbuf", [128, 4096], BF),
-    "nm": ("sbuf", [128, NMW], F32), "zf": ("sbuf", [128, 256 + 4864], F32),
+    "nm": ("sbuf", [128, NMW], F32), "zf": ("sbuf", [128, 4656], F32), "cf": ("sbuf", [128, CW], F32),
     "rf": ("sbuf", [128, RW], F32), "rb": ("sbuf", [128, BW], BF), "ri": ("sbuf", [128, IW], I32),
     "wu": ("sbuf", [128, UW], U16), "wf": ("sbuf", [128, WW], F32),
     "spi": ("sbuf", [128, 256], I32), "gui": ("sbuf", [128, 256], I32), "lni": ("sbuf", [128, 256], I32),
@@ -24,19 +21,19 @@ SCRATCH = {
     "lin": ("dram", [8, 4128], F32),
 }
 for _k in range(8):
-    SCRATCH["p%d" % _k] = ("psum", [128, 32, 16] if _k == 2 else [128, 512], F32)
+    SCRATCH["p%d" % _k] = ("psum", [128, 512], F32)
 SEMAPHORES = (["cV", "cS", "cP", "cG"] + ["d%d" % k for k in range(20)] + ["lo%d" % k for k in range(12)]
-              + ["a1h0", "a1h1", "a1h2", "a1h3", "a2h0"] + ["rc%d" % t for t in range(3)] + ["rn%d" % t for t in range(3)])
+              + ["a1h0", "a1h1", "a1h2", "a1h3", "a2h0", "a2d"] + ["rc%d" % t for t in range(3)] + ["rn%d" % t for t in range(3)])
 
-CUTS = [[0, 512, 1280, 2048, 2816, 3584, 3840, 4096], list(range(0, 4097, 512)), list(range(0, 4097, 512))]
 CY = 0.00092
 HOP = 0.13
 BIG = float(1 << 23)
 HOLD = float(1 << 24)
 RND = float(3 << 22)
 C0 = 23.5 / 32
+TW, TC = 16384.0, 386.0
+A0 = 2 * TW + 512
 VIA = [0, 2]
-VG = [4, 4, 2]
 
 
 def ap(name, lo, hi, step=1, parts=None):
@@ -86,7 +83,29 @@ def helper(r, T, topo):
     return [c for c in topo.cores_of(src) if c not in T.cores and topo.die(c) != topo.die(src) and topo.may_write(c, dst)][0]
 
 
+def rounds(r, T, topo):
+    src, dst = T.cores[r % N], T.cores[(r - 2) % N]
+    chips = sorted(set(topo.chip(c) for c in range(CORES) if topo.chip(c) != topo.chip(src) and topo.same_plane(topo.chip(c), topo.chip(src))))[:2]
+    far = [[c for c in range(CORES) if topo.chip(c) == k and topo.die(c) == d and topo.may_write(c, dst)][0] for d, k in enumerate(chips)]
+    es, near = topo.engines(src, far[0]), helper(r - 1, T, topo)
+    return [(far[0], es[:len(es) // 2]), (far[1], es[len(es) // 2:]), (near, [e for e in topo.engines(src, near) if e not in es])]
+
+
 def hand_on(g, core, T, topo):
+    visit_1(g, core, T, topo)
+    for r in range(N):
+        if helper(r - 1, T, topo) is not None:
+            dst = T.cores[(r - 2) % N]
+            rid, pid, _se = topo.addr(dst)
+            for h, (c, es) in enumerate(rounds(r, T, topo)):
+                if c == core:
+                    g.wait_ge(T.sem.a2d, len(es))
+                    g.remote_dma(T.au2[:, 1024 * h:1024 * h + 1024], T.au2[:, 1024 * h:1024 * h + 1024], T.sem.a2h0, T.sem.lo1,
+                                 pid, rid, topo.mask(core, dst))
+                    g.wait_ge(T.sem.lo1, len(topo.engines(core, dst)))
+
+
+def visit_1(g, core, T, topo):
     for r in range(N):
         if helper(r, T, topo) == core:
             dst = T.cores[(r - 1) % N]
@@ -100,8 +119,8 @@ def hand_on(g, core, T, topo):
 
 
 def build(rank, core, T, topo):
-    ops = []
-    free = {"rf": 0, "rb": 0, "ri": 0, "wu": 0, "wf": 0, "nm": ST}
+    ops, step = [], ["first"]
+    free = {"rf": 0, "rb": 0, "ri": 0, "wu": 0, "wf": 0, "cf": 0}
 
     def R(a):
         if not isinstance(a, tuple):
@@ -117,7 +136,7 @@ def build(rank, core, T, topo):
     def new(buf, n):
         lo = free[buf]
         free[buf] = lo + (n + 15) // 16 * 16
-        assert free[buf] <= (E2B if buf == "nm" else SCRATCH[buf][1][1]), buf
+        assert free[buf] <= SCRATCH[buf][1][1], buf
         return ap(buf, lo, lo + n)
 
     def add(eng, emit, outs, ins, cost, lat=None, sem=None, cnt=0, after=()):
@@ -130,7 +149,7 @@ def build(rank, core, T, topo):
                 rd += regions(a[2])
             else:
                 wr += regions(a)
-        ops.append({"eng": eng, "emit": emit, "rd": rd, "wr": wr, "cost": cost, "lat": cost if lat is None else lat,
+        ops.append({"eng": eng, "step": step[0], "emit": emit, "rd": rd, "wr": wr, "cost": cost, "lat": cost if lat is None else lat,
                     "sem": sem, "cnt": cnt, "after": list(after),
                     "kind": "s" if any(a[0] == "ind" for a in outs) else "g" if any(isinstance(a, tuple) and a[0] == "ind" for a in ins) else ""})
         return len(ops) - 1
@@ -177,11 +196,15 @@ def build(rank, core, T, topo):
         add("V", lambda g: g.vector.memset(R(out), v), [out], [], vcost(out, [out]))
         return out
 
-    def act(out, a, func, bias=0.0, scale=1.0, total=None):
+    def act(out, a, func, bias=0.0, scale=1.0, total=None, on_v=False):
         out = room(out, a)
         c = max(count(a) * (1.56 if a[0] == "ind" else 1), 64) * CY + 0.05
         if total is None:
-            add("S", lambda g: g.scalar.activation(R(out), R(a), func, bias=R(bias), scale=R(scale)), [out], [a, bias, scale], c)
+            i = add("S", lambda g: g.scalar.activation(R(out), R(a), func, bias=R(bias), scale=R(scale)), [out], [a, bias, scale], c)
+            if func in (AF.Copy, AF.Identity) and not in_psum(a) and not in_psum(out):
+                ops[i]["alt"] = lambda g: g.vector.tensor_scalar(R(out), R(a), R(scale), R(bias), ALU.mult, ALU.add)
+                if on_v:
+                    ops[i].update({"eng": "V", "emit": ops[i]["alt"], "alt": ops[i]["emit"]})
         else:
             add("S", lambda g: g.scalar.activation(R(out), R(a), func, bias=R(bias), scale=R(scale), accum_out=R(total)),
                 [out, total], [a, bias, scale], c + 0.02)
@@ -190,10 +213,25 @@ def build(rank, core, T, topo):
     def lin_(out, a, scale, bias):
         return act(out, a, AF.Identity, bias, scale)
 
+    def take(out, a, on_v):
+        return act(out, a, AF.Copy, on_v=on_v)
+
     def mm(out, terms):
-        for k, (l, r) in enumerate(terms):
-            c = max(64, count(r)) * (4 if wide(r) else 1) * CY * 0.8
-            add("P", lambda g, l=l, r=r, k=k: g.tensor.matmul(R(out), R(l), R(r), k == 0, k == len(terms) - 1), [out], [l, r], c, c + 0.06)
+        for k, grp in enumerate(terms):
+            grp = grp if isinstance(grp, list) else [grp]
+            c = sum(max(64, count(e[1])) * (4 if wide(e[1]) else 1) * CY * OPT["pf"] for e in grp)
+
+            def emit(g, grp=grp, k=k):
+                for q, e in enumerate(grp):
+                    ins = g.tensor.matmul(R(e[2] if len(e) > 2 else out), R(e[0]), R(e[1]), k == 0 and q == 0,
+                                          k == len(terms) - 1 and q == len(grp) - 1)
+                return ins
+            add("P", emit, [out], [a for e in grp for a in e[:2]], c, c + 0.06)
+        return out
+
+    def keep(out, a, pat, op, other, base, cm, after=()):
+        out = room(out, a)
+        add("G", lambda g: g.affine_select(R(out), R(a), pat, op, other, base, cm), [out], [a], 0.17 + 2 * count(out) * CY, after=after)
         return out
 
     def iota(out, pat, base, cm, after=()):
@@ -202,6 +240,9 @@ def build(rank, core, T, topo):
         else:
             add("G", lambda g: g.iota(R(out), pat, base, cm, allow_small_or_imprecise_dtypes=True), [out], [], 0.13 + 2 * count(out) * CY, after=after)
         return out
+
+    def const(out, v, after=()):
+        return iota(out, [[0, count(out)]], v, 0, after)
 
     nd = [0]
 
@@ -270,91 +311,92 @@ def build(rank, core, T, topo):
         s = send([item], OPT["l0"], after=[] if s is None else [s])
         recv(a1, "a1h%d" % h, len(topo.engines(theirs if theirs is not None and h in VIA else nxt, core)), [s], OPT["l1"] + OPT["aud"][1] * (3 - h))
 
-    pi = iota(new("ri", 1), [[0, 1]], 0, 1)
-    JB = iota(new("nm", 128), [[1, 8], [0, 16]], 0, 0)
-    RB = iota(new("rb", 384), [[0, 24], [2048, 16]], 0, 0)
-    J = iota(new("nm", 128), [[1, 128]], 0, 0)
     s1 = s
-    JH, PCR, CROW = new("nm", 240), new("nm", 1024), new("rf", 256)
-    iota(ap("nm", XA + 4096, XA + 4352), [[0, 256]], 0, 0, [s])
-    iota(ap("xb", 4096, 4352), [[0, 256]], 0, 0, [s])
-    iota(ap("zf", 256, 640), [[0, 384]], 0, 0, [s])
+    late = [s1]
+    pi = iota(new("ri", 1), [[0, 1]], 0, 1)
+    pcol = iota(new("wf", 1), [[0, 1]], 0, 1)
+    JB = iota(new("cf", 128), [[16, 8], [0, 16]], 0, 0)
+    RB = iota(new("rb", 384), [[0, 24], [2048, 16]], 0, 0)
+    J = iota(new("cf", 128), [[1, 128]], 0, 0)
+    JH, PCR, CROW = new("cf", 128), new("cf", 1040), new("rf", 256)
+    const(ap("xa", 4096, 4352), 0, late)
+    const(ap("xb", 4096, 4352), 0, late)
     J16, J128 = sub(J, 0, 16), sub(J, 0, 128)
     FL = ap("fl", 0, 4352)
     ZERO = ms(new("rb", 256), 0.0)
-    pcol = cp("wf", pi)
     B8 = sub(new("rf", 128), 0, 128, 1, (0, 8))
-    ts(B8, sub(JB, 0, 128, 1, (0, 8)), sub(pcol, 0, 1, 1, (0, 8)), ALU.is_equal)
-    ii = ts("ri", pi, 15, ALU.bitwise_and)
-    gi = ts("ri", pi, 4, ALU.arith_shift_right)
-    icol, gcol = cp("wf", ii), cp("wf", gi)
-    i2k = ts("wf", ii, 2048.0, ALU.mult)
-    AM = ts("rb", RB, i2k, ALU.is_equal, BIG, ALU.mult)
+    ts(B8, sub(JB, 0, 128, 1, (0, 8)), 1.0 / 16, ALU.mult, sub(pcol, 0, 1, 1, (0, 8)), ALU.is_equal)
+    icol = cp("wf", ts("ri", pi, 15, ALU.bitwise_and))
+    g16 = tt("wf", pcol, icol, ALU.subtract)
+    AM = ts("rb", RB, lin_("wf", icol, 2048.0, 0.0), ALU.is_equal, BIG, ALU.mult)
     JJ = lin_("wf", sub(J, 0, 24), 16.0, icol)
     C16 = sub(JJ, 0, 16)
     DUM = lin_("wf", C16, 1.0, 4096.0)
     fs, fg = OPT["fl"]
-    ms(sub(FL, 0, fs), 1.0)
-    act(sub(FL, fs, 2 * fs), sub(FL, 0, fs), AF.Copy)
-    iota(sub(FL, 2 * fs, 2 * fs + fg), [[0, fg]], 1, 0)
-    fm = (2 * fs + fg + 4352) // 2
-    ms(sub(FL, 2 * fs + fg, fm), 1.0)
-    ms(sub(FL, fm, 4352), 1.0)
-    IF = ts("nm", J128, pcol, ALU.is_equal)
-    BO = ts("nm", JB, gcol, ALU.is_equal)
-    BOS = lin_("nm", BO, 1.0 / BIG, 0.0)
-    BOP = lin_("rb", BO, 0.25, 0.0)
-    BON = lin_("rb", BO, -0.25, 0.0)
-    NBO = lin_("nm", BO, -1.0, 0.0)
-    UI, US = new("nm", 128), new("nm", 128)
-    add("G", lambda g: g.affine_select(R(UI), R(NBO), [[-1, 128]], ALU.is_ge, 0.0, 0, 1), [UI], [NBO], 0.44, after=[s])
-    add("G", lambda g: g.affine_select(R(US), R(NBO), [[-1, 128]], ALU.is_gt, 0.0, 0, 1), [US], [NBO], 0.44, after=[s])
+    ms(sub(FL, 0, max(fs, 512)), 1.0)
+    fm = max(fs, 512)
+    if fs:
+        act(sub(FL, fm, fm + fs), sub(FL, 0, fs), AF.Copy)
+    if fg:
+        const(sub(FL, fm + fs, fm + fs + fg), 1)
+    fm += fs + fg
+    for a in range(fm, 4096, 1216):
+        ms(sub(FL, a, min(a + 1216, 4096)), 1.0)
+    IF = ts("cf", J128, pcol, ALU.is_equal)
+    BO = ts("cf", JB, g16, ALU.is_equal)
+    BOP = lin_("rb", BO, 0.5, 0.0)
+    BON = lin_("rb", BO, -0.5, 0.0)
+    NIF = keep("cf", IF, [[-1, 128]], ALU.not_equal, -1.0, 0, 1, late)
+    LS = keep("cf", BO, [[1, 128]], ALU.is_gt, 0.0, 0, -1, late)
+    LI = keep("cf", BO, [[1, 128]], ALU.is_ge, 0.0, 0, -1, late)
     i15 = act("wf", icol, AF.Relu, -14.0)
-    S15 = lin_("nm", BO, i15, 0.0)
-    Z = iota(new("rb", 144), [[0, 144]], 0, 0)
-    ts(sub(Z, 15, 143, 16), sub(J, 0, 8), gcol, ALU.is_equal, 1.0 / 32, ALU.mult)
+    hc = lin_("wf", i15, -HOLD, HOLD)
+    Z = const(new("rb", 144), 0)
+    ts(sub(Z, 15, 143, 16), sub(JB, 0, 128, 16), g16, ALU.is_equal, 1.0 / 32, ALU.mult)
     SEL = [sub(Z, 15 - a, 143 - a) for a in range(16)]
+    Z2 = lin_("rb", Z, -2.0, 0.0) if OPT["two"] else None
     ni8k = lin_("wf", icol, -8192.0, 0.0)
     i256 = lin_("wf", icol, -256.0, -127.5)
     i256p = lin_("wf", icol, -256.0, -255.5)
-    POS8 = new("nm", 256)
-    PT = lin_("wf", ts("wf", J16, icol, ALU.is_le), -2 * BIG - 8192.0, 8192.0)
+    PT = new("wf", 32)
+    lin_(sub(PT, 0, 32, 2), ts("wf", J16, icol, ALU.is_le), -2 * BIG - 8192.0, 8192.0)
+    const(sub(PT, 1, 32, 2), 8192, late)
     JO = cp("wu", J16)
-    JV = lin_("wf", C16, 16.0, 16.0)
-    CE = new("wf", 32)
-    lin_(sub(CE, 0, 16), C16, 1.0, float(E2A - G2))
-    CM = lin_(sub(CE, 16, 32), C16, 1.0, float(E2B - G2))
-    C272 = tt("wf", lin_("wf", C16, 1.0, 272.0), act("wf", C16, AF.Sign, 255.0, -1.0), ALU.mult)
-    DUM2 = lin_("wf", C16, 1.0, 4352.0)
-    I16 = lin_("rb", IF, 1.0 / 16, 0.0)
-    C16K = lin_("wf", C16, 16384.0, 5632.0)
-    RST = iota(new("wf", 32), [[0, 32]], 1, 0, [s])
-    iota(sub(RST, 16, 17), [[0, 1]], 0, 0, [s])
-    T2B = new("wf", 32)
-    lin_(sub(T2B, 16, 32), J16, 0.0, 0.0)
+    JV = lin_("wf", C16, 16.0, lin_("wf", hc, -1.0, 18.0))
+    CM = lin_("wf", C16, 1.0, float(E1 - G1))
+    C272 = lin_("wf", C16, 1.0, 272.0)
+    lin_(sub(C272, 15, 16), i15, -527.0, sub(C272, 15, 16))
+    I4 = lin_("rb", IF, 0.25, 0.0)
+    RST = const(new("wf", 16), 1, late)
+    const(sub(RST, 0, 1), 0, late)
+    ZP = const(new("wf", 16), 0, late)
+    x0 = new("wf", 16)
+    C2 = new("rb", 32)
+    lin_(sub(C2, 0, 16), C16, 2.0, 0.0)
+    lin_(sub(C2, 16, 32), C16, 2.0, 2.0)
+    x1 = new("rb", 16)
+    HBO = lin_("cf", BO, -0.5, 0.0)
+    HLS = keep("rb", BON, [[1, 128]], ALU.is_gt, 0.0, 0, -1, late)
+    HLI = keep("rb", BON, [[1, 128]], ALU.is_ge, 0.0, 0, -1, late)
     AH = new("rb", 384)
-    AH16 = tt(sub(AH, 0, 16), ts("wf", J16, icol, ALU.not_equal), ts("wf", J16, lin_("wf", icol, 1.0, 1.0), ALU.is_equal, HOLD - 1, ALU.mult), ALU.add)
+    tt(sub(AH, 0, 16), lin_("rb", sub(AM, 16, 32), 4.0, 0.0), lin_("rb", sub(AM, 15, 31), 2.0, 0.0), ALU.subtract)
     for lo, k in ((16, 3), (64, 5)):
         dma([(lambda a=a, lo=lo: R(sub(AH, a, a + lo)), lambda lo=lo: R(sub(AH, 0, lo))) for a in range(lo, lo + k * lo, lo)],
             [sub(AH, lo, lo + k * lo)], [sub(AH, 0, lo)], 4.0)
-    inv = lin_("wf", i15, 1.0 - 1.0 / HOLD, 1.0 / HOLD)
     for k in range(3):
         if k:
-            lin_(ap(au[k], 4096, 4104), sub(J, 0, 8), 0.0, float(1 << 21))
+            const(ap(au[k], 4096, 4104), 1 << 21, late)
         if k == 2:
             Z8 = act(ap(au[k], 4104, 4112), sub(JB, 0, 8), AF.Silu, 0.0, 0.0)
             ops[-1]["cost"] = ops[-1]["lat"] = 1.4
-        lin_(ap("nm", GB[k] + 384, GB[k] + 400), J16, 0.0, 4097.0)
-    END, WX, CODE, NC = new("rf", 257), new("rf", 257), new("rf", 257), new("rf", 257)
-    T1, T2 = new("rb", 272), new("rb", 272)
-    lin_(sub(END, 0, 544, 272), sub(J, 0, 2), 0.0, 0.0)
-    lin_(sub(CODE, 0, 544, 272), sub(J, 0, 2), 0.0, 8192001.0)
-    lin_(sub(T1, 0, 16), J16, 0.0, 0.0)
-    ZP = sub(T2B, 16, 32)
+        none = GB[k] + (384 if k == 2 and OPT["moved"] else 512)
+        const(ap("nm", none, none + 16), 4096, late)
+    END, CODE, NC, HD = new("rf", 257), new("rf", 257), new("rf", 257), new("rf", 257)
+    WX, T1, T2 = new("rb", 272), new("rb", 272), new("rb", 272)
+    lin_(sub(END, 0, 1), icol, 0.0, 0.0)
+    const(sub(WX, 0, 288, 287), 0, late)
+    const(sub(NC, 0, 1), 8192001, late)
     pc, pd, pv, pw, pe, pq, pa, pb = [ap("p%d" % k, 0, 512) for k in range(8)]
-
-    def blk(a, b, step=1):
-        return raw("p2", 16 * a, 16 * b, lambda t: t[:, a:b:step, :], 16 * len(range(a, b, step)))
 
     def wrap(out, row):
         n = count(row)
@@ -363,19 +405,18 @@ def build(rank, core, T, topo):
 
     def hold(out, row):
         n = count(row)
-        scan(sub(out, 0, n), sub(AH, 0, n), row, 0.0, ALU.mult, ALU.max)
+        scan(sub(out, 0, n), sub(AH, 0, n), row, 0.0, ALU.add, ALU.min)
         return sub(out, 15, n, 16)
 
-    def unwrap(out, w, mx, ps):
-        tt(mx, ind(w, JO), sub(AM, 0, 256), ALU.mult)
-        mm(ps, [(BOS, mx)])
-        return act(out, ps, AF.Copy)
+    def unwrap(out, w, mx, ps, plus=0.0):
+        for a in range(0, 256, OPT["half"]):
+            b = a + OPT["half"]
+            mm(sub(ps, a, b), [(BO, tt(sub(mx, a, b), ind(w, sub(JO, a // 16, b // 16)), sub(AM, a, b), ALU.mult))])
+        return lin_(out, ps, 1.0 / BIG, plus)
 
     def strew(w, row, t):
-        if OPT["sil"][t]:
-            add("S", lambda g: g.scalar.activation(R(w), R(row), AF.Silu), [w], [row, Z8], 0.97)
-        else:
-            cp(w, row)
+        i = add("S", lambda g: g.scalar.activation(R(w), R(row), AF.Silu), [w], [row, Z8], 0.97)
+        ops[i]["alt"] = lambda g: g.vector.tensor_copy(R(w), R(row))
 
     def fill(w, n, offs, t):
         strew(ind(w, offs), CROW, t)
@@ -389,294 +430,374 @@ def build(rank, core, T, topo):
     lnf = cp(sub(new("rf", 256), 0, 256, 1, (0, 8)), lni)
     pn = mm(sub(pa, 0, 256), [(B8, lnf)])
     scan(sub(END, 1, 257), pn, ZERO, 0.0, ALU.add, ALU.add)
-    W0 = new("nm", 512)
+    W0 = new("cf", 512)
     endw = wrap(sub(W0, 0, 256), sub(END, 1, 257))
     begw = wrap(sub(W0, 256, 512), sub(END, 0, 256))
     cum0 = sub(W0, 15, 512, 16)
-    WA, WB, WC, WD = new("rf", 384), new("rf", 384), new("rf", 256), new("rf", 256)
-    SO = cp("wu", tt("wf", tt("wf", tt("wf", endw, begw, ALU.is_equal), DUM, ALU.mult), begw, ALU.max))
-    NG = ts(ap("da", 4096, 4352), gui, -1.0, ALU.mult)
+    WA, WB, WC, WD = new("rf", 384), new("rf", 256), new("rf", 256), new("rf", 256)
+    first = tt("wf", tt("wf", tt("wf", endw, begw, ALU.is_equal), DUM, ALU.mult), begw, ALU.max)
+    SO = cp("wu", first)
+    NG = cp(ap("db", 4096, 4352), gui)
     cp(ind(FL, SO), ZERO)
-    UO = cp("wu", ts("ri", cp("ri", endw), 255, ALU.bitwise_and))
+    ci = cp("ri", cum0)
+    UO = {e: cp("wu", ts("ri", sub(ci, 0, 16), 255, ALU.bitwise_and, e - 1, ALU.arith_shift_right)) for e in sorted(set(OPT["every"]))}
     LT = act("rb", END, AF.Sign, i256p)
-    EQ = ts("rb", act("rf", sub(END, 1, 257), AF.Abs, i256), 128.0, ALU.is_lt, 2.0, ALU.mult)
+    EQ = ts("rb", act(WD, sub(END, 1, 257), AF.Abs, i256), 128.0, ALU.is_lt, 2.0, ALU.mult)
     nw0 = tt("wf", endw, begw, ALU.subtract)
-    beg16 = lin_("wf", begw, 1.0, 16.0)
-    begO = lin_("wf", begw, 1.0, 16896.0)
-    DUMO = lin_("wf", C16, 1.0, 4096.0 + 16897.0)
+    beg32 = lin_("wf", begw, 2.0, 32.0)
+    begO = lin_("wf", begw, 1.0, A0)
+    DUMO = lin_("wf", C16, 1.0, 4096.0 + A0 + 1)
     SG1, SGN = new("rb", 256), new("rb", 256)
-    act(SG1, NG, AF.Sign, 0.5)
-    zw = ts("wf", mm(sub(pe, 0, 16), pick(SG1)), -1.0 / 32, ALU.is_lt)
-    stat = tt("wf", lin_("wf", nw0, -0.5, ni8k), zw, ALU.subtract)
-    if not all(OPT["wd"][1:]):
-        stat1 = lin_("wf", stat, 1.0, -C0)
-    if any(OPT["wd"]):
-        stat2 = lin_("wf", stat, 1.0, lin_("wf", icol, 8192.0, -C0))
-        ZU, ZD = lin_("rb", Z, 8.0, 0.0), lin_("rb", Z, -8.0, 0.0)
-    dma([(lambda: T.db[:, 4096:4352], lambda: R(NG))], [ap("db", 4096, 4352)], [NG], 4.0)
+    act(SG1, NG, AF.Sign, 0.5, -1.0)
+    zw = ts("wf", mm(sub(pe, 0, 16), [pick(SG1)]), -1.0 / 32, ALU.is_lt)
+    if 2 in OPT["every"]:
+        stat1 = tt("wf", first, tt("wf", zw, nw0, ALU.min), ALU.subtract)
+        stat = lin_("wf", stat1, 1.0, -15.0 / 32) if OPT["every"][0] == 2 else None
+        halves = ts("ri", ci, 1, ALU.arith_shift_right)
+        half = lin_("wf", tt("wf", sub(halves, 0, 16), sub(halves, 16, 32), ALU.add), 1.0, lin_("wf", icol, -16384.0, 0.0))
+        last = tt("wf", lin_("wf", endw, 1.0, -1.0), first, ALU.max)
+    if 1 in OPT["every"]:
+        HIF = lin_("cf", IF, -0.5, 0.0)
+        whole = tt("wf", lin_("wf", nw0, -0.5, lin_("wf", icol, 8192.0, 0.0)), zw, ALU.subtract)
+    if OPT["every"][0] == 2:
+        dma([(lambda: T.da[:, 4096:4352], lambda: R(NG))], [ap("da", 4096, 4352)], [NG], 4.0)
 
-    SPF = ts("rf", spi, 1.0, ALU.add)
+    SPF = cp(WB, spi)
     for h in range(2):
         o = sub(pb, 128 * h, 128 * h + 128)
         i_ = sub(SPF, h, 256, 2)
         add("P", lambda g, o=o, i_=i_: g.tensor.transpose(R(o), R(i_), R(IF)), [o], [i_, IF], 0.45, 0.5)
         act(raw("st3", 0, 256, lambda t, h=h: t[:, :, h, :], 128), o, AF.Copy)
+    WIN = ap("zf", 544, 4656)
     lin = ap("lin", 0, 4128)
     zp8 = sub(ZP, 0, 16, 1, (0, 8))
     pairs = [(lambda g_=g_: T.lin[g_, 16:4112], lambda g_=g_: T.st3[:, g_, :, :]) for g_ in range(8)]
-    pairs += [(lambda: T.lin[:, 0:16], lambda: R(zp8)), (lambda: T.lin[:, 4112:4128], lambda: R(zp8))]
-    s = dma(pairs, [lin], [ap("st3", 0, 256), zp8], 4.0)
-    dma([(lambda i=i: T.nm[i:128:16, NB:NB + 4112], lambda: T.lin[:, 16:4128]) for i in range(8)], [ap("nm", NB, NB + 4112, 2)], [lin], OPT["nm"])
-    far2, got, turn = C[(rank - 2) % N], ap("au1", 0, 4096), ap("cs", 1, 2)
-    lo = 0 if relayed(rank - 1) else 2048
-    out = [send([(ap("au1", lo, 4096), ap("au2", lo, 4096), prv, topo.engines(core, prv), "a2h0")], 4.5, [turn, got])]
+    dma(pairs + [(lambda a=a: T.lin[:, a:a + 16], lambda: R(zp8)) for a in (0, 4112)], [lin], [ap("st3", 0, 256), zp8], 4.0)
+    got, turn = ap("au1", 0, 4096), ap("cs", 1, 2)
+    lo, ways = 0 if relayed(rank - 1) else 3072, []
     if not relayed(rank - 2):
-        out.append(send([(ap("au0", 0, 2048), ap("au2", 0, 2048), far2, topo.engines(core, far2), "a2h0")], 4.5, [turn, got]))
-        ops[out[1]]["more"] = True
-    dma([(lambda i=i: T.nm[i:128:16, NB:NB + 4112], lambda: T.lin[:, 16:4128]) for i in range(8, 16)], [ap("nm", NB + 1, NB + 4112, 2), turn], [lin], OPT["nm"])
-    recv(ap("au2", 0, 4096), "a2h0", len(topo.engines(nxt, core)) + (0 if relayed(rank) else len(topo.engines(C[(rank + 2) % N], core))),
-         out, OPT["l2"])
+        by = rounds(rank, T, topo)
+        ways = [send([(ap("au0", 1024 * h, 1024 * h + 1024), ap("au2", 1024 * h, 1024 * h + 1024), c, es, "a2d") for h, (c, es) in enumerate(by)],
+                     10.7, after=[s1])]
+        ops[ways[0]]["more"] = True
+    early = OPT["early"]
+    if early:
+        dma([(lambda i=i: T.nm[i:128:16, NB:NB + 4112], lambda: T.lin[:, 16:4128]) for i in range(early)], [ap("nm", NB, NB + 4112, 2)], [lin], OPT["nm"])
+    out = [send([(ap("au1", lo, 4096), ap("au2", lo, 4096), prv, topo.engines(core, prv), "a2h0")], 4.5, [turn, got])]
+    dma([(lambda i=i: T.nm[i:128:16, NB:NB + 4112], lambda: T.lin[:, 16:4128]) for i in range(early, 16)], [ap("nm", NB + 1, NB + 4112, 2) if early else ap("nm", NB, NB + 4112), turn], [lin], OPT["nm"])
+    recv(ap("au2", 0, 4096), "a2h0", sum(len(topo.engines(c, core)) for c in [nxt] + [c for c, _es in ([] if relayed(rank) else rounds(rank + 2, T, topo))]),
+         out + ways, OPT["l2"])
     out = [s1] + out
-    iota(JH, [[1, 240]], 128, 0, out[:1])
-    lin_(POS8, sub(J, 0, 256), -131072.0, ni8k)
-    iota(CROW, [[16, 256]], 16, 0, out[:1])
-    iota(ap("zf", 0, 256), [[0, 256]], 0, 0, out)
-    iota(PCR, [[8192, 1024]], 8192, 0, out)
-    WIN = ap("zf", 544, 4656)
-    assert free["nm"] == E2B
+    iota(JH, [[1, 128]], 128, 0, out)
+    iota(CROW, [[16, 256]], 16, 0, out)
+    const(ap("zf", 0, 256), 0, out)
+    for h in range(2):
+        const(ap("nm", PCB + 512 * h, PCB + 512 * h + 512), 0, out)
+        iota(sub(PCR, 520 * h, 520 * h + 520), [[8192, 520]], 8192 * 520 * h - 4096, 0, out)
+    S15 = keep("cf", BO, [[-16, 8], [0, 16]], ALU.is_equal, 0.0, -15, 1, out)
+    BB = const(new("rb", 128), -1, out)
+    keep(BB, BB, [[-16, 8], [0, 16]], ALU.is_ge, 0.0, 0, 1, out)
+    keep(BB, BB, [[16, 8], [0, 16]], ALU.is_ge, 0.0, 15, -1, out)
+    DM = keep("rb", BB, [[1, 128]], ALU.is_equal, 0.0, -1, -1, out)
+    keep(DM, DM, [[-1, 128]], ALU.not_equal, 1.0, 0, 1, out)
+    IB = keep("rb", DM, [[-1, 128]], ALU.is_equal, 0.0, 0, 1, out)
+    S0 = keep("rb", BB, [[-1, 128]], ALU.is_equal, 0.0, -15, 1, out)
+    CG = new("rb", 48)
+    const(sub(CG, 0, 16), 0, out)
+    const(sub(HD, 0, 1), 8400000, out)
+    M256 = const(new("rb", 1), -1024, out)
+    PC = ap("nm", PCB, PCB + 1024)
 
     XS, SG2 = new("rf", 256), new("rb", 256)
     FIL, BKG, MX, NA, NB2, BKR = [new("rf", n) for n in (256, 384, 256, 256, 256, 256)]
     FIB, WAB = new("rb", 384), new("rb", 384)
     SND = new("rf", 384)
     ZF = ap("zf", 0, 528)
-    st = {"cum": cum0, "k": nw0, "l": nw0}
+    st = {"cum": cum0, "cw": endw, "dw": begw, "k": nw0, "l": nw0}
+
+    def total(ps, plus, minus, on_pe):
+        if on_pe:
+            return mm(ps, [(IF, a) for a in plus] + [(NIF, a) for a in minus])
+        a = plus[0]
+        for b, op in [(b, ALU.add) for b in plus[1:]] + [(b, ALU.subtract) for b in minus]:
+            a = tt("wf", a, b, op)
+        return a
 
     def heavy(t):
-        x = [ap("nm", XA, XA + 4352), ap("xb", 0, 4352)][t % 2]
+        xs = ap(["xa", "xb"][t % 2], 0, 4352)
         d = ap(["da", "db"][t % 2], 0, 4352)
         tab = ap(au[t], 0, 4096)
-        w = 2 if t == 0 else 1
-        for k in range(0, 8, w):
-            o, src = sub(x, 512 * k, 512 * (k + w)), ind(tab, sub(SPU, 32 * k, 32 * (k + w)))
-            if k >= 8 - VG[t]:
-                cp(o, src)
-            else:
-                act(o, src, AF.Copy)
-        act(XS, ind(x, SO), AF.Copy)
-        tt(ind(x, SO), XS, NG, ALU.add)
-        terms = []
-        for lo, hi in zip(CUTS[t][:-1], CUTS[t][1:]):
-            scan(sub(d, lo, hi), ap("fl", lo, hi), sub(x, lo, hi), 0.0 if lo == 0 else sub(d, lo - 1, lo), ALU.mult, ALU.add)
-            act(ap("sg", lo, hi), sub(d, lo, hi), AF.Sign, 0.5)
-            terms += [(SEL[a], ap("sg", 256 * a, 256 * a + 256)) for a in range(lo // 256, hi // 256)]
-        mm(sub(pc, 0, 256), terms)
-        act(SG2, sub(pc, 0, 256), AF.Sign, 1.0 / 32)
-        scan(sub(WX, 1, 257), SG2, ZERO, 0.0, ALU.add, ALU.add)
-        tt(sub(T1, 16, 272), ind(WX, UO), EQ, ALU.mult)
-        lin_(sub(T2, 15, 272), LT, sub(WX, 256, 257), 0.0)
-        if OPT["wd"][t]:
-            return mm(sub(pd, 0, 16), [(IF, stat2)] + [(sub(z, 15 - a, 143 - a), sub(row, o + a, o + 256, 16))
-                                                       for row in (T2, T1) for z, o in ((ZU, 16), (ZD, 15)) for a in range(16)] + [(IF, st["l"])])
-        mm(sub(pd, 0, 256), [(BOP, sub(RB, 0, 256)), (BOP, sub(T2, 16, 272)), (BON, sub(T2, 15, 271)), (BOP, sub(T1, 16, 272)), (BON, sub(T1, 15, 271))])
-        return tt("wf", wrap(WC, sub(pd, 0, 256)), tt("wf", stat1 if t else stat, st["l"], ALU.add), ALU.add)
+        step[0] = "gather%d" % t
+        for lo, hi, on_v in OPT["vg"][t]:
+            act(sub(xs, 256 * lo, 256 * hi), ind(tab, sub(SPU, 16 * lo, 16 * hi)), AF.Identity, 0.0, -1.0, on_v=on_v)
+        act(XS, ind(xs, SO), AF.Copy)
+        tt(ind(xs, SO), XS, NG, ALU.add)
+        terms, cuts, done, e = [], OPT["cuts"][t], 0, OPT["every"][t]
+        n = 256 // e
+        for lo, hi in zip(cuts[:-1], cuts[1:]):
+            step[0] = "sums%d" % t
+            if t == 0 and hi == 4096 and OPT["two"]:
+                scan(ap("sg", lo, hi), ap("fl", lo, hi), sub(xs, lo, hi), sub(d, lo - 1, lo), ALU.mult, ALU.add)
+                for a, b in zip(OPT["two"][:-1], OPT["two"][1:]):
+                    ts(ap("sg", a, b), ap("sg", a, b), 0.5, ALU.is_gt, 0.5, ALU.subtract)
+                    terms.append([(sub(Z2, 15 - q, 143 - q), ap("sg", 256 * q, 256 * q + 256)) for q in range(a // 256, b // 256)])
+                continue
+            scan(sub(d, lo, hi), ap("fl", lo, hi), sub(xs, lo, hi), 0.0 if lo == 0 else sub(d, lo - 1, lo), ALU.mult, ALU.add)
+            if hi in OPT["sgn"][t]:
+                step[0] = "signs%d" % t
+                on_v = hi in OPT["vs"][t]
+                if on_v:
+                    ts(ap("sg", done // e, hi // e), sub(d, done + e - 1, hi, e), 0.5, ALU.is_gt, 0.5, ALU.subtract)
+                else:
+                    act(ap("sg", done // e, hi // e), sub(d, done + e - 1, hi, e), AF.Sign, 0.5, -1.0)
+                terms.append([(sub(Z2 if on_v else Z, 15 - a, 143 - a), ap("sg", n * a, n * a + n)) for a in range(done // 256, hi // 256)])
+                done = hi
+        step[0] = "count%d" % t
+        mm(sub(pc, 0, n), terms)
+        tot = new("wf", 1)
+        act(sub(SG2, 0, n), sub(pc, 0, n), AF.Sign, 1.0 / 32, 1.0, tot)
+        scan(sub(WX, 1, n + 1), sub(SG2, 0, n), sub(ZERO, 0, n), 0.0, ALU.add, ALU.add)
+        tt(sub(T1, 16, 272), ind(sub(WX, 0, n + 1), UO[e]), EQ, ALU.mult)
+        lin_(sub(T2, 15, 272), LT, tot, 0.0)
+        mm(sub(pd, 0, 256), [(BOP, sub(RB, 0, 256)), [(BON, sub(T2, 16, 272)), (BOP, sub(T2, 15, 271))], [(BON, sub(T1, 16, 272)), (BOP, sub(T1, 15, 271))]])
+        if e == 1:
+            return mm(sub(pd, 256, 272) if t else sub(pq, 0, 16), [[(IF, whole), (IF, st["l"])], (HIF, wrap(WC, sub(pd, 0, 256)))])
+        q = tt("wf", tt("wf", tt("wf", wrap(WC, sub(pd, 0, 256)), half, ALU.add), last, ALU.min), first, ALU.max)
+        act(SG2, ind(d, cp("wu", q)), AF.Sign, 0.5, -1.0)
+        if t == 0:
+            return mm(sub(pq, 0, 16), [[(IF, stat), (IF, nw0)], (NIF, q), pick(SG2)])
+        under = ts("wf", mm(sub(pe, 32, 48), [pick(SG2)]), -1.0 / 32, ALU.is_lt)
+        return mm(sub(pd, 256, 272), [[(IF, stat1), (IF, st["l"])], (NIF, q), (NIF, under)])
 
     def light(t, d):
         Gt = GB[t]
         cum, k = st["cum"], st["k"]
-        x = new("wf", 32)
-        x0, x1 = sub(x, 0, 16), sub(x, 16, 32)
+        m0, step[0] = 0.0, "released%d" % t
+        if t == 0 and OPT["every"][0] == 2:
+            d, m0 = lin_("wf", d, 1.0, RND), RND
+        tab, dt = ap(au[t], 0, 4112 if t == 2 else 4104), ap(["da", "db"][t % 2], 0, 4352)
         if t:
-            tab = ap(au[t], 0, 4112 if t == 2 else 4104)
-            terms = [(IF, tt("wf", d, st["mq"], ALU.max))]
-            dk = ind(ap(["da", "db"][t % 2], 0, 4352), st["VU"])
-            if t == 2:
-                u = tt(NB2, ind(tab, st["OZ"]), act(NA, dk, AF.Copy), ALU.add)
-                act(SG1, u, AF.Sign, 0.5)
-                terms.append((IF, ts("wf", mm(sub(pe, 16, 32), pick(SG1)), -1.0 / 32, ALU.is_lt, -1.0, ALU.mult)))
-                na = lin_(NA, u, -1.0, 0.0)
-            else:
-                na = lin_(NA, dk, -1.0, 0.0)
-            tt(SGN, ind(tab, st["EW"]), na, ALU.is_ge)
-            v = mm(sub(pq, 0, 16), pick(SGN) + terms[::-1] if OPT["mxl"][t] else terms + pick(SGN))
-        e8 = sub(T2B, 0, 16)
-        if OPT["xs"][t]:
-            m0 = RND if t else 0.0
-            if t:
-                d = lin_("wf", v, 1.0, RND)
-            rs = new("wf", 2)
-            act(x0, d, AF.Relu, -m0, 1.0, sub(rs, 0, 1))
-            act(x1, d, AF.Relu, m0, -1.0, sub(rs, 1, 2))
-            act(e8, d, AF.Relu, 8192.0 * (m0 + 1), -8192.0)
+            d = tt("wf", d, st["mq"], ALU.max)
+        if t == 2:
+            tt(SG1, ind(tab, st["EW0"]), act(NB2, ind(dt, st["VU0"]), AF.Copy), ALU.is_ge)
+            under = ts("wf", mm(sub(pe, 16, 32), [pick(SG1)]), 7.5 / 32, ALU.is_lt)
+            d = tt("wf", d, tt("wf", under, st["both"], ALU.min), ALU.subtract)
+        rs = new("wf", 2)
+        act(x0, d, AF.Relu, -m0, 1.0, sub(rs, 0, 1))
+        e8 = act("rb", d, AF.Relu, 32768.0 * (m0 + 1), -32768.0)
+        sc = scan("wf", sub(x0, -1, 15), RST, 0.0, ALU.add, ALU.mult)
+        ex = mm(sub(pb, 0, 16), [(LS, x0), (I4, e8), (BO, sc)])
+        mm(sub(pw, 0, 1), [(BO, sub(rs, 0, 1))])
+        less = "t" in OPT["pe"][t]
+        mm(sub(pv, 0, 16), [(LI, x0)] + [(NIF, st["cw"])] * less + [(BO, sc)])
+        mm(sub(pv, 16, 32), [(LS, x0)] + [(NIF, st["dw"])] * less + [(BO, sc)])
+        moved = t == 2 and OPT["moved"]
+        if moved:
+            mm(sub(pw, 2, 3), [(BO, sub(rs, 0, 1)), (I4, M256)])
+            OU = tt("wf", ex, lin_("wf", C16, 1.0, 4352.0), ALU.min)
         else:
-            if t:
-                d = cp("ri", v)
-            ts(x1, v if t else d, -0.5, ALU.is_lt)
-            ts(e8, v if t else d, 0.5, ALU.is_lt, 8192.0, ALU.mult)
-            ts(x0, d, 0.0, ALU.max)
-        sc = scan("wf", RST, x, 0.0, ALU.mult, ALU.add)
-        mm(sub(pw, 0, 2), [(BO, rs if OPT["xs"][t] else sub(sc, 15, 32, 16))])
-        ex = mm(sub(pb, 0, 32), [(UI, x), (IF, T2B), (BO, sc)])
-        mm(blk(0, 2), [(US, x), (BO, sc)])
-        mm(blk(2, 4), [(UI, x), (BO, sc)])
-        mn = ts("wf", sub(pw, 0, 1), sub(pw, 1, 2), ALU.min, -256.0, ALU.add)
+            OU = cp("wu", tt("wf", ex, DUM, ALU.min))
+        step[0] = "short%d" % t
+        if t:
+            dk = ind(dt, st["VU"])
+            if t == 2:
+                na = tt(NB2, dk, act(NA, ind(tab, st["OZ"]), AF.Copy), ALU.subtract)
+            else:
+                na = act(NA, dk, AF.Copy)
+            tt(SGN, ind(tab, st["EW"]), na, ALU.is_ge)
+            terms = [(IF, d), pick(SGN)]
+            act(x1, mm(sub(pq, 0, 16), terms[::OPT["mxl"][t]]), AF.Sign, 0.5 - C0, 1.0, sub(rs, 1, 2))
+        else:
+            act(x1, sub(pq, 0, 16), AF.Sign, 0.5, 1.0, sub(rs, 1, 2))
+        mm(sub(pw, 1, 2), [(HBO, sub(rs, 1, 2))])
+        s1 = scan("rb", sub(x1, -1, 15), RST, 0.0, ALU.add, ALU.mult)
+        sh = sub(pq, 32, 64)
+        mm(sub(sh, 0, 16), [[(I4, sub(C2, 16, 32)), (HLI, x1)], (BON, s1)])
+        mm(sub(sh, 16, 32), [[(I4, sub(C2, 0, 16)), (HLS, x1)], (BON, s1)])
+        by = 256.0 if moved else 0.0
+        mn = ts("wf", sub(pw, 1, 2), 128.0 - by, ALU.add, sub(pw, 2, 3) if moved else sub(pw, 0, 1), ALU.min)
         cs, cn = ap("cs", 4 * t, 4 * t + 1), ap("cn", 4 * t, 4 * t + 1)
-        OU = ts("wu", tt("wf", sub(ex, 0, 16), DUM2, ALU.min), mn, ALU.subtract)
-        ts(cs, sub(pw, 0, 1), mn, ALU.subtract, 384.0, ALU.min)
+        ts(cs, sub(pw, 0, 1), mn, ALU.subtract, 128.0 + by, ALU.min)
         s = send([(cs, cn, nxt, small(rank), "rc%d" % t)], 0.65)
         recv(cn, "rc%d" % t, len(small(rank - 1)), [s], OPT["hop"])
-        jj = lin_("wf", JJ, 1.0, mn)
-        idx = ts(sub(new("wf", 48), 32, 48), sub(ex, 16, 32), mn, ALU.subtract, 384.0, ALU.min)
-        top = [4112, E1 + 256, E2B + 256][t]
-        RU, parts = new("wu", 24), ((16, 24), (0, 16)) if OPT["split"][t] else ((0, 24),)
+        if moved:
+            OU = ts("wu", OU, mn, ALU.subtract)
+            idx = ts("wu", sub(sh, 16, 32), mn, ALU.subtract, 384.0, ALU.min)
+            jj = lin_("wf", sub(JJ, 0, 24), 1.0, mn)
+        else:
+            SU = ts("wu", sub(JJ, 0, 8), mn, ALU.add)
+            idx = tt("wf", ts("wf", sub(sh, 16, 32), mn, ALU.is_ge, lin_("wf", mn, -1.0, 384.0), ALU.mult), sub(sh, 16, 32), ALU.add)
+            jj = sub(JJ, 0, 24)
+        top = PCB + 1024 if t else PCB
+        RU, parts, step[0] = new("wu", 24), ((16, 24), (0, 16)) if moved and OPT["split"] else ((0, 24),), "spots%d" % t
         if t == 0:
-            tt(MX, ind(tt("wf", nw0, x0, ALU.subtract), JO), sub(AM, 0, 256), ALU.mult)
-            kept = scan(sub(NC, 1, 257), mm(sub(pa, 0, 256), [(BOS, MX)]), ZERO, 32.0, ALU.add, ALU.add)
-            strew(ind(ap("zf", 256, 256 + 4864), OU), kept, 0)
-            scan(BKG, ap("zf", 256, 640), ap("zf", 256, 640), 0.0, ALU.max, ALU.max)
+            kept = unwrap(sub(NC, 1, 257), tt("wf", endw, x0, ALU.subtract), MX, sub(pa, 0, 256), 32.0)
+            const(ap("da", 0, 384), 0)
+            strew(ind(ap("da", 0, 4352), OU), kept, 0)
+            scan(BKG, const(FIB, 1), ap("da", 0, 384), 0.0, ALU.add, ALU.max)
+            dma([(lambda: T.da[:, 4096:4352], lambda: R(NG))], [ap("da", 4096, 4352)], [NG], 3.0)
             for lo, hi in parts:
                 w = wrap(sub(WA, 16 * lo, 16 * hi), sub(BKG, 16 * lo, 16 * hi))
-                ts(sub(RU, lo, hi), tt("wf", w, sub(jj, lo, hi), ALU.add), -32.0, ALU.add, top - 1.0, ALU.min)
+                ts(sub(RU, lo, hi), w, -32.0, ALU.add, top - 1.0, ALU.min)
         else:
-            rm = tt("wf", st["m"], x0, ALU.subtract)
-            rc = ts("wf", rm, -512.0, ALU.max, -8192.0, ALU.mult)
-            if OPT["po"][t]:
-                off = mm(sub(pa, 256, 272), [(IF, st["bk"]), (IF, rm), (IF, rc)])
-            else:
-                off = tt("wf", tt("wf", st["bk"], rm, ALU.add), rc, ALU.add)
-            unwrap(sub(NC, 1, 257), tt("wf", ts("wf", sub(ex, 0, 16), 8191.0, ALU.mult), off, ALU.add), MX, sub(pa, 0, 256))
+            off = total(sub(pv, 32, 48), st["b0"], [x0, act("wf", d, AF.Relu, TW * (TC + m0), -TW)], "o" in OPT["pe"][t])
+            unwrap(sub(NC, 1, 257), tt("wf", ts("wf", sub(ex, 0, 16), TW - 1, ALU.mult), off, ALU.add), MX, sub(pa, 0, 256))
             zo = 768 - 384 * t
             if t == 1:
-                iota(ap("xb", 384, 768), [[0, 384]], 0, 0)
-                iota(ap("xb", 0, 384), [[0, 384]], 0, 0)
+                const(ap("xb", 384, 768), 0)
+                const(ap("xb", 0, 384), 0)
             c1 = fill(ap("xb", zo, 384 + 4864), 384, OU, t)
             cu = ts("wu", c1, 1.0 / 16, ALU.mult)
-            cj = mm(sub(pw, 16, 40), [(IF, lin_("wf", jj, 8192.0, 16384.0 + 511.0 + [0, E1, E2A][t])), (I16, c1)])
+            base = A0 + PCB - 3
+            cj = [(IF, lin_("wf", jj, TW, float(base) if t == 1 else lin_("wf", hc, -1.0, base))), (I4, c1)]
+            if "f" not in OPT["pe"][t]:
+                cj = mm(sub(pb, 16, 40), cj)
+            if t == 2:
+                cap = lin_("wf", c1, 0.25, 510.0 + PCB)
             for lo, hi in parts:
                 row, wa = act(sub(BKG, 16 * lo, 16 * hi), ind(NC, sub(cu, lo, hi)), AF.Copy), sub(WA, 16 * lo, 16 * hi)
                 if t == 1:
                     pf = wrap(wa, row)
                     p = cp("ri", pf)
                 else:
-                    pf = p = ts("ri", hold(wa, row), inv, ALU.mult)
-                far = tt("wf", tt("wf", sub(cj, lo, hi), pf, ALU.subtract), sub(jj, lo, hi), ALU.max)
-                ts(sub(RU, lo, hi), tt("wf", far, ts("ri", p, 8191, ALU.bitwise_and), ALU.add), -512.0, ALU.add, top - 1.0, ALU.min)
-        snd, arr = sub(SND, 128 * t, 128 * t + 128), ap("nm", Gt + 256, Gt + 384)
-        act(snd, ind(ap("nm", NB, top), sub(RU, 16, 24)), AF.Copy)
+                    pf = hold(wa, row)
+                    p = ts("ri", pf, hc, ALU.add)
+                if "f" in OPT["pe"][t]:
+                    far = mm(sub(pb, 16, 40), cj + [(NIF, pf)])
+                else:
+                    far = tt("wf", sub(cj, lo, hi), pf, ALU.subtract)
+                far = tt("wf", far, sub(jj, lo, hi), ALU.max)
+                a = tt("wf", far, ts("ri", p, 8191, ALU.bitwise_and), ALU.add)
+                if t == 2:
+                    a = tt("wf", a, sub(cap, lo, hi), ALU.min)
+                ts(sub(RU, lo, hi), a, -512.0, ALU.add, top - 1.0, ALU.min)
+        snd, arr = sub(SND, 128 * t, 128 * t + 128), ap("nm", Gt + 384 - 128 * moved, Gt + 512 - 128 * moved)
+        if moved:
+            act(snd, ind(ap("nm", NB, top), sub(RU, 16, 24)), AF.Copy)
+            act(ap("nm", Gt, Gt + 256), ind(ap("nm", NB, top), sub(RU, 0, 16)), AF.Copy)
+        else:
+            act(ap("nm", Gt, Gt + 384), ind(ap("nm", NB, top), RU), AF.Copy)
+            act(snd, ind(ap("nm", Gt, Gt + 384), SU), AF.Copy)
         s = send([(snd, arr, nxt, small(rank), "rn%d" % t)], 0.8)
         recv(arr, "rn%d" % t, len(small(rank - 1)), [s], OPT["hop"])
-        act(ap("nm", Gt, Gt + 256), ind(ap("nm", NB, top), sub(RU, 0, 16)), AF.Copy)
-        t1 = tt("wf", cum, blk(0, 4, 2), ALU.subtract)
-        gp = ts("wf", blk(1, 4, 2), mn, ALU.subtract, cn, ALU.min)
-        cum = ts(sub(new("wf", 80), 0, 32), tt("wf", t1, gp, ALU.add), mn, ALU.add, 4096.0, ALU.min)
+        step[0] = "lengths%d" % t
+        t1 = None if less else tt("wf", cum, sub(pv, 0, 32), ALU.subtract)
+        gp = ts("wf", sh, mn, ALU.subtract, cn, ALU.min)
+        t1 = tt("wf", gp, sub(pv, 0, 32), ALU.subtract) if less else tt("wf", t1, gp, ALU.add)
+        cum = ts(sub(new("wf", 80), 0, 32), t1, mn, ALU.add, 4096.0, ALU.min)
         l = tt("wf", sub(cum, 0, 16), sub(cum, 16, 32), ALU.subtract)
-        k = tt("wf", k, l, ALU.min)
         if t == 2:
-            return idx, cum, l, k
-        bk = tt("wf", begO, k, ALU.add)
+            return idx, cum, l
+        k = tt("wf", k, l, ALU.min)
+        later = "o" in OPT["pe"][t + 1]
+        bk = [begO, k] if later and "v" in OPT["pe"][t] else [tt("wf", begO, k, ALU.add)]
         m = tt("wf", l, k, ALU.subtract)
         if t == 0:
-            gw = ap("nm", G0, G0 + 400)
-            EN = cp("wu", tt("wf", ts("wf", m, 1.0, ALU.is_lt, 384.0, ALU.mult), idx, ALU.max))
+            gw = ap("nm", G0, G0 + 528)
+            EN = ts("wu", tt("wf", act("wf", m, AF.Relu, 512.0, -512.0), idx, ALU.max), 512.0, ALU.min)
             en = ap("nm", E1, E1 + 256)
-            st["mq"] = lin_("wf", m, 1.0, -1.0 - C0)
+            st["cm"] = [lin_("wf", m, -TW, TW), CM]
+            if "m" not in OPT["pe"][1]:
+                st["cm"] = [total(None, st["cm"], [], False)]
+            st["b0"] = [lin_("wf", m, 1 - TW, TW * TC)] + bk
         else:
-            gw = ap("nm", E1, G1 + 400)
-            mm_ = tt("wf", st["m"], m, ALU.min)
-            nf = tt("wf", m, mm_, ALU.subtract)
-            ex2 = new("wf", 32)
-            ix = tt(sub(ex2, 16, 32), ts("wf", nf, -384.0, ALU.mult, 384.0, ALU.add), idx, ALU.max)
-            gone = lin_("wf", mm_, -16384.0, 16384.0)
-            tt(sub(ex2, 0, 16), mm(sub(pw, 64, 80), [(IF, CM), (IF, gone)]) if OPT["po"][0] else tt("wf", CM, gone, ALU.add), ix, ALU.min)
-            EU = ts("wu", ex2, 256.0, ALU.add)
-            EN, en = sub(EU, 16, 32), ap("nm", E2B, E2B + 256)
-            act(ap("nm", E2A, E2A + 256), ind(gw, sub(EU, 0, 16)), AF.Copy)
-            st["OZ"] = ts("wu", tt("wf", st["en"], mm_, ALU.mult), 4104.0, ALU.add)
-            st["mq"] = lin_("wf", nf, 1.0, -C0)
-            unwrap(BKR, bk, MX, sub(pa, 0, 256))
-            f = new("wf", 32)
-            act(sub(f, 0, 16), m, AF.Relu, 16384.0, -16384.0)
-            act(sub(f, 16, 32), m, AF.Relu, 32768.0, -16384.0)
-            st["old"] = tt("wf", f, CE, ALU.add)
-            st["ck"] = tt("wf", C16K, k, ALU.subtract)
+            gw = ap("nm", E1, G1 + 528)
+            df = tt("wf", m, st["m"], ALU.subtract)
+            ix = tt("wf", act("wf", df, AF.Relu, 512.0, -512.0), idx, ALU.max)
+            old = total(sub(pb, 48, 64), st["cm"] + [act("wf", df, AF.Abs, 0.0, TW)], [], "m" in OPT["pe"][1])
+            EN = ts("wu", tt("wf", old, ix, ALU.min), 256.0, ALU.add, 768.0, ALU.min)
+            en = sub(PC, 2, 1024, 4)
+            both = st["both"] = act("wf", m, AF.Relu, -TW, TW)
+            st["EW0"], st["VU0"] = st["EW"], st["VU"]
+            st["OZ"] = ts("wu", tt("wf", st["en"], both, ALU.mult), 1.0 / TW, ALU.mult, 4104.0, ALU.add)
+            st["no"] = new("wf", 32)
+            lin_(sub(st["no"], 0, 16), both, -0.5 / TW, 0.5)
+            act(sub(st["no"], 16, 32), m, AF.Relu, 0.5, -0.5)
+            st["b0"] = [lin_("wf", m, 1 - 1.5 * TW, TW * TC), both] + bk
+            unwrap(BKR, tt("wf", begO, l, ALU.add), MX, sub(pa, 0, 256))
+        st["mq"] = lin_("wf", m, 1.0, -1.0)
         act(en, ind(gw, EN), AF.Copy)
         ew = hold(WD, en)
-        st["EW"] = ts("wu", ew, inv, ALU.mult, -1.0, ALU.add)
+        st["EW"] = ts("wu", ew, hc, ALU.add)
         if t == 0:
-            st["en"] = ts("wf", ew, inv, ALU.mult, -4105.0, ALU.add)
-        zz = tt("wf", act("wf", k, AF.Relu, 1.0, -1.0), DUMO, ALU.mult)
-        st["VU"] = ts("wu", tt("wf", bk, zz, ALU.max), -16897.0, ALU.add)
-        st.update({"cum": cum, "k": k, "l": l, "m": m, "bk": bk})
+            st["en"] = ts("wf", ew, hc, ALU.add, -4104.0, ALU.add)
+            if OPT["e1g"]:
+                keep(sub(PC, 1, 1024, 4), en, [[0, 256]], ALU.is_ge, 0.0, 0, 0)
+            else:
+                act(sub(PC, 1, 1024, 4), en, AF.Copy)
+        if not later:
+            st["b0"] = [total(None, st["b0"], [], False)]
+        zz = total(sub(pb, 64, 80), bk + [act("wf", k, AF.Relu, 8192.0, -8192.0)], [], "v" in OPT["pe"][t])
+        st["VU"] = ts("wu", tt("wf", zz, DUMO, ALU.min), -A0 - 1, ALU.add)
+        st.update({"cum": cum, "cw": sub(cum, 0, 16), "dw": sub(cum, 16, 32), "k": k, "l": l, "m": m})
         return None
 
-    def final(idx, cum, l, k):
-        PC, PEN, PS = ap("xb", 0, 1024), ap("xb", 1024, 2048), ap("xb", 2048, 3072)
-        gw = ap("nm", E2A, G2 + 400)
-        ex = ap("wf", idx[2] - 32, idx[3])
-        for s in range(2):
-            tt(sub(ex, 16 * s, 16 * s + 16), sub(st["old"], 16 * s, 16 * s + 16), idx, ALU.min)
-        EU = ts("wu", ex, float(G2 - E2A), ALU.add)
+    def final(idx, cum, l):
+        PEN, PS, step[0] = ap("xb", 1024, 2048), ap("xb", 2048, 3072), "last"
         cw, dw = sub(cum, 0, 16), sub(cum, 16, 32)
-        kw = tt(sub(cum, 32, 48), dw, k, ALU.add)
-        code = unwrap(NB2, tt("wf", st["ck"], dw, ALU.subtract), MX, sub(pa, 0, 256))
+        u3 = new("wf", 48)
+        u = tt(sub(u3, 32, 48), dw, st["l"], ALU.add)
+        code = unwrap(NB2, u, MX, sub(pa, 0, 256))
         q32 = ts("ri", cum, 0.0625, ALU.mult, -0.46875, ALU.add)
         pe_, pq_ = sub(q32, 0, 16), sub(q32, 16, 32)
         OU = cp("wu", tt("wf", tt("wf", tt("wf", pq_, pe_, ALU.is_equal), C272, ALU.mult), pq_, ALU.max))
-        for s in (1, 2):
-            tt(sub(cum, 32 + 16 * s, 48 + 16 * s), lin_("wf", kw, 1.0, float(s)), cw, ALU.min)
-        r4 = ts("ri", cp("ri", sub(cum, 16, 80)), 15, ALU.bitwise_and)
-        PU = cp("wu", r4)
-        BU = ts("wu", tt("wf", beg16, sub(r4, 0, 16), ALU.subtract), 4111.0, ALU.min)
-        if OPT["sil"][3]:
-            c1 = fill(ZF, 256, OU, 3)
-            cu = ts("wu", c1, 1.0 / 16, ALU.mult, -1.0, ALU.add)
-            nw = wrap(WA, act(FIL, ind(code, cu), AF.Copy))
-            act(sub(BKG, 0, 256), ind(BKR, cu), AF.Copy)
-            y5 = ts("ri", tt("ri", nw, JV, ALU.add), 16383, ALU.bitwise_and)
-            c4 = lin_("wf", c1, 0.25, -4.0)
-        else:
-            cp(ind(ZF, OU), code)
-            scan(FIL, sub(ZF, 0, 256), sub(ZF, 0, 256), 0.0, ALU.max, ALU.max)
-            nw = wrap(WA, FIL)
-            act(sub(BKG, 0, 256), ind(BKR, ts("wu", nw, 1.0 / 16384, ALU.mult)), AF.Copy)
-            a = tt("ri", nw, JV, ALU.add)
-            y5 = ts("ri", a, 16383, ALU.bitwise_and)
-            c4 = ts("ri", a, 12, ALU.arith_shift_right, 1020, ALU.bitwise_and)
-        GU = ts("wu", tt("wf", ts("wf", y5, 5632.0, ALU.max, 5635.0, ALU.min), c4, ALU.add), -5632.0, ALU.add)
-        AU = ts("wu", tt("wf", wrap(WB, sub(BKG, 0, 256)), y5, ALU.add), 16.0 - 5632.0 - 16896.0, ALU.add, 4111.0, ALU.min)
-        HJ = lin_(MX, ind(PCR, GU), 1.0, 4097.0)
-        for s in range(4):
-            o, i_ = sub(PEN, s, 1024, 4), ind(PT, sub(PU, 16 * s, 16 * s + 16))
-            if s < OPT["pen"]:
-                cp(o, i_)
-            else:
-                act(o, i_, AF.Copy)
-        lin_(sub(PC, 0, 1024, 4), ind(WIN, BU), 1.0, 4096.0)
         for s in range(3):
-            if s < OPT["pc"]:
-                ts(sub(PC, 1 + s, 1024, 4), ind(gw, sub(EU, 16 * s, 16 * s + 16)), 4096.0, ALU.add)
+            if s < 2:
+                lin_(sub(u3, 16 * s, 16 * s + 16), u, 1.0, s - 2.0)
+            if OPT["three"]:
+                mm(sub(pe, 64 + 16 * s, 80 + 16 * s), [(IF, cw)])
             else:
-                lin_(sub(PC, 1 + s, 1024, 4), ind(gw, sub(EU, 16 * s, 16 * s + 16)), 1.0, 4096.0)
-        scan(PS, PEN, PC, 8192.0, ALU.add, ALU.max)
+                tt(sub(cum, 32 + 16 * s, 48 + 16 * s), sub(u3, 16 * s, 16 * s + 16), cw, ALU.min)
+        if OPT["three"]:
+            tt(sub(cum, 32, 80), u3, sub(pe, 64, 112), ALU.min)
+        tt(sub(cum, 32, 64), sub(cum, 32, 64), st["no"], ALU.add)
+        r4 = ts("ri", ts("ri", sub(cum, 16, 80), 2.0, ALU.mult), 31, ALU.bitwise_and)
+        PU = cp("wu", r4)
+        BU = ts("wu", tt("wf", beg32, sub(r4, 0, 16), ALU.subtract), 0.5, ALU.mult, 4111.0, ALU.min)
+        c1 = fill(ZF, 256, OU, 3)
+        cu = ts("wu", c1, 1.0 / 16, ALU.mult, -1.0, ALU.add)
+        y = tt("wf", JV, hold(WA, take(FIL, ind(code, cu), OPT["pc"][2])), ALU.subtract)
+        act(sub(BKG, 0, 256), ind(BKR, cu), AF.Copy)
+        c4, gifts = lin_(sub(CG, 16, 32), c1, 0.25, -4.0), ts(sub(CG, 32, 48), y, 0.0, ALU.max, 3.0, ALU.min)
+        gu, gd = sub(pw, 80, 96), sub(pw, 96, 112)
+        mm(sub(pw, 80, 112), [[(DM, sub(CG, 0, 32)), (IB, c4, gu), (S0, sub(CG, 15, 31), gd)], [(IB, gifts, gu), (DM, gifts, gd), (S0, sub(CG, 31, 47), gd)]])
+        GU = ts("wu", sub(pw, 80, 112), 1024.0, ALU.min)
+        GU, GD = sub(GU, 0, 16), sub(GU, 16, 32)
+        AU = ts("wu", tt("wf", hold(WB, sub(BKG, 0, 256)), y, ALU.add), lin_("wf", hc, 1.0, 14.0 - A0), ALU.add, 4111.0, ALU.min)
+        act(sub(HD, 1, 257), ind(WIN, AU), AF.Copy)
+        for s in range(4):
+            take(sub(PEN, s, 1024, 4), ind(PT, sub(PU, 16 * s, 16 * s + 16)), s < OPT["pen"])
+        take(sub(PC, 0, 1024, 4), ind(WIN, BU), OPT["pc"][0])
+        gift = ind(ap("nm", G2, G2 + 400), idx) if OPT["moved"] else ind(ap("nm", G2, G2 + 528), ts("wu", idx, 512.0, ALU.min))
+        take(sub(PC, 3, 1024, 4), gift, OPT["pc"][1])
+        scan(PS, PEN, PC, 0.0, ALU.add, ALU.max)
         o = sub(pe, 128, 256, 1, (0, 16))
         add("P", lambda g: g.tensor.transpose(R(o), R(l), R(IF)), [o], [l, IF], 0.45, 0.5)
         yn = act(sub(WD, 0, 128, 1, (0, 16)), o, AF.Copy)
         dma([(lambda g_=g_: T.yn[g_, :], lambda g_=g_: R(sub(yn, 16 * g_, 16 * g_ + 16, 1, (0, 16)))) for g_ in range(8)], [], [yn], 2.5)
-        tcol = lin_("wf", mm(sub(pw, 8, 9), [(S15, sub(cw, 15, 16))]), 8192.0, -4096.0)
-        mk = lin_(sub(pc, 0, 256), act(NA, POS8, AF.Relu, tcol), 1.0, -1.0)
-        tt(sub(CODE, 1, 257), ind(WIN, AU), HJ, ALU.subtract)
-        tt(FIL, ind(PS, GU), HJ, ALU.subtract)
+        tcol = lin_("wf", mm(sub(pw, 8, 9), [(S15, sub(cw, 15, 16))]), 8192.0, ni8k)
+        mk = lin_(sub(pc, 0, 256), act(NA, sub(J, 0, 256), AF.Relu, tcol, -131072.0), 1.0, -1.0)
+        tt(sub(CODE, 0, 256), ind(PCR, GD), sub(HD, 0, 256), ALU.add)
         YO = XS
         for lo in range(0, 256, OPT["last"]):
             hi = lo + OPT["last"]
-            h3 = tt(sub(gui, lo, hi), sub(FIL, lo, hi), sub(CODE, lo, hi), ALU.min)
+            h3 = tt(sub(gui, lo, hi), ind(PS, sub(GU, lo // 16, hi // 16)), sub(CODE, lo, hi), ALU.min)
             tt(sub(YO, lo, hi), ts(sub(spi, lo, hi), h3, 4095, ALU.bitwise_and), sub(mk, lo, hi), ALU.min)
             dma([(lambda lo=lo, hi=hi: T.yo[:, lo:hi], lambda lo=lo, hi=hi: R(sub(YO, lo, hi)))], [], [sub(YO, lo, hi)], 2.3, "Y" if lo else "S")
 
+    def shifted(k, gate):
+        lo, hi = OPT["parts"][k:k + 2]
+        if hi > lo:
+            dma([(lambda i=i: T.zf[i:128:16, 544:4656], lambda i=i: T.lin[:, i:i + 4112]) for i in range(lo, hi)],
+                [ap("zf", 544 + k, 4656, 3), gate], [lin], 8.0)
+
     light(0, heavy(0))
-    dma([(lambda i=i: T.zf[i:128:16, 544:4656], lambda i=i: T.lin[:, i:i + 4112]) for i in range(16)], [WIN, sub(SND, 0, 128)], [lin], 13.0)
+    shifted(0, ap("cs", 0, 1))
+    shifted(1, sub(SND, 0, 128))
     light(1, heavy(1))
+    shifted(2, ap("cs", 4, 5))
     final(*light(2, heavy(2)))
+    OPT["used"] = dict(free)
     return ops
 
 
@@ -684,6 +805,9 @@ def order(ops):
     n = len(ops)
     seen = {}
     for i, o in enumerate(ops):
+        if o["sem"] is None and "slow" not in o:
+            o["slow"] = (SLOW - 1) * o["cost"]
+            o["cost"], o["lat"] = o["cost"] + o["slow"], o["lat"] + o["slow"]
         soft = set(o["after"])
         hard = set()
         for kind, regs in (("r", o["rd"]), ("w", o["wr"])):
@@ -693,9 +817,7 @@ def order(ops):
                     hit = l2 < hi and lo < h2 and (kind == "w" or k2 == "w") and not (sp == s2 and (lo - l2) % sp)
                     if ps and ops[j]["eng"] == "P" and o["eng"] == "P":
                         soft.add(j)
-                    elif hit and kind == "w" and k2 == "r" and ops[j]["eng"] == o["eng"] and o["sem"] is None and ops[j]["sem"] is None:
-                        soft.add(j)
-                    elif hit or (ps and ops[j]["eng"] != o["eng"]):
+                    elif j != i and hit or (ps and ops[j]["eng"] != o["eng"]):
                         hard.add(j)
         for kind, regs in (("r", o["rd"]), ("w", o["wr"])):
             for (b, lo, hi, sp) in regs:
@@ -755,27 +877,175 @@ def order(ops):
         rng = np.random.default_rng(OPT["seed"])
         at = place([-v for v in lev], False)
         best = (span(at), at)
-        for it in range(ROUNDS // 300):
+        kinds = sorted(set((o["step"], o["eng"]) for o in ops if o["eng"] in ("V", "S")))
+        for it in range(OPT["tries"]):
             mid, half, amp = rng.random() * best[0], 2 + 12 * rng.random(), 4 * rng.random()
             noise = rng.random(n) * amp
-            at = place([t + (noise[i] if abs(t - mid) < half else 0.5 * amp) for i, t in enumerate(best[1])], False)
+            if it % 2:
+                by = {kinds[int(rng.random() * len(kinds))]: OPT["move"] * (2 * rng.random() - 1) for _k in range(1 + it % 4 // 2)}
+                at = place([t + by.get((o["step"], o["eng"]), 0.0) for o, t in zip(ops, best[1])], False)
+            else:
+                at = place([t + (noise[i] if abs(t - mid) < half else 0.5 * amp) for i, t in enumerate(best[1])], False)
             bk = place([-(at[i] + cost[i]) for i in range(n)], True)
             at = place([-(bk[i] + cost[i]) for i in range(n)], False)
             end = span(at)
             if end <= best[0] + 0.02:
                 best = (end, at)
-        KNOWN["t"] = improve(ops, pre, cost, best[1], rng)
+        KNOWN["t"], OPT["mid"] = best[1], round(best[0], 1)
+        for rounds, hot in OPT["plan"]:
+            at = improve(ops, eng, pre, KNOWN["t"], rng, rounds, hot)
+            for _k in range(3):
+                bk = place([-(at[i] + cost[i]) for i in range(n)], True)
+                new = place([-(bk[i] + cost[i]) for i in range(n)], False)
+                at = new if span(new) <= span(at) else place(at, False)
+            KNOWN["t"] = at
+        OPT["ends"] = round(span(at), 1)
+        KNOWN["t"] = list(zip(KNOWN["t"], eng))
         KNOWN["few"] = [t for t, o in zip(KNOWN["t"], ops) if "more" not in o]
     at = KNOWN["t" if n == len(KNOWN["t"]) else "few"]
     assert len(at) == n
+    for o, (t, e) in zip(ops, at):
+        if e != o["eng"]:
+            o["emit"] = o["alt"]
+        o["t"], o["eng"] = t, e
+    return sorted(range(n), key=lambda i: (at[i][0], i))
+
+
+def shorten(seq, eng, case, rng, steps):
+    before, cost, lat = case
+    n = len(seq)
+    after = [[] for _ in range(n)]
     for i in range(n):
-        ops[i]["t"] = at[i]
-    return sorted(range(n), key=lambda i: (at[i], i))
+        for j, w in before[i]:
+            after[j].append((i, w))
+    need = [len(b) for b in before]
+    up, down, last = [-1] * n, [-1] * n, {}
+    for i in seq:
+        if eng[i] is not None:
+            p = last.get(eng[i], -1)
+            up[i] = p
+            if p >= 0:
+                down[p] = i
+            last[eng[i]] = i
+
+    def times():
+        left = [need[i] + (up[i] >= 0) for i in range(n)]
+        free, head, line = [0.0] * n, [0.0] * n, [i for i in range(n) if not left[i]]
+        for i in line:
+            s, p = free[i], up[i]
+            if p >= 0 and head[p] + cost[p] > s:
+                s = head[p] + cost[p]
+            head[i] = s
+            for k, w in after[i]:
+                if s + w > free[k]:
+                    free[k] = s + w
+                left[k] -= 1
+                if not left[k]:
+                    line.append(k)
+            k = down[i]
+            if k >= 0:
+                left[k] -= 1
+                if not left[k]:
+                    line.append(k)
+        rest, tail = [0.0] * n, [0.0] * n
+        for i in reversed(line):
+            s = lat[i]
+            for k, w in after[i]:
+                if tail[k] + w > s:
+                    s = tail[k] + w
+            rest[i] = s
+            k = down[i]
+            if k >= 0 and tail[k] + cost[i] > s:
+                s = tail[k] + cost[i]
+            tail[i] = s
+        return free, head, rest, tail, line
+
+    best, barred, since = (1e9, None, None, None), {}, 0
+    draw = rng.random((steps, 3)).tolist()
+    for it in range(steps):
+        free, head, rest, tail, line = times()
+        end = max(tail)
+        if end < best[0] - 1e-6:
+            best, since = (end, up[:], down[:], sorted(line, key=lambda i: head[i])), it
+        elif it - since > OPT["back"]:
+            up[:], down[:], since, barred = best[1], best[2], it, {}
+            continue
+        tops = [i for i in range(n) if head[i] == 0.0 and tail[i] > end - 1e-6]
+        i, runs = tops[int(draw[it][0] * len(tops))], []
+        cur, flip = [i], draw[it][1] < 0.5
+        while True:
+            k = down[i]
+            on = k >= 0 and tail[k] + cost[i] > tail[i] - 1e-7
+            off = [c for c, w in after[i] if tail[c] + w > tail[i] - 1e-7]
+            if on and (flip or not off):
+                cur.append(k)
+            elif off:
+                runs.append(cur)
+                k = off[0]
+                cur = [k]
+            else:
+                runs.append(cur)
+                break
+            i = k
+        pick = (1e9, None, None)
+        for run in runs:
+            m = len(run)
+            for a in range(m - 1):
+                u = run[a]
+                p = up[u]
+                start = head[p] + cost[p] if p >= 0 else 0.0
+                for b in range(a + 1, min(m, a + OPT["far"])):
+                    if a and b < m - 1 and b > a + 1:
+                        continue
+                    v = run[b]
+                    part = run[a:b + 1]
+                    k = down[v]
+                    for new in ([v] + part[:-1], part[1:] + [u]) if b > a + 1 else ([v, u],):
+                        if new[0] == v:
+                            lim = head[u] + cost[u] - 1e-9
+                            if any(head[j] >= lim or j == u for j, _w in before[v]):
+                                continue
+                        elif any(tail[c] >= tail[v] + cost[c] - 1e-9 or c == v for c, _w in after[u]):
+                            continue
+                        s, hs = start, []
+                        for c in new:
+                            if free[c] > s:
+                                s = free[c]
+                            hs.append(s)
+                            s += cost[c]
+                        q, est = (tail[k] if k >= 0 else -1e9), 0.0
+                        for c in reversed(new):
+                            q += cost[c]
+                            if rest[c] > q:
+                                q = rest[c]
+                            s = hs.pop() + q
+                            if s > est:
+                                est = s
+                        if est < pick[0] and (est < best[0] - 1e-6 or not any(
+                                barred.get((v, c) if new[0] == v else (c, u), -1) > it for c in part)):
+                            pick = (est, new, part)
+        if pick[1] is None:
+            barred = {}
+            continue
+        _e, new, part = pick
+        p, k = up[part[0]], down[part[-1]]
+        for c in new:
+            up[c] = p
+            if p >= 0:
+                down[p] = c
+            p = c
+        down[p] = k
+        if k >= 0:
+            up[k] = p
+        until = it + OPT["bar"] + int(draw[it][2] * OPT["bar"])
+        for c in part:
+            barred[(c, part[-1]) if new[0] == part[-1] else (part[0], c)] = until
+    OPT["mid"] = round(best[0], 1)
+    return best[3]
 
 
-def improve(ops, pre, cost, at, rng):
+def improve(ops, eng, pre, at, rng, rounds, hot):
     n = len(ops)
-    eng = [o["eng"] for o in ops]
     anc, lean = [0] * n, []
     for i in range(n):
         far = 0
@@ -787,11 +1057,16 @@ def improve(ops, pre, cost, at, rng):
     for gather, scatter, slow, hop, dma in CASES:
         cost = [max(o["cost"], 1e-3) if o["sem"] else slow * (0.04 + (o["cost"] - 0.04) * {"g": gather, "s": scatter, "": 1.0}[o["kind"]]) for o in ops]
         lat = [o["lat"] * dma if o["sem"] else c + o["lat"] - o["cost"] for o, c in zip(ops, cost)]
-        cases.append(([[(j, cost[j] if j not in o["hard"] and eng[j] == o["eng"] else max(lat[j], cost[j]) + hop) for j in lean[i]]
-                       for i, o in enumerate(ops)], cost, lat))
+        before = [[(j, cost[j] if j not in o["hard"] and eng[j] == o["eng"] else max(lat[j], cost[j]) + hop) for j in lean[i]]
+                  for i, o in enumerate(ops)]
+        after = [[] for _ in range(n)]
+        for i in range(n):
+            for j, w in before[i]:
+                after[j].append((i, w))
+        cases.append((before, cost, lat, after))
 
     def run(seq, case, a=0, old=None):
-        before, cost, lat = case
+        before, cost, lat, _after = case
         t, by = (old[1][:], old[2][:]) if a else ([0.0] * n, [-1] * n)
         free = {eng[i]: i for i in seq[:a]}
         end, last = 0.0, -1
@@ -809,24 +1084,93 @@ def improve(ops, pre, cost, at, rng):
             t[i], by[i] = s, b
             if s + lat[i] > end:
                 end, last = s + lat[i], i
-        return end + 0.3 * sum(t) / n, t, by, last, end
+        return end + OPT["mean"] * sum(t) / n, t, by, last, end
+
+    def rest(seq, case, got):
+        _before, cost, lat, after = case
+        tail, up, down, last = [0.0] * n, [-1] * n, [-1] * n, {}
+        for i in reversed(seq):
+            s = lat[i]
+            for k, w in after[i]:
+                if tail[k] + w > s:
+                    s = tail[k] + w
+            e = eng[i]
+            if e is not None:
+                k = last.get(e)
+                if k is not None:
+                    down[i], up[k] = k, i
+                    if tail[k] + cost[i] > s:
+                        s = tail[k] + cost[i]
+                last[e] = i
+            tail[i] = s
+        return got[:5] + (tail, up, down, {})
+
+    def least(part, case, old):
+        before, cost, lat, after = case
+        t0, tail, up, down = old[1], old[5], old[6], old[7]
+        inside, t, free, end = set(part), {}, {}, 0.0
+        for i in part:
+            e = eng[i]
+            if e is not None:
+                if up[i] not in inside:
+                    free[e] = t0[up[i]] + cost[up[i]] if up[i] >= 0 else 0.0
+                if down[i] not in inside:
+                    free[e, 1] = tail[down[i]] if down[i] >= 0 else -1e9
+        for i in part:
+            e = eng[i]
+            s = free[e] if e is not None else 0.0
+            for j, w in before[i]:
+                c = (t[j] if j in inside else t0[j]) + w
+                if c > s:
+                    s = c
+            t[i] = s
+            free[e] = s + cost[i]
+            q = lat[i]
+            for k, w in after[i]:
+                if k not in inside and tail[k] + w > q:
+                    q = tail[k] + w
+            if s + q > end:
+                end = s + q
+        for e in "VSPGY":
+            if (e, 1) in free and free[e] + free[e, 1] > end:
+                end = free[e] + free[e, 1]
+        return end
 
     seq = sorted(range(n), key=lambda i: (at[i], i))
-    now = [run(seq, c) for c in cases]
+    now = [rest(seq, c, run(seq, c)) for c in cases]
     weight = [66.0 / r[4] / len(cases) for r in now]
     val = sum(w * r[0] for w, r in zip(weight, now))
-    best = (val, seq)
-    for it, r in enumerate(rng.random((ROUNDS, 7)).tolist()):
-        slack = OPT["hot"] * (0.015 / OPT["hot"]) ** (it / ROUNDS)
-        _v, _t, by, last, _e = now[int(r[6] * len(cases))]
-        pairs, i = [], last if r[0] < 0.7 else int(r[1] * n)
-        while i != -1:
-            if by[i] <= -2:
-                pairs.append((-2 - by[i], i))
-            i = -2 - by[i] if by[i] <= -2 else by[i]
+    best = (val, seq, eng[:])
+    for it, r in enumerate(rng.random((rounds, 7)).tolist()):
+        slack = hot * (0.015 / hot) ** (it / rounds)
+        by, last, _end, _tail, _up, _down, ways = now[int(r[6] * len(cases))][2:]
+        i = last if r[0] < 0.7 else int(r[1] * n)
+        if i not in ways:
+            pairs = ways[i] = []
+            while i != -1:
+                if by[i] <= -2:
+                    pairs.append((-2 - by[i], i))
+                i = -2 - by[i] if by[i] <= -2 else by[i]
+        else:
+            pairs = ways[i]
         if not pairs:
             continue
         p, i = pairs[int(r[2] * len(pairs))]
+        if r[6] * 977 % 1 < OPT["swap"]:
+            c = i if r[5] < 0.5 else p
+            if "alt" in ops[c]:
+                eng[c] = "S" if eng[c] == "V" else "V"
+                got = [run(seq, q, min(seq.index(c), n - 40), old) for q, old in zip(cases, now)]
+                v = sum(w * q[0] for w, q in zip(weight, got))
+                if v <= val - slack * math.log(1 - r[4]):
+                    val = v
+                    seq = sorted(seq, key=lambda j: got[0][1][j])
+                    now = [rest(seq, q, x) for q, x in zip(cases, got)]
+                    if val < best[0]:
+                        best = (val, seq, eng[:])
+                else:
+                    eng[c] = "S" if eng[c] == "V" else "V"
+                continue
         a, b = seq.index(p), seq.index(i)
         more = int(-math.log2(1 - r[3]))
         if r[5] < 0.5:
@@ -840,7 +1184,7 @@ def improve(ops, pre, cost, at, rng):
             if anc[i] >> seq[a] & 1:
                 continue
             mid = seq[a:b]
-            new = seq[:a] + [j for j in mid if anc[i] >> j & 1] + [i] + [j for j in mid if not anc[i] >> j & 1] + seq[b + 1:]
+            new = [j for j in mid if anc[i] >> j & 1] + [i] + [j for j in mid if not anc[i] >> j & 1]
         else:
             for _k in range(more):
                 c = b + 1
@@ -852,26 +1196,43 @@ def improve(ops, pre, cost, at, rng):
             if anc[seq[b]] >> p & 1:
                 continue
             mid = seq[a + 1:b + 1]
-            new = seq[:a] + [j for j in mid if not anc[j] >> p & 1] + [p] + [j for j in mid if anc[j] >> p & 1] + seq[b + 1:]
+            new = [j for j in mid if not anc[j] >> p & 1] + [p] + [j for j in mid if anc[j] >> p & 1]
+        limit = val - slack * math.log(1 - r[4])
+        if val + sum(w * (least(new, c, q) - q[4]) for w, c, q in zip(weight, cases, now)) > limit + 0.02:
+            continue
+        new = seq[:a] + new + seq[b + 1:]
         a = min(a, n - 40)
         got = [run(new, c, a, q) for c, q in zip(cases, now)]
         v = sum(w * q[0] for w, q in zip(weight, got))
-        if v <= val or r[4] < math.exp((val - v) / slack):
-            val, now = v, got
+        if v <= limit:
+            val = v
             seq = sorted(new, key=lambda j: got[0][1][j])
+            now = [rest(seq, c, q) for c, q in zip(cases, got)]
             if val < best[0]:
-                best = (val, seq)
-    OPT["ends"] = [round(run(best[1], c)[4], 1) for c in cases]
+                best = (val, seq, eng[:])
+    eng[:] = best[2]
     t = run(best[1], cases[0])[1]
     for k, i in enumerate(best[1]):
         t[i] += 1e-7 * k
     return t
 
 
+def share(step, on_v):
+    cut = 16 - on_v
+    return ([(a, min(a + step, cut), False) for a in range(0, cut, step)] + [(a, min(a + step, 16), True) for a in range(cut, 16, step)])
+
+
 KNOWN = {}
 ROUNDS = 270000
-CASES = [(1, 1, 1.05, 0.13, 1.0)]
-OPT = {"hop": 0.7, "seed": 1, "hot": 0.12, "wd": [0, 0, 0], "po": [0, 0, 0], "split": [1, 0, 0], "sil": [1, 1, 1, 0], "fl": [800, 480], "aud": [2.3, 0.7], "l0": 3.0, "l1": 3.5, "l2": 2.5, "nm": 7.0, "pc": 1, "pen": 1, "last": 128, "xs": [1, 1, 1], "mxl": [0, 1, 1]}
+SLOW = 1.05
+CASES = [(1, 1, 1.0, 0.13, 1.0)]
+EIGHTHS = list(range(0, 4097, 512))
+OPT = {"half": 128, "pf": 0.9, "three": False, "parts": [0, 6, 12, 16], "moved": False, "split": False, "mxl": [1, 1, -1], "swap": 0.1, "mean": 0.5, "tries": 500, "move": 6.0, "plan": [(120000, 0.3), (60000, 0.12), (30000, 0.06)], "seed": 3,
+       "hop": 0.7, "aud": [2.3, 0.7], "l0": 3.0, "l1": 3.5, "l2": 2.5, "nm": 10.0, "early": 0,
+       "sil": [1, 1, 1, 1], "fl": [800, 480], "pc": [0, 0, 0], "pen": 0, "vs": [[], [], []], "last": 128, "e1g": 1,
+       "vg": [share(4, 8), share(2, 4), share(2, 4)], "every": [1, 1, 1], "pe": ["", "", ""],
+       "cuts": [[0, 512, 1280, 4096], EIGHTHS, EIGHTHS], "sgn": [[512, 1280], EIGHTHS, EIGHTHS],
+       "two": [1280, 2304, 3328, 4096]}
 
 
 def rank_program(g, core, T, topo):

import math
import numpy as np
from concourse.bass import DstId, RemoteDMATransfer
from concourse.mybir import AluOpType as ALU, ActivationFunctionType as AF

N, CORES = 4, 48
F32, BF, I32, U16 = "float32", "bfloat16", "int32", "uint16"
NB, PCB, E1, G1, G0, G2, NMW = 0, 4112, 5136, 5392, 5920, 6448, 6976
GB = [G0, G1, G2]
CW, RW, BW, IW, UW, WW = 3328, 5376, 6144, 640, 1024, 3584
SCRATCH = {
    "au0": ("sbuf", [128, 4112], BF), "au1": ("sbuf", [128, 4112], BF), "au2": ("sbuf", [128, 4112], BF),
    "xa": ("sbuf", [128, 4352], F32), "xb": ("sbuf", [128, 384 + 4864], F32),
    "da": ("sbuf", [128, 4352], F32), "db": ("sbuf", [128, 4352], F32),
    "fl": ("sbuf", [128, 4352], BF), "sg": ("sbuf", [128, 4096], BF),
    "nm": ("sbuf", [128, NMW], F32), "zf": ("sbuf", [128, 4656], F32), "cf": ("sbuf", [128, CW], F32),
    "rf": ("sbuf", [128, RW], F32), "rb": ("sbuf", [128, BW], BF), "ri": ("sbuf", [128, IW], I32),
    "wu": ("sbuf", [128, UW], U16), "wf": ("sbuf", [128, WW], F32),
    "spi": ("sbuf", [128, 256], I32), "gui": ("sbuf", [128, 256], I32), "lni": ("sbuf", [128, 256], I32),
    "st3": ("sbuf", [128, 8, 2, 16], F32), "cs": ("sbuf", [128, 12], F32), "cn": ("sbuf", [128, 12], F32),
    "lin": ("dram", [8, 4128], F32),
}
for _k in range(8):
    SCRATCH["p%d" % _k] = ("psum", [128, 512], F32)
SEMAPHORES = (["cV", "cS", "cP", "cG"] + ["d%d" % k for k in range(20)] + ["lo%d" % k for k in range(12)]
              + ["a1h0", "a1h1", "a1h2", "a1h3", "a2h0", "a2d"] + ["rc%d" % t for t in range(3)] + ["rn%d" % t for t in range(3)])

CY = 0.00092
HOP = 0.13
BIG = float(1 << 23)
HOLD = float(1 << 24)
RND = float(3 << 22)
C0 = 23.5 / 32
TW, TC = 16384.0, 386.0
A0 = 2 * TW + 512
VIA = [0, 2]


def ap(name, lo, hi, step=1, parts=None):
    return ("ap", name, lo, hi, step, parts)


def sub(a, lo, hi, step=1, parts=None):
    return ("ap", a[1], a[2] + lo, a[2] + hi, step, parts)


def ind(w, o):
    return ("ind", w, o)


def raw(name, lo, hi, fn, n):
    return ("raw", name, lo, hi, fn, n)


def count(a):
    if a[0] == "ind":
        return 16 * count(a[2])
    if a[0] == "raw":
        return a[5]
    return (a[3] - a[2] + a[4] - 1) // a[4]


def regions(a):
    if not isinstance(a, tuple):
        return []
    if a[0] == "ind":
        return regions(a[1]) + regions(a[2])
    return [(a[1], a[2], a[3], a[4] if a[0] == "ap" else 1)]


def wide(a):
    return SCRATCH[a[1][1] if a[0] == "ind" else a[1]][2] in (F32, I32)


def in_psum(a):
    return a[0] != "ind" and SCRATCH[a[1]][0] == "psum"


def helper(r, T, topo):
    src, dst = T.cores[r % N], T.cores[(r - 1) % N]
    if topo.chip(src) == topo.chip(dst):
        return None
    return [c for c in topo.cores_of(src) if c not in T.cores and topo.die(c) != topo.die(src) and topo.may_write(c, dst)][0]


def rounds(r, T, topo):
    src, dst = T.cores[r % N], T.cores[(r - 2) % N]
    chips = sorted(set(topo.chip(c) for c in range(CORES) if topo.chip(c) != topo.chip(src) and topo.same_plane(topo.chip(c), topo.chip(src))))[:2]
    far = [[c for c in range(CORES) if topo.chip(c) == k and topo.die(c) == d and topo.may_write(c, dst)][0] for d, k in enumerate(chips)]
    es, near = topo.engines(src, far[0]), helper(r - 1, T, topo)
    return [(far[0], es[:len(es) // 2]), (far[1], es[len(es) // 2:]), (near, [e for e in topo.engines(src, near) if e not in es])]


def hand_on(g, core, T, topo):
    visit_1(g, core, T, topo)
    for r in range(N):
        if helper(r - 1, T, topo) is not None:
            dst = T.cores[(r - 2) % N]
            rid, pid, _se = topo.addr(dst)
            for h, (c, es) in enumerate(rounds(r, T, topo)):
                if c == core:
                    g.wait_ge(T.sem.a2d, len(es))
                    g.remote_dma(T.au2[:, 1024 * h:1024 * h + 1024], T.au2[:, 1024 * h:1024 * h + 1024], T.sem.a2h0, T.sem.lo1,
                                 pid, rid, topo.mask(core, dst))
                    g.wait_ge(T.sem.lo1, len(topo.engines(core, dst)))


def visit_1(g, core, T, topo):
    for r in range(N):
        if helper(r, T, topo) == core:
            dst = T.cores[(r - 1) % N]
            rid, pid, _se = topo.addr(dst)
            into = [e for e in topo.engines(T.cores[r], core) if e not in topo.engines(T.cores[r], dst)]
            for h in VIA:
                g.wait_ge(T.sem["a1h%d" % h], len(into))
                g.remote_dma(T.au1[:, 1024 * h:1024 * h + 1024], T.au0[:, 1024 * h:1024 * h + 1024], T.sem["a1h%d" % h], T.sem["lo0"],
                             pid, rid, topo.mask(core, dst))
            g.wait_ge(T.sem["lo0"], len(VIA) * len(topo.engines(core, dst)))


def build(rank, core, T, topo):
    ops, step = [], ["first"]
    free = {"rf": 0, "rb": 0, "ri": 0, "wu": 0, "wf": 0, "cf": 0}

    def R(a):
        if not isinstance(a, tuple):
            return a
        if a[0] == "ind":
            return R(a[1]).indirect(R(a[2]))
        if a[0] == "raw":
            return a[4](T[a[1]])
        p = a[5]
        rows = slice(None) if p is None else slice(p[0], p[1], p[2] if len(p) > 2 else None)
        return T[a[1]][rows, slice(a[2], a[3], a[4] if a[4] != 1 else None)]

    def new(buf, n):
        lo = free[buf]
        free[buf] = lo + (n + 15) // 16 * 16
        assert free[buf] <= SCRATCH[buf][1][1], buf
        return ap(buf, lo, lo + n)

    def add(eng, emit, outs, ins, cost, lat=None, sem=None, cnt=0, after=()):
        rd, wr = [], []
        for a in ins:
            rd += regions(a)
        for a in outs:
            if isinstance(a, tuple) and a[0] == "ind":
                wr += regions(a[1])
                rd += regions(a[2])
            else:
                wr += regions(a)
        ops.append({"eng": eng, "step": step[0], "emit": emit, "rd": rd, "wr": wr, "cost": cost, "lat": cost if lat is None else lat,
                    "sem": sem, "cnt": cnt, "after": list(after),
                    "kind": "s" if any(a[0] == "ind" for a in outs) else "g" if any(isinstance(a, tuple) and a[0] == "ind" for a in ins) else ""})
        return len(ops) - 1

    def vcost(out, ins, two=False):
        n = max(count(out), count(ins[0]))
        if out[0] == "ind":
            c = 3.8 * n
        elif ins[0][0] == "ind":
            c = 1.56 * n
        elif two:
            c = n * (1 if any(in_psum(a) for a in ins) else 2)
        else:
            c = n * (1 if any(wide(a) for a in [out] + ins) else 0.5)
        return max(c, 64) * CY + 0.03

    def room(out, a):
        return new(out, count(a)) if isinstance(out, str) else out

    def cp(out, a):
        out = room(out, a)
        add("V", lambda g: g.vector.tensor_copy(R(out), R(a)), [out], [a], vcost(out, [a]))
        return out

    def tt(out, a, b, op):
        out = room(out, a)
        add("V", lambda g: g.vector.tensor_tensor(R(out), R(a), R(b), op), [out], [a, b], vcost(out, [a, b], True))
        return out

    def ts(out, a, s1, op0, s2=None, op1=None):
        out = room(out, a)
        if op1 is None:
            add("V", lambda g: g.vector.tensor_scalar(R(out), R(a), R(s1), None, op0), [out], [a, s1], vcost(out, [a]))
        else:
            add("V", lambda g: g.vector.tensor_scalar(R(out), R(a), R(s1), R(s2), op0, op1), [out], [a, s1, s2], vcost(out, [a]))
        return out

    def scan(out, a, b, init, op0, op1):
        out = room(out, a)
        add("V", lambda g: g.vector.tensor_tensor_scan(R(out), R(a), R(b), R(init), op0, op1), [out], [a, b, init], vcost(out, [a, b]))
        return out

    def ms(out, v):
        add("V", lambda g: g.vector.memset(R(out), v), [out], [], vcost(out, [out]))
        return out

    def act(out, a, func, bias=0.0, scale=1.0, total=None, on_v=False):
        out = room(out, a)
        c = max(count(a) * (1.56 if a[0] == "ind" else 1), 64) * CY + 0.05
        if total is None:
            i = add("S", lambda g: g.scalar.activation(R(out), R(a), func, bias=R(bias), scale=R(scale)), [out], [a, bias, scale], c)
            if func in (AF.Copy, AF.Identity) and not in_psum(a) and not in_psum(out):
                ops[i]["alt"] = lambda g: g.vector.tensor_scalar(R(out), R(a), R(scale), R(bias), ALU.mult, ALU.add)
                if on_v:
                    ops[i].update({"eng": "V", "emit": ops[i]["alt"], "alt": ops[i]["emit"]})
        else:
            add("S", lambda g: g.scalar.activation(R(out), R(a), func, bias=R(bias), scale=R(scale), accum_out=R(total)),
                [out, total], [a, bias, scale], c + 0.02)
        return out

    def lin_(out, a, scale, bias):
        return act(out, a, AF.Identity, bias, scale)

    def take(out, a, on_v):
        return act(out, a, AF.Copy, on_v=on_v)

    def mm(out, terms):
        for k, grp in enumerate(terms):
            grp = grp if isinstance(grp, list) else [grp]
            c = sum(max(64, count(e[1])) * (4 if wide(e[1]) else 1) * CY * OPT["pf"] for e in grp)

            def emit(g, grp=grp, k=k):
                for q, e in enumerate(grp):
                    ins = g.tensor.matmul(R(e[2] if len(e) > 2 else out), R(e[0]), R(e[1]), k == 0 and q == 0,
                                          k == len(terms) - 1 and q == len(grp) - 1)
                return ins
            add("P", emit, [out], [a for e in grp for a in e[:2]], c, c + 0.06)
        return out

    def keep(out, a, pat, op, other, base, cm, after=()):
        out = room(out, a)
        add("G", lambda g: g.affine_select(R(out), R(a), pat, op, other, base, cm), [out], [a], 0.17 + 2 * count(out) * CY, after=after)
        return out

    def iota(out, pat, base, cm, after=()):
        if SCRATCH[out[1]][2] == I32:
            add("G", lambda g: g.iota(R(out), pat, base, cm), [out], [], 0.13 + 2 * count(out) * CY)
        else:
            add("G", lambda g: g.iota(R(out), pat, base, cm, allow_small_or_imprecise_dtypes=True), [out], [], 0.13 + 2 * count(out) * CY, after=after)
        return out

    def const(out, v, after=()):
        return iota(out, [[0, count(out)]], v, 0, after)

    nd = [0]

    def dma(pairs, outs, ins, lat, eng="Y"):
        s = "d%d" % nd[0]
        nd[0] += 1

        def emit(g):
            q = g.sync if eng == "Y" else g.scalar
            for o, i in pairs:
                q.dma_start(o(), i()).then_inc(T.sem[s], 16)
        return add(eng, emit, outs, ins, 0.08 * len(pairs), lat, s, 16 * len(pairs))

    nl = [0]

    def send(items, lat, gate=(), after=()):
        s = "lo%d" % nl[0]
        nl[0] += 1

        def emit(g):
            if len(items) == 1:
                src, dst, c, es, rs = items[0]
                rid, pid, _se = topo.addr(c)
                g.remote_dma(R(dst), R(src), T.sem[rs], T.sem[s], pid, rid, sum(1 << e for e in es))
            else:
                tr = []
                for src, dst, c, es, rs in items:
                    rid, pid, _se = topo.addr(c)
                    tr.append(RemoteDMATransfer(dst_ids=[DstId(rid=rid, pnc=pid)], dma_engine_mask=sum(1 << e for e in es),
                                                remote_sem=T.sem[rs], src=R(src), dst=R(dst)))
                g.remote_dma_fused(tr, local_sem=T.sem[s])
        return add("G", emit, [], [it[0] for it in items] + list(gate), 0.6, lat, s, sum(len(it[3]) for it in items), after)

    def recv(dst, sem, cnt, after, lat):
        return add(None, None, [dst], [], 0.0, lat, sem, cnt, after)

    C = T.cores
    nxt, prv = C[(rank + 1) % N], C[(rank - 1) % N]

    def same(a, b):
        return topo.chip(C[a % N]) == topo.chip(C[b % N])

    def relayed(r):
        return same(r, r + 1) and not same(r, r + 2)

    def small(r):
        return topo.engines(C[r % N], C[(r + 1) % N])[:8]

    au = ["au0", "au1", "au2"]
    lni, spi, gui = ap("lni", 0, 256, 1, (0, 8)), ap("spi", 0, 256), ap("gui", 0, 256)
    dma([(lambda: R(lni), lambda: T.lens[:])], [lni], [], 1.6, "S")
    for h in range(4):
        a = ap("au0", 1024 * h, 1024 * h + 1024)
        s = dma([(lambda a=a: R(a), lambda h=h: T.aud[:, 1024 * h:1024 * h + 1024])], [a], [], OPT["aud"][0] + OPT["aud"][1] * h)
        ops[s]["after"] = [s - 1] if h else []
    dma([(lambda: R(spi), lambda: T.spots[:])], [spi], [], 2.0, "S")
    ops[dma([(lambda: R(gui), lambda: T.gua[:])], [gui], [], OPT["aud"][0] + 3 * OPT["aud"][1] + 0.4)]["after"] = [s]
    mine, theirs = helper(rank, T, topo), helper(rank + 1, T, topo)
    s = None
    for h in range(4):
        a0, a1 = ap("au0", 1024 * h, 1024 * h + 1024), ap("au1", 1024 * h, 1024 * h + 1024)
        if mine is not None and h in VIA:
            item = (a0, a0, mine, [e for e in topo.engines(core, mine) if e not in topo.engines(core, prv)], "a1h%d" % h)
        else:
            item = (a0, a1, prv, topo.engines(core, prv), "a1h%d" % h)
        s = send([item], OPT["l0"], after=[] if s is None else [s])
        recv(a1, "a1h%d" % h, len(topo.engines(theirs if theirs is not None and h in VIA else nxt, core)), [s], OPT["l1"] + OPT["aud"][1] * (3 - h))

    s1 = s
    late = [s1]
    pi = iota(new("ri", 1), [[0, 1]], 0, 1)
    pcol = iota(new("wf", 1), [[0, 1]], 0, 1)
    JB = iota(new("cf", 128), [[16, 8], [0, 16]], 0, 0)
    RB = iota(new("rb", 384), [[0, 24], [2048, 16]], 0, 0)
    J = iota(new("cf", 128), [[1, 128]], 0, 0)
    JH, PCR, CROW = new("cf", 128), new("cf", 1040), new("rf", 256)
    const(ap("xa", 4096, 4352), 0, late)
    const(ap("xb", 4096, 4352), 0, late)
    J16, J128 = sub(J, 0, 16), sub(J, 0, 128)
    FL = ap("fl", 0, 4352)
    ZERO = ms(new("rb", 256), 0.0)
    B8 = sub(new("rf", 128), 0, 128, 1, (0, 8))
    ts(B8, sub(JB, 0, 128, 1, (0, 8)), 1.0 / 16, ALU.mult, sub(pcol, 0, 1, 1, (0, 8)), ALU.is_equal)
    icol = cp("wf", ts("ri", pi, 15, ALU.bitwise_and))
    g16 = tt("wf", pcol, icol, ALU.subtract)
    AM = ts("rb", RB, lin_("wf", icol, 2048.0, 0.0), ALU.is_equal, BIG, ALU.mult)
    JJ = lin_("wf", sub(J, 0, 24), 16.0, icol)
    C16 = sub(JJ, 0, 16)
    DUM = lin_("wf", C16, 1.0, 4096.0)
    fs, fg = OPT["fl"]
    ms(sub(FL, 0, max(fs, 512)), 1.0)
    fm = max(fs, 512)
    if fs:
        act(sub(FL, fm, fm + fs), sub(FL, 0, fs), AF.Copy)
    if fg:
        const(sub(FL, fm + fs, fm + fs + fg), 1)
    fm += fs + fg
    for a in range(fm, 4096, 1216):
        ms(sub(FL, a, min(a + 1216, 4096)), 1.0)
    IF = ts("cf", J128, pcol, ALU.is_equal)
    BO = ts("cf", JB, g16, ALU.is_equal)
    BOP = lin_("rb", BO, 0.5, 0.0)
    BON = lin_("rb", BO, -0.5, 0.0)
    NIF = keep("cf", IF, [[-1, 128]], ALU.not_equal, -1.0, 0, 1, late)
    LS = keep("cf", BO, [[1, 128]], ALU.is_gt, 0.0, 0, -1, late)
    LI = keep("cf", BO, [[1, 128]], ALU.is_ge, 0.0, 0, -1, late)
    i15 = act("wf", icol, AF.Relu, -14.0)
    hc = lin_("wf", i15, -HOLD, HOLD)
    Z = const(new("rb", 144), 0)
    ts(sub(Z, 15, 143, 16), sub(JB, 0, 128, 16), g16, ALU.is_equal, 1.0 / 32, ALU.mult)
    SEL = [sub(Z, 15 - a, 143 - a) for a in range(16)]
    Z2 = lin_("rb", Z, -2.0, 0.0) if OPT["two"] else None
    ni8k = lin_("wf", icol, -8192.0, 0.0)
    i256 = lin_("wf", icol, -256.0, -127.5)
    i256p = lin_("wf", icol, -256.0, -255.5)
    PT = new("wf", 32)
    lin_(sub(PT, 0, 32, 2), ts("wf", J16, icol, ALU.is_le), -2 * BIG - 8192.0, 8192.0)
    const(sub(PT, 1, 32, 2), 8192, late)
    JO = cp("wu", J16)
    JV = lin_("wf", C16, 16.0, lin_("wf", hc, -1.0, 18.0))
    CM = lin_("wf", C16, 1.0, float(E1 - G1))
    C272 = lin_("wf", C16, 1.0, 272.0)
    lin_(sub(C272, 15, 16), i15, -527.0, sub(C272, 15, 16))
    I4 = lin_("rb", IF, 0.25, 0.0)
    RST = const(new("wf", 16), 1, late)
    const(sub(RST, 0, 1), 0, late)
    ZP = const(new("wf", 16), 0, late)
    x0 = new("wf", 16)
    C2 = new("rb", 32)
    lin_(sub(C2, 0, 16), C16, 2.0, 0.0)
    lin_(sub(C2, 16, 32), C16, 2.0, 2.0)
    x1 = new("rb", 16)
    HBO = lin_("cf", BO, -0.5, 0.0)
    HLS = keep("rb", BON, [[1, 128]], ALU.is_gt, 0.0, 0, -1, late)
    HLI = keep("rb", BON, [[1, 128]], ALU.is_ge, 0.0, 0, -1, late)
    AH = new("rb", 384)
    tt(sub(AH, 0, 16), lin_("rb", sub(AM, 16, 32), 4.0, 0.0), lin_("rb", sub(AM, 15, 31), 2.0, 0.0), ALU.subtract)
    for lo, k in ((16, 3), (64, 5)):
        dma([(lambda a=a, lo=lo: R(sub(AH, a, a + lo)), lambda lo=lo: R(sub(AH, 0, lo))) for a in range(lo, lo + k * lo, lo)],
            [sub(AH, lo, lo + k * lo)], [sub(AH, 0, lo)], 4.0)
    for k in range(3):
        if k:
            const(ap(au[k], 4096, 4104), 1 << 21, late)
        if k == 2:
            Z8 = act(ap(au[k], 4104, 4112), sub(JB, 0, 8), AF.Silu, 0.0, 0.0)
            ops[-1]["cost"] = ops[-1]["lat"] = 1.4
        none = GB[k] + (384 if k == 2 and OPT["moved"] else 512)
        const(ap("nm", none, none + 16), 4096, late)
    END, CODE, NC, HD = new("rf", 257), new("rf", 257), new("rf", 257), new("rf", 257)
    WX, T1, T2 = new("rb", 272), new("rb", 272), new("rb", 272)
    lin_(sub(END, 0, 1), icol, 0.0, 0.0)
    const(sub(WX, 0, 288, 287), 0, late)
    const(sub(NC, 0, 1), 8192001, late)
    pc, pd, pv, pw, pe, pq, pa, pb = [ap("p%d" % k, 0, 512) for k in range(8)]

    def wrap(out, row):
        n = count(row)
        scan(sub(out, 0, n), sub(AM, 0, n), row, 0.0, ALU.add, ALU.min)
        return sub(out, 15, n, 16)

    def hold(out, row):
        n = count(row)
        scan(sub(out, 0, n), sub(AH, 0, n), row, 0.0, ALU.add, ALU.min)
        return sub(out, 15, n, 16)

    def unwrap(out, w, mx, ps, plus=0.0):
        for a in range(0, 256, OPT["half"]):
            b = a + OPT["half"]
            mm(sub(ps, a, b), [(BO, tt(sub(mx, a, b), ind(w, sub(JO, a // 16, b // 16)), sub(AM, a, b), ALU.mult))])
        return lin_(out, ps, 1.0 / BIG, plus)

    def strew(w, row, t):
        i = add("S", lambda g: g.scalar.activation(R(w), R(row), AF.Silu), [w], [row, Z8], 0.97)
        ops[i]["alt"] = lambda g: g.vector.tensor_copy(R(w), R(row))

    def fill(w, n, offs, t):
        strew(ind(w, offs), CROW, t)
        scan(sub(FIB, 0, n), sub(w, 0, n), sub(w, 0, n), 0.0, ALU.max, ALU.max)
        return wrap(WAB, sub(FIB, 0, n))

    def pick(row):
        return [(SEL[a], sub(row, a, 256, 16)) for a in range(16)]

    SPU = cp("wu", spi)
    lnf = cp(sub(new("rf", 256), 0, 256, 1, (0, 8)), lni)
    pn = mm(sub(pa, 0, 256), [(B8, lnf)])
    scan(sub(END, 1, 257), pn, ZERO, 0.0, ALU.add, ALU.add)
    W0 = new("cf", 512)
    endw = wrap(sub(W0, 0, 256), sub(END, 1, 257))
    begw = wrap(sub(W0, 256, 512), sub(END, 0, 256))
    cum0 = sub(W0, 15, 512, 16)
    WA, WB, WC, WD = new("rf", 384), new("rf", 256), new("rf", 256), new("rf", 256)
    first = tt("wf", tt("wf", tt("wf", endw, begw, ALU.is_equal), DUM, ALU.mult), begw, ALU.max)
    SO = cp("wu", first)
    NG = cp(ap("db", 4096, 4352), gui)
    cp(ind(FL, SO), ZERO)
    ci = cp("ri", cum0)
    UO = {e: cp("wu", ts("ri", sub(ci, 0, 16), 255, ALU.bitwise_and, e - 1, ALU.arith_shift_right)) for e in sorted(set(OPT["every"]))}
    LT = act("rb", END, AF.Sign, i256p)
    EQ = ts("rb", act(WD, sub(END, 1, 257), AF.Abs, i256), 128.0, ALU.is_lt, 2.0, ALU.mult)
    nw0 = tt("wf", endw, begw, ALU.subtract)
    beg32 = lin_("wf", begw, 2.0, 32.0)
    begO = lin_("wf", begw, 1.0, A0)
    DUMO = lin_("wf", C16, 1.0, 4096.0 + A0 + 1)
    SG1, SGN = new("rb", 256), new("rb", 256)
    act(SG1, NG, AF.Sign, 0.5, -1.0)
    zw = ts("wf", mm(sub(pe, 0, 16), [pick(SG1)]), -1.0 / 32, ALU.is_lt)
    if 2 in OPT["every"]:
        stat1 = tt("wf", first, tt("wf", zw, nw0, ALU.min), ALU.subtract)
        stat = lin_("wf", stat1, 1.0, -15.0 / 32) if OPT["every"][0] == 2 else None
        halves = ts("ri", ci, 1, ALU.arith_shift_right)
        half = lin_("wf", tt("wf", sub(halves, 0, 16), sub(halves, 16, 32), ALU.add), 1.0, lin_("wf", icol, -16384.0, 0.0))
        last = tt("wf", lin_("wf", endw, 1.0, -1.0), first, ALU.max)
    if 1 in OPT["every"]:
        HIF = lin_("cf", IF, -0.5, 0.0)
        whole = tt("wf", lin_("wf", nw0, -0.5, lin_("wf", icol, 8192.0, 0.0)), zw, ALU.subtract)
    if OPT["every"][0] == 2:
        dma([(lambda: T.da[:, 4096:4352], lambda: R(NG))], [ap("da", 4096, 4352)], [NG], 4.0)

    SPF = cp(WB, spi)
    for h in range(2):
        o = sub(pb, 128 * h, 128 * h + 128)
        i_ = sub(SPF, h, 256, 2)
        add("P", lambda g, o=o, i_=i_: g.tensor.transpose(R(o), R(i_), R(IF)), [o], [i_, IF], 0.45, 0.5)
        act(raw("st3", 0, 256, lambda t, h=h: t[:, :, h, :], 128), o, AF.Copy)
    WIN = ap("zf", 544, 4656)
    lin = ap("lin", 0, 4128)
    zp8 = sub(ZP, 0, 16, 1, (0, 8))
    pairs = [(lambda g_=g_: T.lin[g_, 16:4112], lambda g_=g_: T.st3[:, g_, :, :]) for g_ in range(8)]
    dma(pairs + [(lambda a=a: T.lin[:, a:a + 16], lambda: R(zp8)) for a in (0, 4112)], [lin], [ap("st3", 0, 256), zp8], 4.0)
    got, turn = ap("au1", 0, 4096), ap("cs", 1, 2)
    lo, ways = 0 if relayed(rank - 1) else 3072, []
    if not relayed(rank - 2):
        by = rounds(rank, T, topo)
        ways = [send([(ap("au0", 1024 * h, 1024 * h + 1024), ap("au2", 1024 * h, 1024 * h + 1024), c, es, "a2d") for h, (c, es) in enumerate(by)],
                     10.7, after=[s1])]
        ops[ways[0]]["more"] = True
    early = OPT["early"]
    if early:
        dma([(lambda i=i: T.nm[i:128:16, NB:NB + 4112], lambda: T.lin[:, 16:4128]) for i in range(early)], [ap("nm", NB, NB + 4112, 2)], [lin], OPT["nm"])
    out = [send([(ap("au1", lo, 4096), ap("au2", lo, 4096), prv, topo.engines(core, prv), "a2h0")], 4.5, [turn, got])]
    dma([(lambda i=i: T.nm[i:128:16, NB:NB + 4112], lambda: T.lin[:, 16:4128]) for i in range(early, 16)], [ap("nm", NB + 1, NB + 4112, 2) if early else ap("nm", NB, NB + 4112), turn], [lin], OPT["nm"])
    recv(ap("au2", 0, 4096), "a2h0", sum(len(topo.engines(c, core)) for c in [nxt] + [c for c, _es in ([] if relayed(rank) else rounds(rank + 2, T, topo))]),
         out + ways, OPT["l2"])
    out = [s1] + out
    iota(JH, [[1, 128]], 128, 0, out)
    iota(CROW, [[16, 256]], 16, 0, out)
    const(ap("zf", 0, 256), 0, out)
    for h in range(2):
        const(ap("nm", PCB + 512 * h, PCB + 512 * h + 512), 0, out)
        iota(sub(PCR, 520 * h, 520 * h + 520), [[8192, 520]], 8192 * 520 * h - 4096, 0, out)
    S15 = keep("cf", BO, [[-16, 8], [0, 16]], ALU.is_equal, 0.0, -15, 1, out)
    BB = const(new("rb", 128), -1, out)
    keep(BB, BB, [[-16, 8], [0, 16]], ALU.is_ge, 0.0, 0, 1, out)
    keep(BB, BB, [[16, 8], [0, 16]], ALU.is_ge, 0.0, 15, -1, out)
    DM = keep("rb", BB, [[1, 128]], ALU.is_equal, 0.0, -1, -1, out)
    keep(DM, DM, [[-1, 128]], ALU.not_equal, 1.0, 0, 1, out)
    IB = keep("rb", DM, [[-1, 128]], ALU.is_equal, 0.0, 0, 1, out)
    S0 = keep("rb", BB, [[-1, 128]], ALU.is_equal, 0.0, -15, 1, out)
    CG = new("rb", 48)
    const(sub(CG, 0, 16), 0, out)
    const(sub(HD, 0, 1), 8400000, out)
    M256 = const(new("rb", 1), -1024, out)
    PC = ap("nm", PCB, PCB + 1024)

    XS, SG2 = new("rf", 256), new("rb", 256)
    FIL, BKG, MX, NA, NB2, BKR = [new("rf", n) for n in (256, 384, 256, 256, 256, 256)]
    FIB, WAB = new("rb", 384), new("rb", 384)
    SND = new("rf", 384)
    ZF = ap("zf", 0, 528)
    st = {"cum": cum0, "cw": endw, "dw": begw, "k": nw0, "l": nw0}

    def total(ps, plus, minus, on_pe):
        if on_pe:
            return mm(ps, [(IF, a) for a in plus] + [(NIF, a) for a in minus])
        a = plus[0]
        for b, op in [(b, ALU.add) for b in plus[1:]] + [(b, ALU.subtract) for b in minus]:
            a = tt("wf", a, b, op)
        return a

    def heavy(t):
        xs = ap(["xa", "xb"][t % 2], 0, 4352)
        d = ap(["da", "db"][t % 2], 0, 4352)
        tab = ap(au[t], 0, 4096)
        step[0] = "gather%d" % t
        for lo, hi, on_v in OPT["vg"][t]:
            act(sub(xs, 256 * lo, 256 * hi), ind(tab, sub(SPU, 16 * lo, 16 * hi)), AF.Identity, 0.0, -1.0, on_v=on_v)
        act(XS, ind(xs, SO), AF.Copy)
        tt(ind(xs, SO), XS, NG, ALU.add)
        terms, cuts, done, e = [], OPT["cuts"][t], 0, OPT["every"][t]
        n = 256 // e
        for lo, hi in zip(cuts[:-1], cuts[1:]):
            step[0] = "sums%d" % t
            if t == 0 and hi == 4096 and OPT["two"]:
                scan(ap("sg", lo, hi), ap("fl", lo, hi), sub(xs, lo, hi), sub(d, lo - 1, lo), ALU.mult, ALU.add)
                for a, b in zip(OPT["two"][:-1], OPT["two"][1:]):
                    ts(ap("sg", a, b), ap("sg", a, b), 0.5, ALU.is_gt, 0.5, ALU.subtract)
                    terms.append([(sub(Z2, 15 - q, 143 - q), ap("sg", 256 * q, 256 * q + 256)) for q in range(a // 256, b // 256)])
                continue
            scan(sub(d, lo, hi), ap("fl", lo, hi), sub(xs, lo, hi), 0.0 if lo == 0 else sub(d, lo - 1, lo), ALU.mult, ALU.add)
            if hi in OPT["sgn"][t]:
                step[0] = "signs%d" % t
                on_v = hi in OPT["vs"][t]
                if on_v:
                    ts(ap("sg", done // e, hi // e), sub(d, done + e - 1, hi, e), 0.5, ALU.is_gt, 0.5, ALU.subtract)
                else:
                    act(ap("sg", done // e, hi // e), sub(d, done + e - 1, hi, e), AF.Sign, 0.5, -1.0)
                terms.append([(sub(Z2 if on_v else Z, 15 - a, 143 - a), ap("sg", n * a, n * a + n)) for a in range(done // 256, hi // 256)])
                done = hi
        step[0] = "count%d" % t
        mm(sub(pc, 0, n), terms)
        tot = new("wf", 1)
        act(sub(SG2, 0, n), sub(pc, 0, n), AF.Sign, 1.0 / 32, 1.0, tot)
        scan(sub(WX, 1, n + 1), sub(SG2, 0, n), sub(ZERO, 0, n), 0.0, ALU.add, ALU.add)
        tt(sub(T1, 16, 272), ind(sub(WX, 0, n + 1), UO[e]), EQ, ALU.mult)
        lin_(sub(T2, 15, 272), LT, tot, 0.0)
        mm(sub(pd, 0, 256), [(BOP, sub(RB, 0, 256)), [(BON, sub(T2, 16, 272)), (BOP, sub(T2, 15, 271))], [(BON, sub(T1, 16, 272)), (BOP, sub(T1, 15, 271))]])
        if e == 1:
            return mm(sub(pd, 256, 272) if t else sub(pq, 0, 16), [[(IF, whole), (IF, st["l"])], (HIF, wrap(WC, sub(pd, 0, 256)))])
        q = tt("wf", tt("wf", tt("wf", wrap(WC, sub(pd, 0, 256)), half, ALU.add), last, ALU.min), first, ALU.max)
        act(SG2, ind(d, cp("wu", q)), AF.Sign, 0.5, -1.0)
        if t == 0:
            return mm(sub(pq, 0, 16), [[(IF, stat), (IF, nw0)], (NIF, q), pick(SG2)])
        under = ts("wf", mm(sub(pe, 32, 48), [pick(SG2)]), -1.0 / 32, ALU.is_lt)
        return mm(sub(pd, 256, 272), [[(IF, stat1), (IF, st["l"])], (NIF, q), (NIF, under)])

    def light(t, d):
        Gt = GB[t]
        cum, k = st["cum"], st["k"]
        m0, step[0] = 0.0, "released%d" % t
        if t == 0 and OPT["every"][0] == 2:
            d, m0 = lin_("wf", d, 1.0, RND), RND
        tab, dt = ap(au[t], 0, 4112 if t == 2 else 4104), ap(["da", "db"][t % 2], 0, 4352)
        if t:
            d = tt("wf", d, st["mq"], ALU.max)
        if t == 2:
            tt(SG1, ind(tab, st["EW0"]), act(NB2, ind(dt, st["VU0"]), AF.Copy), ALU.is_ge)
            under = ts("wf", mm(sub(pe, 16, 32), [pick(SG1)]), 7.5 / 32, ALU.is_lt)
            d = tt("wf", d, tt("wf", under, st["both"], ALU.min), ALU.subtract)
        rs = new("wf", 2)
        act(x0, d, AF.Relu, -m0, 1.0, sub(rs, 0, 1))
        e8 = act("rb", d, AF.Relu, 32768.0 * (m0 + 1), -32768.0)
        sc = scan("wf", sub(x0, -1, 15), RST, 0.0, ALU.add, ALU.mult)
        ex = mm(sub(pb, 0, 16), [(LS, x0), (I4, e8), (BO, sc)])
        mm(sub(pw, 0, 1), [(BO, sub(rs, 0, 1))])
        less = "t" in OPT["pe"][t]
        mm(sub(pv, 0, 16), [(LI, x0)] + [(NIF, st["cw"])] * less + [(BO, sc)])
        mm(sub(pv, 16, 32), [(LS, x0)] + [(NIF, st["dw"])] * less + [(BO, sc)])
        moved = t == 2 and OPT["moved"]
        if moved:
            mm(sub(pw, 2, 3), [(BO, sub(rs, 0, 1)), (I4, M256)])
            OU = tt("wf", ex, lin_("wf", C16, 1.0, 4352.0), ALU.min)
        else:
            OU = cp("wu", tt("wf", ex, DUM, ALU.min))
        step[0] = "short%d" % t
        if t:
            dk = ind(dt, st["VU"])
            if t == 2:
                na = tt(NB2, dk, act(NA, ind(tab, st["OZ"]), AF.Copy), ALU.subtract)
            else:
                na = act(NA, dk, AF.Copy)
            tt(SGN, ind(tab, st["EW"]), na, ALU.is_ge)
            terms = [(IF, d), pick(SGN)]
            act(x1, mm(sub(pq, 0, 16), terms[::OPT["mxl"][t]]), AF.Sign, 0.5 - C0, 1.0, sub(rs, 1, 2))
        else:
            act(x1, sub(pq, 0, 16), AF.Sign, 0.5, 1.0, sub(rs, 1, 2))
        mm(sub(pw, 1, 2), [(HBO, sub(rs, 1, 2))])
        s1 = scan("rb", sub(x1, -1, 15), RST, 0.0, ALU.add, ALU.mult)
        sh = sub(pq, 32, 64)
        mm(sub(sh, 0, 16), [[(I4, sub(C2, 16, 32)), (HLI, x1)], (BON, s1)])
        mm(sub(sh, 16, 32), [[(I4, sub(C2, 0, 16)), (HLS, x1)], (BON, s1)])
        by = 256.0 if moved else 0.0
        mn = ts("wf", sub(pw, 1, 2), 128.0 - by, ALU.add, sub(pw, 2, 3) if moved else sub(pw, 0, 1), ALU.min)
        cs, cn = ap("cs", 4 * t, 4 * t + 1), ap("cn", 4 * t, 4 * t + 1)
        ts(cs, sub(pw, 0, 1), mn, ALU.subtract, 128.0 + by, ALU.min)
        s = send([(cs, cn, nxt, small(rank), "rc%d" % t)], 0.65)
        recv(cn, "rc%d" % t, len(small(rank - 1)), [s], OPT["hop"])
        if moved:
            OU = ts("wu", OU, mn, ALU.subtract)
            idx = ts("wu", sub(sh, 16, 32), mn, ALU.subtract, 384.0, ALU.min)
            jj = lin_("wf", sub(JJ, 0, 24), 1.0, mn)
        else:
            SU = ts("wu", sub(JJ, 0, 8), mn, ALU.add)
            idx = tt("wf", ts("wf", sub(sh, 16, 32), mn, ALU.is_ge, lin_("wf", mn, -1.0, 384.0), ALU.mult), sub(sh, 16, 32), ALU.add)
            jj = sub(JJ, 0, 24)
        top = PCB + 1024 if t else PCB
        RU, parts, step[0] = new("wu", 24), ((16, 24), (0, 16)) if moved and OPT["split"] else ((0, 24),), "spots%d" % t
        if t == 0:
            kept = unwrap(sub(NC, 1, 257), tt("wf", endw, x0, ALU.subtract), MX, sub(pa, 0, 256), 32.0)
            const(ap("da", 0, 384), 0)
            strew(ind(ap("da", 0, 4352), OU), kept, 0)
            scan(BKG, const(FIB, 1), ap("da", 0, 384), 0.0, ALU.add, ALU.max)
            dma([(lambda: T.da[:, 4096:4352], lambda: R(NG))], [ap("da", 4096, 4352)], [NG], 3.0)
            for lo, hi in parts:
                w = wrap(sub(WA, 16 * lo, 16 * hi), sub(BKG, 16 * lo, 16 * hi))
                ts(sub(RU, lo, hi), w, -32.0, ALU.add, top - 1.0, ALU.min)
        else:
            off = total(sub(pv, 32, 48), st["b0"], [x0, act("wf", d, AF.Relu, TW * (TC + m0), -TW)], "o" in OPT["pe"][t])
            unwrap(sub(NC, 1, 257), tt("wf", ts("wf", sub(ex, 0, 16), TW - 1, ALU.mult), off, ALU.add), MX, sub(pa, 0, 256))
            zo = 768 - 384 * t
            if t == 1:
                const(ap("xb", 384, 768), 0)
                const(ap("xb", 0, 384), 0)
            c1 = fill(ap("xb", zo, 384 + 4864), 384, OU, t)
            cu = ts("wu", c1, 1.0 / 16, ALU.mult)
            base = A0 + PCB - 3
            cj = [(IF, lin_("wf", jj, TW, float(base) if t == 1 else lin_("wf", hc, -1.0, base))), (I4, c1)]
            if "f" not in OPT["pe"][t]:
                cj = mm(sub(pb, 16, 40), cj)
            if t == 2:
                cap = lin_("wf", c1, 0.25, 510.0 + PCB)
            for lo, hi in parts:
                row, wa = act(sub(BKG, 16 * lo, 16 * hi), ind(NC, sub(cu, lo, hi)), AF.Copy), sub(WA, 16 * lo, 16 * hi)
                if t == 1:
                    pf = wrap(wa, row)
                    p = cp("ri", pf)
                else:
                    pf = hold(wa, row)
                    p = ts("ri", pf, hc, ALU.add)
                if "f" in OPT["pe"][t]:
                    far = mm(sub(pb, 16, 40), cj + [(NIF, pf)])
                else:
                    far = tt("wf", sub(cj, lo, hi), pf, ALU.subtract)
                far = tt("wf", far, sub(jj, lo, hi), ALU.max)
                a = tt("wf", far, ts("ri", p, 8191, ALU.bitwise_and), ALU.add)
                if t == 2:
                    a = tt("wf", a, sub(cap, lo, hi), ALU.min)
                ts(sub(RU, lo, hi), a, -512.0, ALU.add, top - 1.0, ALU.min)
        snd, arr = sub(SND, 128 * t, 128 * t + 128), ap("nm", Gt + 384 - 128 * moved, Gt + 512 - 128 * moved)
        if moved:
            act(snd, ind(ap("nm", NB, top), sub(RU, 16, 24)), AF.Copy)
            act(ap("nm", Gt, Gt + 256), ind(ap("nm", NB, top), sub(RU, 0, 16)), AF.Copy)
        else:
            act(ap("nm", Gt, Gt + 384), ind(ap("nm", NB, top), RU), AF.Copy)
            act(snd, ind(ap("nm", Gt, Gt + 384), SU), AF.Copy)
        s = send([(snd, arr, nxt, small(rank), "rn%d" % t)], 0.8)
        recv(arr, "rn%d" % t, len(small(rank - 1)), [s], OPT["hop"])
        step[0] = "lengths%d" % t
        t1 = None if less else tt("wf", cum, sub(pv, 0, 32), ALU.subtract)
        gp = ts("wf", sh, mn, ALU.subtract, cn, ALU.min)
        t1 = tt("wf", gp, sub(pv, 0, 32), ALU.subtract) if less else tt("wf", t1, gp, ALU.add)
        cum = ts(sub(new("wf", 80), 0, 32), t1, mn, ALU.add, 4096.0, ALU.min)
        l = tt("wf", sub(cum, 0, 16), sub(cum, 16, 32), ALU.subtract)
        if t == 2:
            return idx, cum, l
        k = tt("wf", k, l, ALU.min)
        later = "o" in OPT["pe"][t + 1]
        bk = [begO, k] if later and "v" in OPT["pe"][t] else [tt("wf", begO, k, ALU.add)]
        m = tt("wf", l, k, ALU.subtract)
        if t == 0:
            gw = ap("nm", G0, G0 + 528)
            EN = ts("wu", tt("wf", act("wf", m, AF.Relu, 512.0, -512.0), idx, ALU.max), 512.0, ALU.min)
            en = ap("nm", E1, E1 + 256)
            st["cm"] = [lin_("wf", m, -TW, TW), CM]
            if "m" not in OPT["pe"][1]:
                st["cm"] = [total(None, st["cm"], [], False)]
            st["b0"] = [lin_("wf", m, 1 - TW, TW * TC)] + bk
        else:
            gw = ap("nm", E1, G1 + 528)
            df = tt("wf", m, st["m"], ALU.subtract)
            ix = tt("wf", act("wf", df, AF.Relu, 512.0, -512.0), idx, ALU.max)
            old = total(sub(pb, 48, 64), st["cm"] + [act("wf", df, AF.Abs, 0.0, TW)], [], "m" in OPT["pe"][1])
            EN = ts("wu", tt("wf", old, ix, ALU.min), 256.0, ALU.add, 768.0, ALU.min)
            en = sub(PC, 2, 1024, 4)
            both = st["both"] = act("wf", m, AF.Relu, -TW, TW)
            st["EW0"], st["VU0"] = st["EW"], st["VU"]
            st["OZ"] = ts("wu", tt("wf", st["en"], both, ALU.mult), 1.0 / TW, ALU.mult, 4104.0, ALU.add)
            st["no"] = new("wf", 32)
            lin_(sub(st["no"], 0, 16), both, -0.5 / TW, 0.5)
            act(sub(st["no"], 16, 32), m, AF.Relu, 0.5, -0.5)
            st["b0"] = [lin_("wf", m, 1 - 1.5 * TW, TW * TC), both] + bk
            unwrap(BKR, tt("wf", begO, l, ALU.add), MX, sub(pa, 0, 256))
        st["mq"] = lin_("wf", m, 1.0, -1.0)
        act(en, ind(gw, EN), AF.Copy)
        ew = hold(WD, en)
        st["EW"] = ts("wu", ew, hc, ALU.add)
        if t == 0:
            st["en"] = ts("wf", ew, hc, ALU.add, -4104.0, ALU.add)
            if OPT["e1g"]:
                keep(sub(PC, 1, 1024, 4), en, [[0, 256]], ALU.is_ge, 0.0, 0, 0)
            else:
                act(sub(PC, 1, 1024, 4), en, AF.Copy)
        if not later:
            st["b0"] = [total(None, st["b0"], [], False)]
        zz = total(sub(pb, 64, 80), bk + [act("wf", k, AF.Relu, 8192.0, -8192.0)], [], "v" in OPT["pe"][t])
        st["VU"] = ts("wu", tt("wf", zz, DUMO, ALU.min), -A0 - 1, ALU.add)
        st.update({"cum": cum, "cw": sub(cum, 0, 16), "dw": sub(cum, 16, 32), "k": k, "l": l, "m": m})
        return None

    def final(idx, cum, l):
        PEN, PS, step[0] = ap("xb", 1024, 2048), ap("xb", 2048, 3072), "last"
        cw, dw = sub(cum, 0, 16), sub(cum, 16, 32)
        u3 = new("wf", 48)
        u = tt(sub(u3, 32, 48), dw, st["l"], ALU.add)
        code = unwrap(NB2, u, MX, sub(pa, 0, 256))
        q32 = ts("ri", cum, 0.0625, ALU.mult, -0.46875, ALU.add)
        pe_, pq_ = sub(q32, 0, 16), sub(q32, 16, 32)
        OU = cp("wu", tt("wf", tt("wf", tt("wf", pq_, pe_, ALU.is_equal), C272, ALU.mult), pq_, ALU.max))
        for s in range(3):
            if s < 2:
                lin_(sub(u3, 16 * s, 16 * s + 16), u, 1.0, s - 2.0)
            if OPT["three"]:
                mm(sub(pe, 64 + 16 * s, 80 + 16 * s), [(IF, cw)])
            else:
                tt(sub(cum, 32 + 16 * s, 48 + 16 * s), sub(u3, 16 * s, 16 * s + 16), cw, ALU.min)
        if OPT["three"]:
            tt(sub(cum, 32, 80), u3, sub(pe, 64, 112), ALU.min)
        tt(sub(cum, 32, 64), sub(cum, 32, 64), st["no"], ALU.add)
        r4 = ts("ri", ts("ri", sub(cum, 16, 80), 2.0, ALU.mult), 31, ALU.bitwise_and)
        PU = cp("wu", r4)
        BU = ts("wu", tt("wf", beg32, sub(r4, 0, 16), ALU.subtract), 0.5, ALU.mult, 4111.0, ALU.min)
        c1 = fill(ZF, 256, OU, 3)
        cu = ts("wu", c1, 1.0 / 16, ALU.mult, -1.0, ALU.add)
        y = tt("wf", JV, hold(WA, take(FIL, ind(code, cu), OPT["pc"][2])), ALU.subtract)
        act(sub(BKG, 0, 256), ind(BKR, cu), AF.Copy)
        c4, gifts = lin_(sub(CG, 16, 32), c1, 0.25, -4.0), ts(sub(CG, 32, 48), y, 0.0, ALU.max, 3.0, ALU.min)
        gu, gd = sub(pw, 80, 96), sub(pw, 96, 112)
        mm(sub(pw, 80, 112), [[(DM, sub(CG, 0, 32)), (IB, c4, gu), (S0, sub(CG, 15, 31), gd)], [(IB, gifts, gu), (DM, gifts, gd), (S0, sub(CG, 31, 47), gd)]])
        GU = ts("wu", sub(pw, 80, 112), 1024.0, ALU.min)
        GU, GD = sub(GU, 0, 16), sub(GU, 16, 32)
        AU = ts("wu", tt("wf", hold(WB, sub(BKG, 0, 256)), y, ALU.add), lin_("wf", hc, 1.0, 14.0 - A0), ALU.add, 4111.0, ALU.min)
        act(sub(HD, 1, 257), ind(WIN, AU), AF.Copy)
        for s in range(4):
            take(sub(PEN, s, 1024, 4), ind(PT, sub(PU, 16 * s, 16 * s + 16)), s < OPT["pen"])
        take(sub(PC, 0, 1024, 4), ind(WIN, BU), OPT["pc"][0])
        gift = ind(ap("nm", G2, G2 + 400), idx) if OPT["moved"] else ind(ap("nm", G2, G2 + 528), ts("wu", idx, 512.0, ALU.min))
        take(sub(PC, 3, 1024, 4), gift, OPT["pc"][1])
        scan(PS, PEN, PC, 0.0, ALU.add, ALU.max)
        o = sub(pe, 128, 256, 1, (0, 16))
        add("P", lambda g: g.tensor.transpose(R(o), R(l), R(IF)), [o], [l, IF], 0.45, 0.5)
        yn = act(sub(WD, 0, 128, 1, (0, 16)), o, AF.Copy)
        dma([(lambda g_=g_: T.yn[g_, :], lambda g_=g_: R(sub(yn, 16 * g_, 16 * g_ + 16, 1, (0, 16)))) for g_ in range(8)], [], [yn], 2.5)
        tcol = lin_("wf", mm(sub(pw, 8, 9), [(S15, sub(cw, 15, 16))]), 8192.0, ni8k)
        mk = lin_(sub(pc, 0, 256), act(NA, sub(J, 0, 256), AF.Relu, tcol, -131072.0), 1.0, -1.0)
        tt(sub(CODE, 0, 256), ind(PCR, GD), sub(HD, 0, 256), ALU.add)
        YO = XS
        for lo in range(0, 256, OPT["last"]):
            hi = lo + OPT["last"]
            h3 = tt(sub(gui, lo, hi), ind(PS, sub(GU, lo // 16, hi // 16)), sub(CODE, lo, hi), ALU.min)
            tt(sub(YO, lo, hi), ts(sub(spi, lo, hi), h3, 4095, ALU.bitwise_and), sub(mk, lo, hi), ALU.min)
            dma([(lambda lo=lo, hi=hi: T.yo[:, lo:hi], lambda lo=lo, hi=hi: R(sub(YO, lo, hi)))], [], [sub(YO, lo, hi)], 2.3, "Y" if lo else "S")

    def shifted(k, gate):
        lo, hi = OPT["parts"][k:k + 2]
        if hi > lo:
            dma([(lambda i=i: T.zf[i:128:16, 544:4656], lambda i=i: T.lin[:, i:i + 4112]) for i in range(lo, hi)],
                [ap("zf", 544 + k, 4656, 3), gate], [lin], 8.0)

    light(0, heavy(0))
    shifted(0, ap("cs", 0, 1))
    shifted(1, sub(SND, 0, 128))
    light(1, heavy(1))
    shifted(2, ap("cs", 4, 5))
    final(*light(2, heavy(2)))
    OPT["used"] = dict(free)
    return ops


def order(ops):
    n = len(ops)
    seen = {}
    for i, o in enumerate(ops):
        if o["sem"] is None and "slow" not in o:
            o["slow"] = (SLOW - 1) * o["cost"]
            o["cost"], o["lat"] = o["cost"] + o["slow"], o["lat"] + o["slow"]
        soft = set(o["after"])
        hard = set()
        for kind, regs in (("r", o["rd"]), ("w", o["wr"])):
            for (b, lo, hi, sp) in regs:
                ps = SCRATCH[b][0] == "psum"
                for (j, k2, l2, h2, s2) in seen.get(b, []):
                    hit = l2 < hi and lo < h2 and (kind == "w" or k2 == "w") and not (sp == s2 and (lo - l2) % sp)
                    if ps and ops[j]["eng"] == "P" and o["eng"] == "P":
                        soft.add(j)
                    elif j != i and hit or (ps and ops[j]["eng"] != o["eng"]):
                        hard.add(j)
        for kind, regs in (("r", o["rd"]), ("w", o["wr"])):
            for (b, lo, hi, sp) in regs:
                seen.setdefault(b, []).append((i, kind, lo, hi, sp))
        o["deps"] = sorted(soft | hard)
        o["hard"] = sorted(hard)
    succ = [[] for _ in range(n)]
    for i, o in enumerate(ops):
        for j in o["deps"]:
            succ[j].append(i)
    lev = [0.0] * n
    for i in range(n - 1, -1, -1):
        lev[i] = ops[i]["lat"] + HOP + max([lev[s] for s in succ[i]] + [0.0])
    cost = [max(o["cost"], 1e-3) for o in ops]
    lag = {}
    for i, o in enumerate(ops):
        for j in o["deps"]:
            soft = j not in o["hard"] and ops[j]["eng"] == o["eng"]
            lag[j, i] = cost[j] if soft else max(ops[j]["lat"], cost[j]) + HOP

    pre = [[(j, lag[j, i]) for j in ops[i]["deps"]] for i in range(n)]
    post = [[(k, cost[k] + lag[i, k] - cost[i]) for k in succ[i]] for i in range(n)]
    tail = [ops[i]["lat"] - cost[i] for i in range(n)]
    eng = [o["eng"] for o in ops]

    def place(key, back):
        before = post if back else pre
        key = list(key)
        for i in (range(n - 1, -1, -1) if back else range(n)):
            for j, _w in before[i]:
                if key[i] <= key[j]:
                    key[i] = key[j] + 1e-6
        at = [0.0] * n
        used = {e: ([], []) for e in eng}
        for i in sorted(range(n), key=lambda c: key[c]):
            s = tail[i] if back else 0.0
            for j, w in before[i]:
                if at[j] + w > s:
                    s = at[j] + w
            if eng[i] is not None:
                lo, hi = used[eng[i]]
                q = len(lo)
                while q and hi[q - 1] > s + 1e-9:
                    q -= 1
                while q < len(lo) and lo[q] < s + cost[i] - 1e-9:
                    s = max(s, hi[q])
                    q += 1
                lo.insert(q, s)
                hi.insert(q, s + cost[i])
            at[i] = s
        return at

    def span(at):
        return max(at[i] + ops[i]["lat"] for i in range(n))

    if "t" not in KNOWN:
        rng = np.random.default_rng(OPT["seed"])
        at = place([-v for v in lev], False)
        best = (span(at), at)
        kinds = sorted(set((o["step"], o["eng"]) for o in ops if o["eng"] in ("V", "S")))
        for it in range(OPT["tries"]):
            mid, half, amp = rng.random() * best[0], 2 + 12 * rng.random(), 4 * rng.random()
            noise = rng.random(n) * amp
            if it % 2:
                by = {kinds[int(rng.random() * len(kinds))]: OPT["move"] * (2 * rng.random() - 1) for _k in range(1 + it % 4 // 2)}
                at = place([t + by.get((o["step"], o["eng"]), 0.0) for o, t in zip(ops, best[1])], False)
            else:
                at = place([t + (noise[i] if abs(t - mid) < half else 0.5 * amp) for i, t in enumerate(best[1])], False)
            bk = place([-(at[i] + cost[i]) for i in range(n)], True)
            at = place([-(bk[i] + cost[i]) for i in range(n)], False)
            end = span(at)
            if end <= best[0] + 0.02:
                best = (end, at)
        KNOWN["t"], OPT["mid"] = best[1], round(best[0], 1)
        for rounds, hot in OPT["plan"]:
            at = improve(ops, eng, pre, KNOWN["t"], rng, rounds, hot)
            for _k in range(3):
                bk = place([-(at[i] + cost[i]) for i in range(n)], True)
                new = place([-(bk[i] + cost[i]) for i in range(n)], False)
                at = new if span(new) <= span(at) else place(at, False)
            KNOWN["t"] = at
        OPT["ends"] = round(span(at), 1)
        KNOWN["t"] = list(zip(KNOWN["t"], eng))
        KNOWN["few"] = [t for t, o in zip(KNOWN["t"], ops) if "more" not in o]
    at = KNOWN["t" if n == len(KNOWN["t"]) else "few"]
    assert len(at) == n
    for o, (t, e) in zip(ops, at):
        if e != o["eng"]:
            o["emit"] = o["alt"]
        o["t"], o["eng"] = t, e
    return sorted(range(n), key=lambda i: (at[i][0], i))


def shorten(seq, eng, case, rng, steps):
    before, cost, lat = case
    n = len(seq)
    after = [[] for _ in range(n)]
    for i in range(n):
        for j, w in before[i]:
            after[j].append((i, w))
    need = [len(b) for b in before]
    up, down, last = [-1] * n, [-1] * n, {}
    for i in seq:
        if eng[i] is not None:
            p = last.get(eng[i], -1)
            up[i] = p
            if p >= 0:
                down[p] = i
            last[eng[i]] = i

    def times():
        left = [need[i] + (up[i] >= 0) for i in range(n)]
        free, head, line = [0.0] * n, [0.0] * n, [i for i in range(n) if not left[i]]
        for i in line:
            s, p = free[i], up[i]
            if p >= 0 and head[p] + cost[p] > s:
                s = head[p] + cost[p]
            head[i] = s
            for k, w in after[i]:
                if s + w > free[k]:
                    free[k] = s + w
                left[k] -= 1
                if not left[k]:
                    line.append(k)
            k = down[i]
            if k >= 0:
                left[k] -= 1
                if not left[k]:
                    line.append(k)
        rest, tail = [0.0] * n, [0.0] * n
        for i in reversed(line):
            s = lat[i]
            for k, w in after[i]:
                if tail[k] + w > s:
                    s = tail[k] + w
            rest[i] = s
            k = down[i]
            if k >= 0 and tail[k] + cost[i] > s:
                s = tail[k] + cost[i]
            tail[i] = s
        return free, head, rest, tail, line

    best, barred, since = (1e9, None, None, None), {}, 0
    draw = rng.random((steps, 3)).tolist()
    for it in range(steps):
        free, head, rest, tail, line = times()
        end = max(tail)
        if end < best[0] - 1e-6:
            best, since = (end, up[:], down[:], sorted(line, key=lambda i: head[i])), it
        elif it - since > OPT["back"]:
            up[:], down[:], since, barred = best[1], best[2], it, {}
            continue
        tops = [i for i in range(n) if head[i] == 0.0 and tail[i] > end - 1e-6]
        i, runs = tops[int(draw[it][0] * len(tops))], []
        cur, flip = [i], draw[it][1] < 0.5
        while True:
            k = down[i]
            on = k >= 0 and tail[k] + cost[i] > tail[i] - 1e-7
            off = [c for c, w in after[i] if tail[c] + w > tail[i] - 1e-7]
            if on and (flip or not off):
                cur.append(k)
            elif off:
                runs.append(cur)
                k = off[0]
                cur = [k]
            else:
                runs.append(cur)
                break
            i = k
        pick = (1e9, None, None)
        for run in runs:
            m = len(run)
            for a in range(m - 1):
                u = run[a]
                p = up[u]
                start = head[p] + cost[p] if p >= 0 else 0.0
                for b in range(a + 1, min(m, a + OPT["far"])):
                    if a and b < m - 1 and b > a + 1:
                        continue
                    v = run[b]
                    part = run[a:b + 1]
                    k = down[v]
                    for new in ([v] + part[:-1], part[1:] + [u]) if b > a + 1 else ([v, u],):
                        if new[0] == v:
                            lim = head[u] + cost[u] - 1e-9
                            if any(head[j] >= lim or j == u for j, _w in before[v]):
                                continue
                        elif any(tail[c] >= tail[v] + cost[c] - 1e-9 or c == v for c, _w in after[u]):
                            continue
                        s, hs = start, []
                        for c in new:
                            if free[c] > s:
                                s = free[c]
                            hs.append(s)
                            s += cost[c]
                        q, est = (tail[k] if k >= 0 else -1e9), 0.0
                        for c in reversed(new):
                            q += cost[c]
                            if rest[c] > q:
                                q = rest[c]
                            s = hs.pop() + q
                            if s > est:
                                est = s
                        if est < pick[0] and (est < best[0] - 1e-6 or not any(
                                barred.get((v, c) if new[0] == v else (c, u), -1) > it for c in part)):
                            pick = (est, new, part)
        if pick[1] is None:
            barred = {}
            continue
        _e, new, part = pick
        p, k = up[part[0]], down[part[-1]]
        for c in new:
            up[c] = p
            if p >= 0:
                down[p] = c
            p = c
        down[p] = k
        if k >= 0:
            up[k] = p
        until = it + OPT["bar"] + int(draw[it][2] * OPT["bar"])
        for c in part:
            barred[(c, part[-1]) if new[0] == part[-1] else (part[0], c)] = until
    OPT["mid"] = round(best[0], 1)
    return best[3]


def improve(ops, eng, pre, at, rng, rounds, hot):
    n = len(ops)
    anc, lean = [0] * n, []
    for i in range(n):
        far = 0
        for j, _w in pre[i]:
            far |= anc[j]
            anc[i] |= anc[j] | (1 << j)
        lean.append([j for j, _w in pre[i] if not (far >> j & 1) or ops[j]["sem"] is not None])
    cases = []
    for gather, scatter, slow, hop, dma in CASES:
        cost = [max(o["cost"], 1e-3) if o["sem"] else slow * (0.04 + (o["cost"] - 0.04) * {"g": gather, "s": scatter, "": 1.0}[o["kind"]]) for o in ops]
        lat = [o["lat"] * dma if o["sem"] else c + o["lat"] - o["cost"] for o, c in zip(ops, cost)]
        before = [[(j, cost[j] if j not in o["hard"] and eng[j] == o["eng"] else max(lat[j], cost[j]) + hop) for j in lean[i]]
                  for i, o in enumerate(ops)]
        after = [[] for _ in range(n)]
        for i in range(n):
            for j, w in before[i]:
                after[j].append((i, w))
        cases.append((before, cost, lat, after))

    def run(seq, case, a=0, old=None):
        before, cost, lat, _after = case
        t, by = (old[1][:], old[2][:]) if a else ([0.0] * n, [-1] * n)
        free = {eng[i]: i for i in seq[:a]}
        end, last = 0.0, -1
        for i in seq[a:]:
            s, b = 0.0, -1
            for j, w in before[i]:
                if t[j] + w > s:
                    s, b = t[j] + w, j
            e = eng[i]
            if e is not None:
                p = free.get(e)
                if p is not None and t[p] + cost[p] > s:
                    s, b = t[p] + cost[p], -2 - p
                free[e] = i
            t[i], by[i] = s, b
            if s + lat[i] > end:
                end, last = s + lat[i], i
        return end + OPT["mean"] * sum(t) / n, t, by, last, end

    def rest(seq, case, got):
        _before, cost, lat, after = case
        tail, up, down, last = [0.0] * n, [-1] * n, [-1] * n, {}
        for i in reversed(seq):
            s = lat[i]
            for k, w in after[i]:
                if tail[k] + w > s:
                    s = tail[k] + w
            e = eng[i]
            if e is not None:
                k = last.get(e)
                if k is not None:
                    down[i], up[k] = k, i
                    if tail[k] + cost[i] > s:
                        s = tail[k] + cost[i]
                last[e] = i
            tail[i] = s
        return got[:5] + (tail, up, down, {})

    def least(part, case, old):
        before, cost, lat, after = case
        t0, tail, up, down = old[1], old[5], old[6], old[7]
        inside, t, free, end = set(part), {}, {}, 0.0
        for i in part:
            e = eng[i]
            if e is not None:
                if up[i] not in inside:
                    free[e] = t0[up[i]] + cost[up[i]] if up[i] >= 0 else 0.0
                if down[i] not in inside:
                    free[e, 1] = tail[down[i]] if down[i] >= 0 else -1e9
        for i in part:
            e = eng[i]
            s = free[e] if e is not None else 0.0
            for j, w in before[i]:
                c = (t[j] if j in inside else t0[j]) + w
                if c > s:
                    s = c
            t[i] = s
            free[e] = s + cost[i]
            q = lat[i]
            for k, w in after[i]:
                if k not in inside and tail[k] + w > q:
                    q = tail[k] + w
            if s + q > end:
                end = s + q
        for e in "VSPGY":
            if (e, 1) in free and free[e] + free[e, 1] > end:
                end = free[e] + free[e, 1]
        return end

    seq = sorted(range(n), key=lambda i: (at[i], i))
    now = [rest(seq, c, run(seq, c)) for c in cases]
    weight = [66.0 / r[4] / len(cases) for r in now]
    val = sum(w * r[0] for w, r in zip(weight, now))
    best = (val, seq, eng[:])
    for it, r in enumerate(rng.random((rounds, 7)).tolist()):
        slack = hot * (0.015 / hot) ** (it / rounds)
        by, last, _end, _tail, _up, _down, ways = now[int(r[6] * len(cases))][2:]
        i = last if r[0] < 0.7 else int(r[1] * n)
        if i not in ways:
            pairs = ways[i] = []
            while i != -1:
                if by[i] <= -2:
                    pairs.append((-2 - by[i], i))
                i = -2 - by[i] if by[i] <= -2 else by[i]
        else:
            pairs = ways[i]
        if not pairs:
            continue
        p, i = pairs[int(r[2] * len(pairs))]
        if r[6] * 977 % 1 < OPT["swap"]:
            c = i if r[5] < 0.5 else p
            if "alt" in ops[c]:
                eng[c] = "S" if eng[c] == "V" else "V"
                got = [run(seq, q, min(seq.index(c), n - 40), old) for q, old in zip(cases, now)]
                v = sum(w * q[0] for w, q in zip(weight, got))
                if v <= val - slack * math.log(1 - r[4]):
                    val = v
                    seq = sorted(seq, key=lambda j: got[0][1][j])
                    now = [rest(seq, q, x) for q, x in zip(cases, got)]
                    if val < best[0]:
                        best = (val, seq, eng[:])
                else:
                    eng[c] = "S" if eng[c] == "V" else "V"
                continue
        a, b = seq.index(p), seq.index(i)
        more = int(-math.log2(1 - r[3]))
        if r[5] < 0.5:
            for _k in range(more):
                c = a - 1
                while c >= 0 and eng[seq[c]] != eng[i]:
                    c -= 1
                if c < 0 or anc[i] >> seq[c] & 1:
                    break
                a = c
            if anc[i] >> seq[a] & 1:
                continue
            mid = seq[a:b]
            new = [j for j in mid if anc[i] >> j & 1] + [i] + [j for j in mid if not anc[i] >> j & 1]
        else:
            for _k in range(more):
                c = b + 1
                while c < n and eng[seq[c]] != eng[p]:
                    c += 1
                if c >= n or anc[seq[c]] >> p & 1:
                    break
                b = c
            if anc[seq[b]] >> p & 1:
                continue
            mid = seq[a + 1:b + 1]
            new = [j for j in mid if not anc[j] >> p & 1] + [p] + [j for j in mid if anc[j] >> p & 1]
        limit = val - slack * math.log(1 - r[4])
        if val + sum(w * (least(new, c, q) - q[4]) for w, c, q in zip(weight, cases, now)) > limit + 0.02:
            continue
        new = seq[:a] + new + seq[b + 1:]
        a = min(a, n - 40)
        got = [run(new, c, a, q) for c, q in zip(cases, now)]
        v = sum(w * q[0] for w, q in zip(weight, got))
        if v <= limit:
            val = v
            seq = sorted(new, key=lambda j: got[0][1][j])
            now = [rest(seq, c, q) for c, q in zip(cases, got)]
            if val < best[0]:
                best = (val, seq, eng[:])
    eng[:] = best[2]
    t = run(best[1], cases[0])[1]
    for k, i in enumerate(best[1]):
        t[i] += 1e-7 * k
    return t


def share(step, on_v):
    cut = 16 - on_v
    return ([(a, min(a + step, cut), False) for a in range(0, cut, step)] + [(a, min(a + step, 16), True) for a in range(cut, 16, step)])


KNOWN = {}
ROUNDS = 270000
SLOW = 1.05
CASES = [(1, 1, 1.0, 0.13, 1.0)]
EIGHTHS = list(range(0, 4097, 512))
OPT = {"half": 128, "pf": 0.9, "three": False, "parts": [0, 6, 12, 16], "moved": False, "split": False, "mxl": [1, 1, -1], "swap": 0.1, "mean": 0.5, "tries": 500, "move": 6.0, "plan": [(120000, 0.3), (60000, 0.12), (30000, 0.06)], "seed": 3,
       "hop": 0.7, "aud": [2.3, 0.7], "l0": 3.0, "l1": 3.5, "l2": 2.5, "nm": 10.0, "early": 0,
       "sil": [1, 1, 1, 1], "fl": [800, 480], "pc": [0, 0, 0], "pen": 0, "vs": [[], [], []], "last": 128, "e1g": 1,
       "vg": [share(4, 8), share(2, 4), share(2, 4)], "every": [1, 1, 1], "pe": ["", "", ""],
       "cuts": [[0, 512, 1280, 4096], EIGHTHS, EIGHTHS], "sgn": [[512, 1280], EIGHTHS, EIGHTHS],
       "two": [1280, 2304, 3328, 4096]}


def rank_program(g, core, T, topo):
    rank = T.rank_of(core)
    if rank is None:
        return hand_on(g, core, T, topo)
    if "t" not in KNOWN:
        order(max((build(r, c, T, topo) for r, c in enumerate(T.cores)), key=len))
    ops = build(rank, core, T, topo)
    seq = order(ops)
    queue = {"V": g.vector, "S": g.scalar, "P": g.tensor, "G": g, "Y": g.sync}
    pos = {i: k for k, i in enumerate(seq)}
    marked = set()
    known = {q: {} for q in queue}
    keep = []
    for i in seq:
        last, own = {}, []
        for j in ops[i]["hard"]:
            if ops[j]["sem"] is not None:
                own.append(j)
            elif ops[j]["eng"] not in last or pos[j] > pos[last[ops[j]["eng"]]]:
                last[ops[j]["eng"]] = j
        e = ops[i]["eng"]
        ws = []
        if e is not None:
            for j in own:
                if known[e].get(ops[j]["sem"], -1) < 0:
                    known[e][ops[j]["sem"]] = 1
                    ws.append(j)
            for e2, j in last.items():
                if known[e].get("c" + e2, -1) < pos[j]:
                    known[e]["c" + e2] = pos[j]
                    ws.append(j)
                    marked.add(j)
        keep.append(ws)
    val, total, waited = {}, {"V": 0, "S": 0, "P": 0, "G": 0}, set()
    for i, ws in zip(seq, keep):
        o = ops[i]
        if o["eng"] is None:
            continue
        q = queue[o["eng"]]
        for j in ws:
            if ops[j]["sem"] is not None:
                q.wait_ge(T.sem[ops[j]["sem"]], ops[j]["cnt"])
                waited.add(j)
            else:
                q.wait_ge(T.sem["c" + ops[j]["eng"]], val[j])
        ins = o["emit"](g)
        if i in marked:
            total[o["eng"]] += 1
            val[i] = total[o["eng"]]
            ins.then_inc(T.sem["c" + o["eng"]], 1)
    for i in seq:
        if ops[i]["sem"] is not None and i not in waited:
            (g.sync if ops[i]["eng"] in ("Y", "S") else g).wait_ge(T.sem[ops[i]["sem"]], ops[i]["cnt"])
